import numpy as np
import ml_dtypes


def mxq(x, axis, fmt="e4m3"):
    dtype, down = {"e4m3": (ml_dtypes.float8_e4m3fn, 7), "e5m2": (ml_dtypes.float8_e5m2, 14)}[fmt]
    v = np.moveaxis(np.asarray(x, np.float32).astype(ml_dtypes.bfloat16).astype(np.float64), axis, -1)
    blocks = v.reshape(v.shape[:-1] + (-1, 32))
    amax = np.abs(blocks).max(-1, keepdims=True)
    byte = np.maximum(np.where(amax > 0, np.frexp(amax)[1] - 1 + 127, 0) - down, 1)
    scale = np.exp2(byte - 127.0)
    codes = (blocks / scale).astype(np.float32).astype(dtype).astype(np.float64)
    return np.moveaxis((codes * scale).reshape(v.shape), -1, axis)


WIDE = False


def mx_kscale(k):
    if not WIDE:
        return np.ones(k)
    levels = np.array([10, -10, 5, -5, 0])
    if k % 512:
        return np.exp2(np.random.permutation(np.resize(levels, k // 32))).repeat(32)
    a = np.empty((k // 512, 16))
    for p in range(k // 512):
        a[p, :8] = np.random.permutation(np.resize(levels, 8))
        for g in range(8):
            far = levels[np.abs(levels - a[p, g]) >= 10]
            a[p, g + 8] = far[np.random.randint(len(far))]
    return np.exp2(a.ravel()).repeat(32)


def f64(x):
    return np.asarray(x).astype(np.float64)


def striped(idx):
    return np.tile(idx.reshape(-1, 16).T, (8, 1)).astype(np.uint16)


def unstriped(offs):
    return offs[:16].T.reshape(-1).astype(np.int64)


E2M1 = np.array([0.0, 0.5, 1.0, 1.5, 2.0, 3.0, 4.0, 6.0, -0.0, -0.5, -1.0, -1.5, -2.0, -3.0, -4.0, -6.0])


def pack_weight(w, fmt):
    k, n = w.shape
    w = f64(np.asarray(w, np.float32).astype(ml_dtypes.bfloat16)).reshape(k // 32, 32, n)
    amax = np.abs(w).max(1)
    if fmt == "e4m3":
        byte = np.frexp(amax)[1] - 1 + 127 - 7
    else:
        mant, ex = np.frexp(amax / 6.0)
        byte = np.where(mant > 0.5, ex, ex - 1) + 127
    byte = np.clip(np.where(amax > 0, byte, 1), 1, 254)
    scaled = (w * np.exp2(127.0 - byte)[:, None, :]).reshape(k, n).astype(np.float32)
    by_word = np.ascontiguousarray(scaled.reshape(k // 512, 128, 4, n).transpose(0, 1, 3, 2))
    if fmt == "e4m3":
        words = by_word.astype(ml_dtypes.float8_e4m3fn).view(np.uint8)
    else:
        c = by_word.astype(ml_dtypes.float4_e2m1fn).view(np.uint8) & 0xF
        words = (c[..., 0::2] | (c[..., 1::2] << 4)).reshape(k // 512, 128, 2 * n)
    return np.ascontiguousarray(words), np.ascontiguousarray(byte.astype(np.uint8).reshape(k // 512, 16, n))


def unpack_weight(words, scales, fmt):
    g, _, n = scales.shape
    words = np.ascontiguousarray(words).reshape(g, 128, n, -1)
    if fmt == "e4m3":
        vals = words.view(ml_dtypes.float8_e4m3fn).astype(np.float64)
    else:
        nib = np.empty((g, 128, n, 4), np.uint8)
        nib[..., 0::2] = words & 0xF
        nib[..., 1::2] = words >> 4
        vals = E2M1[nib]
    vals = vals * np.repeat(np.exp2(scales.astype(np.float64) - 127.0), 8, axis=1)[..., None]
    return vals.transpose(0, 1, 3, 2).reshape(g * 512, n)


def silu(v):
    return v / (1.0 + np.exp(-np.maximum(v, -700.0)))


def d_silu(v):
    s = 1.0 / (1.0 + np.exp(-np.maximum(v, -700.0)))
    return s * (1.0 + v * (1.0 - s))


K, T, E1, C1, E2, C2, H = 512, 768, 3, 256, 6, 128, 512
N = 1024


def by_expert(wq, xq, E, C):
    return np.concatenate([wq[e].T @ xq[:, e * C:(e + 1) * C] for e in range(E)], axis=1)


def setup_inputs():
    n = np.random.standard_normal
    v = mx_kscale(N)
    u = mx_kscale(H)
    slots1, slots2 = np.random.permutation(T), np.random.permutation(T)
    dy = pack_weight(n((N, T)) * v[:, None], "e4m3")
    w2t = pack_weight(n((N, H)) / np.sqrt(N) / v[:, None] * u, "e4m3")
    wat = [pack_weight(m, "e4m3") for m in n((E1, H, K)) / np.sqrt(H) / u[None, :, None]]
    wbt = [pack_weight(m, "e2m1") for m in n((E2, H, K)) / np.sqrt(H) / u[None, :, None]]
    return {
        "dy_words": dy[0],
        "dy_scales": dy[1],
        "w2t_words": w2t[0],
        "w2t_scales": w2t[1],
        "wat_words": np.stack([m[0] for m in wat]),
        "wat_scales": np.stack([m[1] for m in wat]),
        "wbt_words": np.stack([m[0] for m in wbt]),
        "wbt_scales": np.stack([m[1] for m in wbt]),
        "a": (n((H, T))).astype(np.float32),
        "c": (n((H, T))).astype(np.float32),
        "offs": striped(slots1),
        "offs2": striped(slots2),
    }


def reference(dy_words, dy_scales, w2t_words, w2t_scales, wat_words, wat_scales, wbt_words, wbt_scales, a, c, offs, offs2):
    w2t = unpack_weight(w2t_words, w2t_scales, "e4m3")
    wat = np.stack([unpack_weight(wat_words[e], wat_scales[e], "e4m3") for e in range(E1)])
    wbt = np.stack([unpack_weight(wbt_words[e], wbt_scales[e], "e2m1") for e in range(E2)])
    idx, idx2 = unstriped(offs), unstriped(offs2)
    dh = w2t.T @ unpack_weight(dy_words, dy_scales, "e4m3")
    da = dh * f64(c) * d_silu(f64(a))
    dc = dh * silu(f64(a))
    out = np.zeros((K, T))
    out[:, idx] = by_expert(wat, mxq(da[:, idx], 0, "e4m3"), E1, C1)
    out[:, idx2] += by_expert(wbt, mxq(dc[:, idx2], 0, "e4m3"), E2, C2)
    return out

@@ -1,0 +1,270 @@
+from contextlib import ExitStack
+
+import concourse.mybir as mybir
+
+F32 = mybir.dt.float32
+BF16 = mybir.dt.bfloat16
+I32 = mybir.dt.int32
+U32 = mybir.dt.uint32
+U16 = mybir.dt.uint16
+U8 = mybir.dt.uint8
+FP8X4 = mybir.dt.float8_e4m3fn_x4
+FP4X4 = mybir.dt.float4_e2m1fn_x4
+ACT = mybir.ActivationFunctionType
+ALU = mybir.AluOpType
+
+K, T, H, N = 512, 768, 512, 1024
+E1, C1, E2, C2 = 3, 256, 6, 128
+P = 128
+TC = 256
+FLOPS = 2 * N * H * T + 2 * 2 * H * K * T
+USE_G = True
+
+
+def tile_moe_plb_silu_kernel(
+    tc, dy_words, dy_scales, w2t_words, w2t_scales, wat_words, wat_scales, wbt_words, wbt_scales, a, c, offs, offs2, out
+):
+    nc = tc.nc
+    with ExitStack() as ctx:
+        sb = ctx.enter_context(tc.tile_pool(name="sb", bufs=1))
+        ps = ctx.enter_context(tc.psum_pool(name="ps", bufs=1))
+
+        def tile(shape, dtype, name, tag=None):
+            return sb.tile(shape, dtype, name=name, tag=tag or name, align_bytes=64)
+
+        w2_sc_raw = tile([P, H], U8, "w2_sc_raw")
+        dy_sc = tile([P, T], U8, "dy_sc")
+        warm = tile([P, 1], F32, "warm", tag="a_all")
+        nc.gpsimd.memset(w2_sc_raw[:].bitcast(I32), 0)
+        nc.gpsimd.memset(dy_sc[:].bitcast(I32), 0)
+        nc.gpsimd.memset(warm[:], 0.0)
+
+        idx2 = tile([P, T // 16], U16, "idx2")
+        idx1 = tile([P, T // 16], U16, "idx1")
+        nc.sync.dma_start(idx2[:], offs2)
+        nc.sync.dma_start(idx1[:], offs)
+        w2_raw = tile([P, 2, H], U32, "w2_raw", tag="w2_raw")
+        nc.sync.dma_start(w2_raw[:].bitcast(I32), w2t_words.rearrange("s p i d -> p s (i d)").bitcast(I32))
+        dy = tile([P, 2, T], U32, "dy", tag="dy")
+        nc.sync.dma_start(dy[:].bitcast(I32), dy_words.rearrange("s p t d -> p s (t d)").bitcast(I32))
+        w2_sc_hbm = w2t_scales.bitcast(I32)
+        dy_sc_hbm = dy_scales.bitcast(I32)
+        for q in range(4):
+            nc.scalar.dma_start(w2_sc_raw[32 * q : 32 * q + 8, :].bitcast(I32), w2_sc_hbm[:, 4 * q : 4 * q + 4, :])
+        for q in range(4):
+            (nc.gpsimd if q < 2 else nc.sync).dma_start(dy_sc[32 * q : 32 * q + 8, :].bitcast(I32), dy_sc_hbm[:, 4 * q : 4 * q + 4, :])
+        warm_out = tile([P, 1], F32, "warm_out")
+        nc.scalar.activation(warm_out[:], warm[:], ACT.Silu)
+
+        a_all = tile([P, 6, 2 * TC], F32, "a_all", tag="a_all")
+        a_v = a.rearrange("(p j) t -> p j t", j=4)
+        c_v = c.rearrange("(p j) t -> p j t", j=4)
+        for h in range(2):
+            for g in range(3):
+                nc.sync.dma_start(
+                    a_all[:, 3 * h + g, :].rearrange("p (e t) -> p e t", e=2),
+                    a_v[:, 2 * h : 2 * h + 2, g * TC : (g + 1) * TC],
+                )
+        wb_sc_hbm = wbt_scales.bitcast(I32).rearrange("f s (q r) k -> r q (f s) k", r=4)
+        wa_sc_hbm = wat_scales.bitcast(I32).rearrange("f s (q r) k -> r q (f s) k", r=4)
+
+        w2 = tile([P, 2, H], U32, "w2", tag="w2")
+        w2_sc = tile([P, H], U8, "w2_sc")
+        for s in range(2):
+            nc.vector.tensor_copy(
+                out=w2[:, s, :].bitcast(I32).rearrange("p (j b i) -> p b j i", j=4, i=4),
+                in_=w2_raw[:, s, :].bitcast(I32).rearrange("p (b i j) -> p b j i", j=4, i=4),
+            )
+        nc.vector.tensor_copy(
+            out=w2_sc[:].rearrange("p (j m) -> p m j", j=4),
+            in_=w2_sc_raw[:].rearrange("p (m j) -> p m j", j=4),
+        )
+        wb_sc = tile([P, E2, K], U8, "wb_sc", tag="w2_sc_raw")
+        nc.gpsimd.memset(wb_sc[:].rearrange("p f k -> p (f k)").bitcast(I32), 0)
+        for r in range(4):
+            nc.gpsimd.dma_start(wb_sc[r:P:32, :, :].bitcast(I32), wb_sc_hbm[r])
+        wb = tile([P, E2, 2 * K], U8, "wb", tag="w2_raw")
+        nc.sync.dma_start(wb[:].bitcast(I32), wbt_words.bitcast(I32).rearrange("f s p k -> p (f s) k"))
+
+        dh = {}
+        dc = [tile([P, T, 2], BF16, f"dc{h}") for h in range(2)]
+        for h in range(2):
+            for g in range(3):
+                bank = ps.tile([P, 2, TC], F32, name=f"dh{h}{g}", tag=f"bank{3 * h + g}")
+                dh[h, g] = bank
+                cols = slice(g * TC, (g + 1) * TC)
+                for e in range(2):
+                    j = 2 * h + e
+                    for s in range(2):
+                        nc.tensor.matmul_mx(
+                            out=bank[:, e, :],
+                            lhsT=w2[:, s, j * P : (j + 1) * P].bitcast(FP8X4),
+                            lhsT_scale=w2_sc[4 * s : P, j * P : (j + 1) * P],
+                            rhs=dy[:, s, cols].bitcast(FP8X4),
+                            rhs_scale=dy_sc[4 * s : P, cols],
+                            start=(s == 0),
+                            stop=(s == 1),
+                        )
+                y = tile([P, TC, 2], F32, f"y{h}{g}")
+                nc.scalar.activation(y[:], a_all[:, 3 * h + g, :].rearrange("p (e t) -> p t e", e=2), ACT.Silu)
+                nc.vector.tensor_tensor(dc[h][:, cols, :], bank[:].rearrange("p e t -> p t e"), y[:], ALU.mult)
+        c_sb = [tile([P, 2, T], F32, "c0", tag="dy"), tile([P, 2, T], F32, "c1", tag="w2")]
+        for h in range(2):
+            nc.sync.dma_start(c_sb[h][:], c_v[:, 2 * h : 2 * h + 2, :])
+
+        wa_sc = tile([P, E1, K], U8, "wa_sc", tag="w2_sc")
+        nc.gpsimd.memset(wa_sc[:].rearrange("p f k -> p (f k)").bitcast(I32), 0)
+        for r in range(4):
+            nc.sync.dma_start(wa_sc[r:P:32, :, :].bitcast(I32), wa_sc_hbm[r])
+
+        def offsets(idx, lo, hi):
+            return idx[:, lo // 16 : hi // 16]
+
+        def dc_words(h):
+            return dc[h][:].rearrange("p t e -> p (t e)").bitcast(U32)
+
+        def quantise(src, n, name):
+            codes = tile([P, n], U32, name + "_codes")
+            scales = tile([P, n], U8, name + "_scales")
+            nc.vector.quantize_mx(out=codes[:].bitcast(FP8X4), scales=scales[:], in_=src)
+            return codes, scales
+
+        def q_matmul(dst, f, kb, codes, scales, lo):
+            nc.tensor.matmul_mx(
+                out=dst,
+                lhsT=wb[:, f, 2 * P * kb : 2 * P * (kb + 1)].bitcast(FP4X4),
+                lhsT_scale=wb_sc[:, f, P * kb : P * (kb + 1)],
+                rhs=codes[:, lo : lo + C2].bitcast(FP8X4),
+                rhs_scale=scales[:, lo : lo + C2],
+                start=True,
+                stop=True,
+            )
+
+        q_win = [tile([P, T], F32, f"q_win{kb}") for kb in range(4)]
+        r_win = [tile([P, T], F32, f"r_win{kb}") for kb in range(4)]
+
+        def scatter(win, idx, lo, hi, src):
+            nc.vector.tensor_copy(win[:].indirect(offsets(idx, lo, hi)), src)
+
+        NA = 256
+        gA = tile([P, 2, NA], U32, "gA")
+        for h in range(2):
+            nc.vector.tensor_copy(gA[:, h, :], dc_words(h).indirect(offsets(idx2, 0, NA)))
+        NB = T - NA
+        gB = tile([P, 2 * NB], U32, "gB")
+        wA = gB[:, NB : 2 * NB]
+        nc.scalar.copy(wA.rearrange("p (n h) -> p n h", h=2), gA[:].rearrange("p h n -> p n h"))
+        nc.vector.tensor_copy(gB[:, 0:NB], dc_words(0).indirect(offsets(idx2, NA, T)))
+        cA, sA = quantise(wA.bitcast(BF16), NA, "qA")
+        nc.vector.tensor_copy(gB[:, NB : 2 * NB], dc_words(1).indirect(offsets(idx2, NA, T)))
+        wa = tile([P, E1, K], U32, "wa", tag="dc0")
+        nc.sync.dma_start(wa[:].bitcast(I32), wat_words.rearrange("e s p k d -> p (e s) (k d)").bitcast(I32))
+
+        banksA = []
+        for b in range(2):
+            bank = ps.tile([P, 2, NA], F32, name=f"qA{b}", tag=f"bank{6 + b}")
+            for u in range(2):
+                for f in range(2):
+                    q_matmul(bank[:, u, f * C2 : (f + 1) * C2], f, 2 * b + u, cA, sA, f * C2)
+            banksA.append(bank)
+        stA = [tile([P, 2, NA], F32, f"stA{b}") for b in range(2)]
+        nc.vector.tensor_copy(stA[0][:], banksA[0][:])
+        for u in range(2):
+            scatter(q_win[u], idx2, 0, NA, stA[0][:, u, :])
+        wB = tile([P, T - NA, 2], U32, "wB")
+        nc.scalar.copy(wB[:], gB[:].rearrange("p (h n) -> p n h", h=2))
+        nc.scalar.copy(stA[1][:], banksA[1][:])
+        cB, sB = quantise(wB[:].rearrange("p n h -> p (n h)").bitcast(BF16), T - NA, "qB")
+        for u in range(2):
+            scatter(q_win[2 + u], idx2, 0, NA, stA[1][:, u, :])
+        banksB = []
+        for kb in range(4):
+            bank = ps.tile([P, T - NA], F32, name=f"qB{kb}", tag=f"bank{6 + kb % 2}")
+            for f in range(2, E2):
+                q_matmul(bank[:, (f - 2) * C2 : (f - 1) * C2], f, kb, cB, sB, (f - 2) * C2)
+            banksB.append(bank)
+            if kb < 3:
+                stB = tile([P, T - NA], F32, f"stB{kb}")
+                nc.scalar.copy(stB[:], bank[:])
+                scatter(q_win[kb], idx2, NA, T, stB[:])
+
+        z = [tile([P, 3, 2 * TC], F32, f"z{h}", tag=f"y1{1 + h}") for h in range(2)]
+        for h in range(2):
+            for g in range(3):
+                nc.scalar.activation(z[h][:, g, :], a_all[:, 3 * h + g, :], ACT.Silu, scale=-1.0)
+        for h in range(2):
+            for g in range(3):
+                nc.scalar.activation(a_all[:, 3 * h + g, :], a_all[:, 3 * h + g, :], ACT.Sigmoid)
+        eng = nc.gpsimd if USE_G else nc.vector
+        for h in range(2):
+            for g in range(3):
+                nc.vector.scalar_tensor_tensor(
+                    z[h][:, g, :], z[h][:, g, :], 1.0, dh[h, g][:].rearrange("p e t -> p (e t)"), ALU.subtract, ALU.mult
+                )
+                zv = z[h][:, g, :].rearrange("p (e t) -> p e t", e=2)
+                eng.tensor_tensor(zv, zv, c_sb[h][:, :, g * TC : (g + 1) * TC], ALU.mult)
+        da = [tile([P, 2, T], BF16, f"da{h}") for h in range(2)]
+        for h in range(2):
+            for g in range(3):
+                eng.tensor_tensor(
+                    da[h][:, :, g * TC : (g + 1) * TC],
+                    z[h][:, g, :].rearrange("p (e t) -> p e t", e=2),
+                    a_all[:, 3 * h + g, :].rearrange("p (e t) -> p e t", e=2),
+                    ALU.mult,
+                )
+
+        def r_gather(dst, j, lo, hi):
+            nc.scalar.activation(dst[:, :, j], da[j // 2][:, j % 2, :].indirect(offsets(idx1, lo, hi)), ACT.Copy, scale=-1.0)
+
+        def r_matmul(dst, e, kb, codes, scales, lo):
+            nc.tensor.matmul_mx(
+                out=dst,
+                lhsT=wa[:, e, P * kb : P * (kb + 1)].bitcast(FP8X4),
+                lhsT_scale=wa_sc[:, e, P * kb : P * (kb + 1)],
+                rhs=codes[:, lo : lo + C1].bitcast(FP8X4),
+                rhs_scale=scales[:, lo : lo + C1],
+                start=True,
+                stop=True,
+            )
+
+        g1 = tile([P, C1, 4], BF16, "g1", tag="g1")
+        stB3 = tile([P, T - NA], F32, "stB3", tag="y12")
+        r_gather(g1, 0, 0, C1)
+        r_gather(g1, 1, 0, C1)
+        nc.scalar.copy(stB3[:, 0:256], banksB[3][:, 0:256])
+        scatter(q_win[3], idx2, NA, NA + 256, stB3[:, 0:256])
+        r_gather(g1, 2, 0, C1)
+        r_gather(g1, 3, 0, C1)
+        c1, s1 = quantise(g1[:].rearrange("p n j -> p (n j)"), C1, "r1")
+        nc.scalar.copy(stB3[:, 256:512], banksB[3][:, 256:512])
+        scatter(q_win[3], idx2, NA + 256, T, stB3[:, 256:512])
+        banks1 = []
+        for b in range(2):
+            bank = ps.tile([P, 2, C1], F32, name=f"r1{b}", tag=f"bank{b}")
+            for u in range(2):
+                r_matmul(bank[:, u, :], 0, 2 * b + u, c1, s1, 0)
+            banks1.append(bank)
+        st1 = [tile([P, 2, C1], F32, f"st1{b}") for b in range(2)]
+        nc.vector.tensor_copy(st1[0][:], banks1[0][:])
+        for u in range(2):
+            scatter(r_win[u], idx1, 0, C1, st1[0][:, u, :])
+        g2 = tile([P, T - C1, 4], BF16, "g2", tag="g1")
+        r_gather(g2, 0, C1, T)
+        r_gather(g2, 1, C1, T)
+        nc.scalar.copy(st1[1][:, 0, :], banks1[1][:, 0, :])
+        scatter(r_win[2], idx1, 0, C1, st1[1][:, 0, :])
+        r_gather(g2, 2, C1, T)
+        r_gather(g2, 3, C1, T)
+        c2, s2 = quantise(g2[:].rearrange("p n j -> p (n j)"), T - C1, "r2")
+        nc.scalar.copy(st1[1][:, 1, :], banks1[1][:, 1, :])
+        scatter(r_win[3], idx1, 0, C1, st1[1][:, 1, :])
+        for kb in range(4):
+            bank = ps.tile([P, 2, C1], F32, name=f"r2{kb}", tag=f"bank{2 + kb}")
+            for u in range(2):
+                r_matmul(bank[:, u, :], 1 + u, kb, c2, s2, u * C1)
+            st2 = tile([P, T - C1], F32, f"st2{kb}")
+            nc.scalar.copy(st2[:], bank[:].rearrange("p u n -> p (u n)"))
+            scatter(r_win[kb], idx1, C1, T, st2[:])
+            eng = nc.gpsimd if (USE_G and kb < 3) else nc.vector
+            eng.tensor_tensor(q_win[kb][:], q_win[kb][:], r_win[kb][:], ALU.add)
+            nc.sync.dma_start(out[kb * P : (kb + 1) * P, :], q_win[kb][:])

@@ -35,9 +35,11 @@ def tile_moe_plb_silu_kernel(
         w2_sc_raw = tile([P, H], U8, "w2_sc_raw")
         dy_sc = tile([P, T], U8, "dy_sc")
         warm = tile([P, 1], F32, "warm", tag="a_all")
+        zero = tile([P, 1], F32, "zero", tag="dy")
+        nc.gpsimd.memset(zero[:], 0.0)
         nc.gpsimd.memset(w2_sc_raw[:].bitcast(I32), 0)
+        nc.gpsimd.tensor_copy(warm[:], zero[:])
         nc.gpsimd.memset(dy_sc[:].bitcast(I32), 0)
-        nc.gpsimd.memset(warm[:], 0.0)
 
         idx2 = tile([P, T // 16], U16, "idx2")
         idx1 = tile([P, T // 16], U16, "idx1")
@@ -45,26 +47,26 @@ def tile_moe_plb_silu_kernel(
         nc.sync.dma_start(idx1[:], offs)
         w2_raw = tile([P, 2, H], U32, "w2_raw", tag="w2_raw")
         nc.sync.dma_start(w2_raw[:].bitcast(I32), w2t_words.rearrange("s p i d -> p s (i d)").bitcast(I32))
-        dy = tile([P, 2, T], U32, "dy", tag="dy")
-        nc.sync.dma_start(dy[:].bitcast(I32), dy_words.rearrange("s p t d -> p s (t d)").bitcast(I32))
         w2_sc_hbm = w2t_scales.bitcast(I32)
         dy_sc_hbm = dy_scales.bitcast(I32)
         for q in range(4):
-            nc.scalar.dma_start(w2_sc_raw[32 * q : 32 * q + 8, :].bitcast(I32), w2_sc_hbm[:, 4 * q : 4 * q + 4, :])
-        for q in range(4):
-            (nc.gpsimd if q < 2 else nc.sync).dma_start(dy_sc[32 * q : 32 * q + 8, :].bitcast(I32), dy_sc_hbm[:, 4 * q : 4 * q + 4, :])
+            (nc.scalar if q < 2 else nc.sync).dma_start(w2_sc_raw[32 * q : 32 * q + 8, :].bitcast(I32), w2_sc_hbm[:, 4 * q : 4 * q + 4, :])
+        dy = tile([P, 2, T], U32, "dy", tag="dy")
+        nc.sync.dma_start(dy[:].bitcast(I32), dy_words.rearrange("s p t d -> p s (t d)").bitcast(I32))
         warm_out = tile([P, 1], F32, "warm_out")
         nc.scalar.activation(warm_out[:], warm[:], ACT.Silu)
+        for q in range(4):
+            nc.sync.dma_start(dy_sc[32 * q : 32 * q + 8, :].bitcast(I32), dy_sc_hbm[:, 4 * q : 4 * q + 4, :])
 
-        a_all = tile([P, 6, 2 * TC], F32, "a_all", tag="a_all")
+        a_all = tile([P, 4, 2 * T], F32, "a_all", tag="a_all")
         a_v = a.rearrange("(p j) t -> p j t", j=4)
         c_v = c.rearrange("(p j) t -> p j t", j=4)
-        for h in range(2):
-            for g in range(3):
-                nc.sync.dma_start(
-                    a_all[:, 3 * h + g, :].rearrange("p (e t) -> p e t", e=2),
-                    a_v[:, 2 * h : 2 * h + 2, g * TC : (g + 1) * TC],
-                )
+        a_sb = {}
+        for h, lo, hi in ((0, 0, 2), (0, 2, 3), (1, 0, 1), (1, 1, 2), (1, 2, 3)):
+            part = a_all[:, h, 2 * lo * TC : 2 * hi * TC].rearrange("p (e t) -> p e t", e=2)
+            nc.sync.dma_start(part, a_v[:, 2 * h : 2 * h + 2, lo * TC : hi * TC])
+            for g in range(lo, hi):
+                a_sb[h, g] = part[:, :, (g - lo) * TC : (g - lo + 1) * TC]
         wb_sc_hbm = wbt_scales.bitcast(I32).rearrange("f s (q r) k -> r q (f s) k", r=4)
         wa_sc_hbm = wat_scales.bitcast(I32).rearrange("f s (q r) k -> r q (f s) k", r=4)
 
@@ -106,11 +108,11 @@ def tile_moe_plb_silu_kernel(
                             stop=(s == 1),
                         )
                 y = tile([P, TC, 2], F32, f"y{h}{g}")
-                nc.scalar.activation(y[:], a_all[:, 3 * h + g, :].rearrange("p (e t) -> p t e", e=2), ACT.Silu)
+                nc.scalar.activation(y[:], a_sb[h, g].rearrange("p e t -> p t e"), ACT.Silu, bias=warm_out[:])
                 nc.vector.tensor_tensor(dc[h][:, cols, :], bank[:].rearrange("p e t -> p t e"), y[:], ALU.mult)
-        c_sb = [tile([P, 2, T], F32, "c0", tag="dy"), tile([P, 2, T], F32, "c1", tag="w2")]
+        c_sb = [a_all[:, 2 + h, :].rearrange("p (e t) -> p e t", e=2) for h in range(2)]
         for h in range(2):
-            nc.sync.dma_start(c_sb[h][:], c_v[:, 2 * h : 2 * h + 2, :])
+            nc.sync.dma_start(c_sb[h], c_v[:, 2 * h : 2 * h + 2, :])
 
         wa_sc = tile([P, E1, K], U8, "wa_sc", tag="w2_sc")
         nc.gpsimd.memset(wa_sc[:].rearrange("p f k -> p (f k)").bitcast(I32), 0)
@@ -123,8 +125,8 @@ def tile_moe_plb_silu_kernel(
         def dc_words(h):
             return dc[h][:].rearrange("p t e -> p (t e)").bitcast(U32)
 
-        def quantise(src, n, name):
-            codes = tile([P, n], U32, name + "_codes")
+        def quantise(src, n, name, tag=None):
+            codes = tile([P, n], U32, name + "_codes", tag=tag)
             scales = tile([P, n], U8, name + "_scales")
             nc.vector.quantize_mx(out=codes[:].bitcast(FP8X4), scales=scales[:], in_=src)
             return codes, scales
@@ -146,6 +148,18 @@ def tile_moe_plb_silu_kernel(
         def scatter(win, idx, lo, hi, src):
             nc.vector.tensor_copy(win[:].indirect(offsets(idx, lo, hi)), src)
 
+        z = [tile([P, 3, 2 * TC], F32, f"z{h}", tag=f"y1{1 + h}") for h in range(2)]
+        da = [tile([P, 2, T], BF16, f"da{h}") for h in range(2)]
+
+        def factor(h, g):
+            zv = z[h][:, g, :].rearrange("p (e t) -> p e t", e=2)
+            nc.scalar.activation(zv, a_sb[h, g], ACT.Silu, scale=-1.0)
+            nc.vector.scalar_tensor_tensor(
+                z[h][:, g, :], z[h][:, g, :], 1.0, dh[h, g][:].rearrange("p e t -> p (e t)"), ALU.subtract, ALU.mult
+            )
+            nc.gpsimd.tensor_tensor(zv, zv, c_sb[h][:, :, g * TC : (g + 1) * TC], ALU.mult)
+
+        factor(0, 0)
         NA = 256
         gA = tile([P, 2, NA], U32, "gA")
         for h in range(2):
@@ -154,12 +168,16 @@ def tile_moe_plb_silu_kernel(
         gB = tile([P, 2 * NB], U32, "gB")
         wA = gB[:, NB : 2 * NB]
         nc.scalar.copy(wA.rearrange("p (n h) -> p n h", h=2), gA[:].rearrange("p h n -> p n h"))
+        factor(0, 1)
         nc.vector.tensor_copy(gB[:, 0:NB], dc_words(0).indirect(offsets(idx2, NA, T)))
         cA, sA = quantise(wA.bitcast(BF16), NA, "qA")
+        factor(0, 2)
         nc.vector.tensor_copy(gB[:, NB : 2 * NB], dc_words(1).indirect(offsets(idx2, NA, T)))
         wa = tile([P, E1, K], U32, "wa", tag="dc0")
         nc.sync.dma_start(wa[:].bitcast(I32), wat_words.rearrange("e s p k d -> p (e s) (k d)").bitcast(I32))
 
+        for g in range(3):
+            factor(1, g)
         banksA = []
         for b in range(2):
             bank = ps.tile([P, 2, NA], F32, name=f"qA{b}", tag=f"bank{6 + b}")
@@ -168,7 +186,7 @@ def tile_moe_plb_silu_kernel(
                     q_matmul(bank[:, u, f * C2 : (f + 1) * C2], f, 2 * b + u, cA, sA, f * C2)
             banksA.append(bank)
         stA = [tile([P, 2, NA], F32, f"stA{b}") for b in range(2)]
-        nc.vector.tensor_copy(stA[0][:], banksA[0][:])
+        nc.scalar.copy(stA[0][:], banksA[0][:])
         for u in range(2):
             scatter(q_win[u], idx2, 0, NA, stA[0][:, u, :])
         wB = tile([P, T - NA, 2], U32, "wB")
@@ -177,6 +195,9 @@ def tile_moe_plb_silu_kernel(
         cB, sB = quantise(wB[:].rearrange("p n h -> p (n h)").bitcast(BF16), T - NA, "qB")
         for u in range(2):
             scatter(q_win[2 + u], idx2, 0, NA, stA[1][:, u, :])
+        for h in range(2):
+            for g in range(3):
+                nc.scalar.activation(a_sb[h, g], a_sb[h, g], ACT.Sigmoid)
         banksB = []
         for kb in range(4):
             bank = ps.tile([P, T - NA], F32, name=f"qB{kb}", tag=f"bank{6 + kb % 2}")
@@ -188,28 +209,12 @@ def tile_moe_plb_silu_kernel(
                 nc.scalar.copy(stB[:], bank[:])
                 scatter(q_win[kb], idx2, NA, T, stB[:])
 
-        z = [tile([P, 3, 2 * TC], F32, f"z{h}", tag=f"y1{1 + h}") for h in range(2)]
         for h in range(2):
             for g in range(3):
-                nc.scalar.activation(z[h][:, g, :], a_all[:, 3 * h + g, :], ACT.Silu, scale=-1.0)
-        for h in range(2):
-            for g in range(3):
-                nc.scalar.activation(a_all[:, 3 * h + g, :], a_all[:, 3 * h + g, :], ACT.Sigmoid)
-        eng = nc.gpsimd if USE_G else nc.vector
-        for h in range(2):
-            for g in range(3):
-                nc.vector.scalar_tensor_tensor(
-                    z[h][:, g, :], z[h][:, g, :], 1.0, dh[h, g][:].rearrange("p e t -> p (e t)"), ALU.subtract, ALU.mult
-                )
-                zv = z[h][:, g, :].rearrange("p (e t) -> p e t", e=2)
-                eng.tensor_tensor(zv, zv, c_sb[h][:, :, g * TC : (g + 1) * TC], ALU.mult)
-        da = [tile([P, 2, T], BF16, f"da{h}") for h in range(2)]
-        for h in range(2):
-            for g in range(3):
-                eng.tensor_tensor(
+                nc.gpsimd.tensor_tensor(
                     da[h][:, :, g * TC : (g + 1) * TC],
                     z[h][:, g, :].rearrange("p (e t) -> p e t", e=2),
-                    a_all[:, 3 * h + g, :].rearrange("p (e t) -> p e t", e=2),
+                    a_sb[h, g],
                     ALU.mult,
                 )
 
@@ -227,10 +232,13 @@ def tile_moe_plb_silu_kernel(
                 stop=True,
             )
 
-        g1 = tile([P, C1, 4], BF16, "g1", tag="g1")
+        g1 = tile([P, C1, 4], BF16, "g1")
+        g2 = tile([P, T - C1, 4], BF16, "g2")
         stB3 = tile([P, T - NA], F32, "stB3", tag="y12")
         r_gather(g1, 0, 0, C1)
         r_gather(g1, 1, 0, C1)
+        r_gather(g2, 0, C1, T)
+        r_gather(g2, 1, C1, T)
         nc.scalar.copy(stB3[:, 0:256], banksB[3][:, 0:256])
         scatter(q_win[3], idx2, NA, NA + 256, stB3[:, 0:256])
         r_gather(g1, 2, 0, C1)
@@ -238,26 +246,20 @@ def tile_moe_plb_silu_kernel(
         c1, s1 = quantise(g1[:].rearrange("p n j -> p (n j)"), C1, "r1")
         nc.scalar.copy(stB3[:, 256:512], banksB[3][:, 256:512])
         scatter(q_win[3], idx2, NA + 256, T, stB3[:, 256:512])
-        banks1 = []
+        st1 = []
         for b in range(2):
             bank = ps.tile([P, 2, C1], F32, name=f"r1{b}", tag=f"bank{b}")
             for u in range(2):
                 r_matmul(bank[:, u, :], 0, 2 * b + u, c1, s1, 0)
-            banks1.append(bank)
-        st1 = [tile([P, 2, C1], F32, f"st1{b}") for b in range(2)]
-        nc.vector.tensor_copy(st1[0][:], banks1[0][:])
-        for u in range(2):
-            scatter(r_win[u], idx1, 0, C1, st1[0][:, u, :])
-        g2 = tile([P, T - C1, 4], BF16, "g2", tag="g1")
-        r_gather(g2, 0, C1, T)
-        r_gather(g2, 1, C1, T)
-        nc.scalar.copy(st1[1][:, 0, :], banks1[1][:, 0, :])
-        scatter(r_win[2], idx1, 0, C1, st1[1][:, 0, :])
+            for u in range(2):
+                st1.append(tile([P, C1], F32, f"st1{2 * b + u}"))
+                nc.scalar.copy(st1[-1][:], bank[:, u, :])
+        scatter(r_win[0], idx1, 0, C1, st1[0][:])
         r_gather(g2, 2, C1, T)
         r_gather(g2, 3, C1, T)
-        c2, s2 = quantise(g2[:].rearrange("p n j -> p (n j)"), T - C1, "r2")
-        nc.scalar.copy(st1[1][:, 1, :], banks1[1][:, 1, :])
-        scatter(r_win[3], idx1, 0, C1, st1[1][:, 1, :])
+        c2, s2 = quantise(g2[:].rearrange("p n j -> p (n j)"), T - C1, "r2", tag="st10")
+        for kb in range(1, 4):
+            scatter(r_win[kb], idx1, 0, C1, st1[kb][:])
         for kb in range(4):
             bank = ps.tile([P, 2, C1], F32, name=f"r2{kb}", tag=f"bank{2 + kb}")
             for u in range(2):
@@ -265,6 +267,12 @@ def tile_moe_plb_silu_kernel(
             st2 = tile([P, T - C1], F32, f"st2{kb}")
             nc.scalar.copy(st2[:], bank[:].rearrange("p u n -> p (u n)"))
             scatter(r_win[kb], idx1, C1, T, st2[:])
-            eng = nc.gpsimd if (USE_G and kb < 3) else nc.vector
-            eng.tensor_tensor(q_win[kb][:], q_win[kb][:], r_win[kb][:], ALU.add)
-            nc.sync.dma_start(out[kb * P : (kb + 1) * P, :], q_win[kb][:])
+            rows = slice(kb * P, (kb + 1) * P)
+            if kb < 3:
+                nc.gpsimd.tensor_tensor(q_win[kb][:], q_win[kb][:], r_win[kb][:], ALU.add)
+                nc.sync.dma_start(out[rows, :], q_win[kb][:])
+            else:
+                for half, queue in enumerate((nc.scalar, nc.scalar)):
+                    cols = slice(half * T // 2, (half + 1) * T // 2)
+                    nc.vector.tensor_tensor(q_win[kb][:, cols], q_win[kb][:, cols], r_win[kb][:, cols], ALU.add)
+                    queue.dma_start(out[rows, cols], q_win[kb][:, cols])

@@ -40,6 +40,10 @@ def tile_moe_plb_silu_kernel(
         nc.gpsimd.memset(w2_sc_raw[:].bitcast(I32), 0)
         nc.gpsimd.tensor_copy(warm[:], zero[:])
         nc.gpsimd.memset(dy_sc[:].bitcast(I32), 0)
+        wb_sc = tile([P, E2, K], U8, "wb_sc")
+        wa_sc = tile([P, E1, K], U8, "wa_sc")
+        nc.gpsimd.memset(wb_sc[:].rearrange("p f k -> p (f k)").bitcast(I32), 0)
+        nc.gpsimd.memset(wa_sc[:].rearrange("p f k -> p (f k)").bitcast(I32), 0)
 
         idx2 = tile([P, T // 16], U16, "idx2")
         idx1 = tile([P, T // 16], U16, "idx1")
@@ -62,7 +66,7 @@ def tile_moe_plb_silu_kernel(
         a_v = a.rearrange("(p j) t -> p j t", j=4)
         c_v = c.rearrange("(p j) t -> p j t", j=4)
         a_sb = {}
-        for h, lo, hi in ((0, 0, 2), (0, 2, 3), (1, 0, 1), (1, 1, 2), (1, 2, 3)):
+        for h, lo, hi in ((0, 0, 1), (0, 1, 2), (0, 2, 3), (1, 0, 1), (1, 1, 2), (1, 2, 3)):
             part = a_all[:, h, 2 * lo * TC : 2 * hi * TC].rearrange("p (e t) -> p e t", e=2)
             nc.sync.dma_start(part, a_v[:, 2 * h : 2 * h + 2, lo * TC : hi * TC])
             for g in range(lo, hi):
@@ -81,10 +85,8 @@ def tile_moe_plb_silu_kernel(
             out=w2_sc[:].rearrange("p (j m) -> p m j", j=4),
             in_=w2_sc_raw[:].rearrange("p (m j) -> p m j", j=4),
         )
-        wb_sc = tile([P, E2, K], U8, "wb_sc", tag="w2_sc_raw")
-        nc.gpsimd.memset(wb_sc[:].rearrange("p f k -> p (f k)").bitcast(I32), 0)
         for r in range(4):
-            nc.gpsimd.dma_start(wb_sc[r:P:32, :, :].bitcast(I32), wb_sc_hbm[r])
+            nc.sync.dma_start(wb_sc[r:P:32, :, :].bitcast(I32), wb_sc_hbm[r])
         wb = tile([P, E2, 2 * K], U8, "wb", tag="w2_raw")
         nc.sync.dma_start(wb[:].bitcast(I32), wbt_words.bitcast(I32).rearrange("f s p k -> p (f s) k"))
 
@@ -114,8 +116,6 @@ def tile_moe_plb_silu_kernel(
         for h in range(2):
             nc.sync.dma_start(c_sb[h], c_v[:, 2 * h : 2 * h + 2, :])
 
-        wa_sc = tile([P, E1, K], U8, "wa_sc", tag="w2_sc")
-        nc.gpsimd.memset(wa_sc[:].rearrange("p f k -> p (f k)").bitcast(I32), 0)
         for r in range(4):
             nc.sync.dma_start(wa_sc[r:P:32, :, :].bitcast(I32), wa_sc_hbm[r])
 
@@ -151,33 +151,41 @@ def tile_moe_plb_silu_kernel(
         z = [tile([P, 3, 2 * TC], F32, f"z{h}", tag=f"y1{1 + h}") for h in range(2)]
         da = [tile([P, 2, T], BF16, f"da{h}") for h in range(2)]
 
-        def factor(h, g):
-            zv = z[h][:, g, :].rearrange("p (e t) -> p e t", e=2)
-            nc.scalar.activation(zv, a_sb[h, g], ACT.Silu, scale=-1.0)
-            nc.vector.scalar_tensor_tensor(
-                z[h][:, g, :], z[h][:, g, :], 1.0, dh[h, g][:].rearrange("p e t -> p (e t)"), ALU.subtract, ALU.mult
-            )
-            nc.gpsimd.tensor_tensor(zv, zv, c_sb[h][:, :, g * TC : (g + 1) * TC], ALU.mult)
+        def silu_neg(h):
+            for g in range(3):
+                nc.scalar.activation(z[h][:, g, :].rearrange("p (e t) -> p e t", e=2), a_sb[h, g], ACT.Silu, scale=-1.0)
 
-        factor(0, 0)
+        silu_neg(0)
+
         NA = 256
+        NB = T - NA
+        gB = tile([P, 2, NB], U32, "gB")
         gA = tile([P, 2, NA], U32, "gA")
+        wB = tile([P, NB, 2], U32, "wB")
+        wA = tile([P, NA, 2], U32, "wA")
+        for h in range(2):
+            nc.vector.tensor_copy(gB[:, h, :], dc_words(h).indirect(offsets(idx2, NA, T)))
+        nc.scalar.copy(wB[:], gB[:].rearrange("p h n -> p n h"))
         for h in range(2):
             nc.vector.tensor_copy(gA[:, h, :], dc_words(h).indirect(offsets(idx2, 0, NA)))
-        NB = T - NA
-        gB = tile([P, 2 * NB], U32, "gB")
-        wA = gB[:, NB : 2 * NB]
-        nc.scalar.copy(wA.rearrange("p (n h) -> p n h", h=2), gA[:].rearrange("p h n -> p n h"))
-        factor(0, 1)
-        nc.vector.tensor_copy(gB[:, 0:NB], dc_words(0).indirect(offsets(idx2, NA, T)))
-        cA, sA = quantise(wA.bitcast(BF16), NA, "qA")
-        factor(0, 2)
-        nc.vector.tensor_copy(gB[:, NB : 2 * NB], dc_words(1).indirect(offsets(idx2, NA, T)))
+        nc.scalar.copy(wA[:], gA[:].rearrange("p h n -> p n h"))
+        silu_neg(1)
+        cB, sB = quantise(wB[:].rearrange("p n h -> p (n h)").bitcast(BF16), NB, "qB")
+        cA, sA = quantise(wA[:].rearrange("p n h -> p (n h)").bitcast(BF16), NA, "qA")
+        u_first = tile([P, 1, 2 * TC], F32, "u_first")
+        u_rest = tile([P, 5, 2 * TC], F32, "u_rest", tag="wB")
+
+        def u_sb(h, lo, hi):
+            return u_first[:] if (h, lo) == (0, 0) else u_rest[:, 3 * h + lo - 1 : 3 * h + hi - 1, :]
+
+        for h in range(2):
+            for g in range(3):
+                nc.vector.scalar_tensor_tensor(
+                    u_sb(h, g, g + 1)[:, 0, :], z[h][:, g, :], 1.0, dh[h, g][:].rearrange("p e t -> p (e t)"), ALU.subtract, ALU.mult
+                )
         wa = tile([P, E1, K], U32, "wa", tag="dc0")
         nc.sync.dma_start(wa[:].bitcast(I32), wat_words.rearrange("e s p k d -> p (e s) (k d)").bitcast(I32))
 
-        for g in range(3):
-            factor(1, g)
         banksA = []
         for b in range(2):
             bank = ps.tile([P, 2, NA], F32, name=f"qA{b}", tag=f"bank{6 + b}")
@@ -189,15 +197,32 @@ def tile_moe_plb_silu_kernel(
         nc.scalar.copy(stA[0][:], banksA[0][:])
         for u in range(2):
             scatter(q_win[u], idx2, 0, NA, stA[0][:, u, :])
-        wB = tile([P, T - NA, 2], U32, "wB")
-        nc.scalar.copy(wB[:], gB[:].rearrange("p (h n) -> p n h", h=2))
+        sg = tile([P, 2, 2 * T], F32, "sg", tag="qA_codes")
+
+        def sigmoid(h):
+            nc.scalar.activation(sg[:, h, :], a_all[:, h, :], ACT.Sigmoid)
+
         nc.scalar.copy(stA[1][:], banksA[1][:])
-        cB, sB = quantise(wB[:].rearrange("p n h -> p (n h)").bitcast(BF16), T - NA, "qB")
+        sigmoid(0)
         for u in range(2):
             scatter(q_win[2 + u], idx2, 0, NA, stA[1][:, u, :])
+        sigmoid(1)
         for h in range(2):
-            for g in range(3):
-                nc.scalar.activation(a_sb[h, g], a_sb[h, g], ACT.Sigmoid)
+            mm = tile([P, 2, T], F32, f"mm{h}", tag="wA")
+            for lo, hi in ((0, 1), (1, 2), (2, 3)) if h == 0 else ((0, 3),):
+                nc.gpsimd.tensor_tensor(
+                    mm[:].rearrange("p e (g t) -> p g e t", g=3)[:, lo:hi],
+                    u_sb(h, lo, hi).rearrange("p g (e t) -> p g e t", e=2),
+                    c_sb[h].rearrange("p e (g t) -> p g e t", g=3)[:, lo:hi],
+                    ALU.mult,
+                )
+            for e in range(2):
+                nc.gpsimd.tensor_tensor(
+                    da[h][:, e, :].rearrange("p (g t) -> p g t", g=3),
+                    mm[:, e, :].rearrange("p (g t) -> p g t", g=3),
+                    sg[:, h, :].rearrange("p (g e t) -> p e g t", g=3, e=2)[:, e],
+                    ALU.mult,
+                )
         banksB = []
         for kb in range(4):
             bank = ps.tile([P, T - NA], F32, name=f"qB{kb}", tag=f"bank{6 + kb % 2}")
@@ -208,15 +233,6 @@ def tile_moe_plb_silu_kernel(
                 stB = tile([P, T - NA], F32, f"stB{kb}")
                 nc.scalar.copy(stB[:], bank[:])
                 scatter(q_win[kb], idx2, NA, T, stB[:])
-
-        for h in range(2):
-            for g in range(3):
-                nc.gpsimd.tensor_tensor(
-                    da[h][:, :, g * TC : (g + 1) * TC],
-                    z[h][:, g, :].rearrange("p (e t) -> p e t", e=2),
-                    a_sb[h, g],
-                    ALU.mult,
-                )
 
         def r_gather(dst, j, lo, hi):
             nc.scalar.activation(dst[:, :, j], da[j // 2][:, j % 2, :].indirect(offsets(idx1, lo, hi)), ACT.Copy, scale=-1.0)
@@ -234,7 +250,7 @@ def tile_moe_plb_silu_kernel(
 
         g1 = tile([P, C1, 4], BF16, "g1")
         g2 = tile([P, T - C1, 4], BF16, "g2")
-        stB3 = tile([P, T - NA], F32, "stB3", tag="y12")
+        stB3 = tile([P, T - NA], F32, "stB3", tag="wA")
         r_gather(g1, 0, 0, C1)
         r_gather(g1, 1, 0, C1)
         r_gather(g2, 0, C1, T)

@@ -17,8 +17,9 @@ K, T, H, N = 512, 768, 512, 1024
 E1, C1, E2, C2 = 3, 256, 6, 128
 P = 128
 TC = 256
+HEAD = 256
+REST = T - HEAD
 FLOPS = 2 * N * H * T + 2 * 2 * H * K * T
-USE_G = True
 
 
 def tile_moe_plb_silu_kernel(
@@ -32,70 +33,78 @@ def tile_moe_plb_silu_kernel(
         def tile(shape, dtype, name, tag=None):
             return sb.tile(shape, dtype, name=name, tag=tag or name, align_bytes=64)
 
+        def bank_tile(shape, name, number):
+            return ps.tile(shape, F32, name=name, tag=f"bank{number}")
+
         w2_sc_raw = tile([P, H], U8, "w2_sc_raw")
         dy_sc = tile([P, T], U8, "dy_sc")
-        warm = tile([P, 1], F32, "warm", tag="a_all")
-        zero = tile([P, 1], F32, "zero", tag="dy")
-        nc.gpsimd.memset(zero[:], 0.0)
-        nc.gpsimd.memset(w2_sc_raw[:].bitcast(I32), 0)
-        nc.gpsimd.tensor_copy(warm[:], zero[:])
-        nc.gpsimd.memset(dy_sc[:].bitcast(I32), 0)
         wb_sc = tile([P, E2, K], U8, "wb_sc")
         wa_sc = tile([P, E1, K], U8, "wa_sc")
+        nc.vector.memset(w2_sc_raw[:].bitcast(I32), 0)
+        nc.vector.memset(dy_sc[:].bitcast(I32), 0)
         nc.gpsimd.memset(wb_sc[:].rearrange("p f k -> p (f k)").bitcast(I32), 0)
         nc.gpsimd.memset(wa_sc[:].rearrange("p f k -> p (f k)").bitcast(I32), 0)
 
-        idx2 = tile([P, T // 16], U16, "idx2")
-        idx1 = tile([P, T // 16], U16, "idx1")
-        nc.sync.dma_start(idx2[:], offs2)
-        nc.sync.dma_start(idx1[:], offs)
-        w2_raw = tile([P, 2, H], U32, "w2_raw", tag="w2_raw")
-        nc.sync.dma_start(w2_raw[:].bitcast(I32), w2t_words.rearrange("s p i d -> p s (i d)").bitcast(I32))
         w2_sc_hbm = w2t_scales.bitcast(I32)
         dy_sc_hbm = dy_scales.bitcast(I32)
         for q in range(4):
-            (nc.scalar if q < 2 else nc.sync).dma_start(w2_sc_raw[32 * q : 32 * q + 8, :].bitcast(I32), w2_sc_hbm[:, 4 * q : 4 * q + 4, :])
-        dy = tile([P, 2, T], U32, "dy", tag="dy")
+            nc.sync.dma_start(w2_sc_raw[32 * q : 32 * q + 8, :].bitcast(I32), w2_sc_hbm[:, 4 * q : 4 * q + 4, :])
+        w2_raw = tile([P, 2, H], U32, "w2_raw")
+        nc.sync.dma_start(w2_raw[:].bitcast(I32), w2t_words.rearrange("s p i d -> p s (i d)").bitcast(I32))
+        dy = tile([P, 2, T], U32, "dy")
         nc.sync.dma_start(dy[:].bitcast(I32), dy_words.rearrange("s p t d -> p s (t d)").bitcast(I32))
-        warm_out = tile([P, 1], F32, "warm_out")
-        nc.scalar.activation(warm_out[:], warm[:], ACT.Silu)
         for q in range(4):
             nc.sync.dma_start(dy_sc[32 * q : 32 * q + 8, :].bitcast(I32), dy_sc_hbm[:, 4 * q : 4 * q + 4, :])
 
-        a_all = tile([P, 4, 2 * T], F32, "a_all", tag="a_all")
+        a_all = tile([P, 6, 2, TC], F32, "a_all")
         a_v = a.rearrange("(p j) t -> p j t", j=4)
         c_v = c.rearrange("(p j) t -> p j t", j=4)
-        a_sb = {}
-        for h, lo, hi in ((0, 0, 1), (0, 1, 2), (0, 2, 3), (1, 0, 1), (1, 1, 2), (1, 2, 3)):
-            part = a_all[:, h, 2 * lo * TC : 2 * hi * TC].rearrange("p (e t) -> p e t", e=2)
-            nc.sync.dma_start(part, a_v[:, 2 * h : 2 * h + 2, lo * TC : hi * TC])
-            for g in range(lo, hi):
-                a_sb[h, g] = part[:, :, (g - lo) * TC : (g - lo + 1) * TC]
+        for h in range(2):
+            for g in range(3):
+                nc.sync.dma_start(a_all[:, 3 * h + g], a_v[:, 2 * h : 2 * h + 2, g * TC : (g + 1) * TC])
+        idx2 = tile([P, T // 16], U16, "idx2")
+        idx1 = tile([P, T // 16], U16, "idx1")
+        nc.sync.dma_start(idx2[:], offs2)
         wb_sc_hbm = wbt_scales.bitcast(I32).rearrange("f s (q r) k -> r q (f s) k", r=4)
         wa_sc_hbm = wat_scales.bitcast(I32).rearrange("f s (q r) k -> r q (f s) k", r=4)
+        for r in range(4):
+            nc.sync.dma_start(wb_sc[r:P:32, :, :].bitcast(I32), wb_sc_hbm[r])
+        wb = tile([P, E2, 2 * K], U8, "wb")
+        nc.sync.dma_start(wb[:].bitcast(I32), wbt_words.bitcast(I32).rearrange("f s p k -> p (f s) k"))
+        c_sb = [tile([P, 2, T], F32, f"c{h}") for h in range(2)]
+        for h in range(2):
+            nc.sync.dma_start(c_sb[h][:], c_v[:, 2 * h : 2 * h + 2, :])
+        nc.sync.dma_start(idx1[:], offs)
+        for r in range(4):
+            nc.sync.dma_start(wa_sc[r:P:32, :, :].bitcast(I32), wa_sc_hbm[r])
+        wa = tile([P, E1, K], U32, "wa")
+        nc.sync.dma_start(wa[:].bitcast(I32), wat_words.rearrange("e s p k d -> p (e s) (k d)").bitcast(I32))
 
-        w2 = tile([P, 2, H], U32, "w2", tag="w2")
+        w2 = tile([P, 2, H], U32, "w2")
         w2_sc = tile([P, H], U8, "w2_sc")
+        nc.vector.tensor_copy(
+            out=w2_sc[:].rearrange("p (j m) -> p m j", j=4),
+            in_=w2_sc_raw[:].rearrange("p (m j) -> p m j", j=4),
+        )
         for s in range(2):
             nc.vector.tensor_copy(
                 out=w2[:, s, :].bitcast(I32).rearrange("p (j b i) -> p b j i", j=4, i=4),
                 in_=w2_raw[:, s, :].bitcast(I32).rearrange("p (b i j) -> p b j i", j=4, i=4),
             )
-        nc.vector.tensor_copy(
-            out=w2_sc[:].rearrange("p (j m) -> p m j", j=4),
-            in_=w2_sc_raw[:].rearrange("p (m j) -> p m j", j=4),
-        )
-        for r in range(4):
-            nc.sync.dma_start(wb_sc[r:P:32, :, :].bitcast(I32), wb_sc_hbm[r])
-        wb = tile([P, E2, 2 * K], U8, "wb", tag="w2_raw")
-        nc.sync.dma_start(wb[:].bitcast(I32), wbt_words.bitcast(I32).rearrange("f s p k -> p (f s) k"))
 
-        dh = {}
         dc = [tile([P, T, 2], BF16, f"dc{h}") for h in range(2)]
+        pn = [tile([P, T, 2], F32, f"pn{h}") for h in range(2)]
+
+        def make_dc(h):
+            for g in range(3):
+                cols = slice(g * TC, (g + 1) * TC)
+                nc.vector.scalar_tensor_tensor(
+                    dc[h][:, cols, :], pn[h][:, cols, :], -1.0, a_all[:, 3 * h + g].rearrange("p e t -> p t e"), ALU.mult, ALU.mult
+                )
+
         for h in range(2):
             for g in range(3):
-                bank = ps.tile([P, 2, TC], F32, name=f"dh{h}{g}", tag=f"bank{3 * h + g}")
-                dh[h, g] = bank
+                bank = bank_tile([P, 2, TC], f"dh{h}{g}", 3 * h + g)
                 cols = slice(g * TC, (g + 1) * TC)
                 for e in range(2):
                     j = 2 * h + e
@@ -109,26 +118,31 @@ def tile_moe_plb_silu_kernel(
                             start=(s == 0),
                             stop=(s == 1),
                         )
-                y = tile([P, TC, 2], F32, f"y{h}{g}")
-                nc.scalar.activation(y[:], a_sb[h, g].rearrange("p e t -> p t e"), ACT.Silu, bias=warm_out[:])
-                nc.vector.tensor_tensor(dc[h][:, cols, :], bank[:].rearrange("p e t -> p t e"), y[:], ALU.mult)
-        c_sb = [a_all[:, 2 + h, :].rearrange("p (e t) -> p e t", e=2) for h in range(2)]
-        for h in range(2):
-            nc.sync.dma_start(c_sb[h], c_v[:, 2 * h : 2 * h + 2, :])
-
-        for r in range(4):
-            nc.sync.dma_start(wa_sc[r:P:32, :, :].bitcast(I32), wa_sc_hbm[r])
+                sg = tile([P, TC, 2], F32, f"sg{h}{g}")
+                nc.scalar.activation(sg[:], a_all[:, 3 * h + g].rearrange("p e t -> p t e"), ACT.Sigmoid)
+                nc.vector.scalar_tensor_tensor(pn[h][:, cols, :], bank[:].rearrange("p e t -> p t e"), -1.0, sg[:], ALU.mult, ALU.mult)
+            make_dc(h)
+        z = tile([P, 6, TC, 2], F32, "z")
+        nc.scalar.activation(z[:], a_all[:].rearrange("p k e t -> p k t e"), ACT.Silu, scale=-1.0)
 
         def offsets(idx, lo, hi):
             return idx[:, lo // 16 : hi // 16]
 
-        def dc_words(h):
-            return dc[h][:].rearrange("p t e -> p (t e)").bitcast(U32)
+        def gather(dst, src, idx, lo, hi):
+            nc.vector.tensor_copy(dst, src[:].rearrange("p t e -> p (t e)").bitcast(U32).indirect(offsets(idx, lo, hi)))
 
-        def quantise(src, n, name, tag=None):
-            codes = tile([P, n], U32, name + "_codes", tag=tag)
+        def weave_vector(dst, src):
+            nc.vector.tensor_copy(
+                dst[:].bitcast(I32).rearrange("p (b i) h -> p b h i", i=4), src[:].bitcast(I32).rearrange("p h (b i) -> p b h i", i=4)
+            )
+
+        def weave_scalar(dst, src):
+            nc.scalar.copy(dst[:], src[:].rearrange("p h n -> p n h"))
+
+        def quantise(src, n, name):
+            codes = tile([P, n], U32, name + "_codes")
             scales = tile([P, n], U8, name + "_scales")
-            nc.vector.quantize_mx(out=codes[:].bitcast(FP8X4), scales=scales[:], in_=src)
+            nc.vector.quantize_mx(out=codes[:].bitcast(FP8X4), scales=scales[:], in_=src[:].rearrange("p n h -> p (n h)").bitcast(BF16))
             return codes, scales
 
         def q_matmul(dst, f, kb, codes, scales, lo):
@@ -142,101 +156,6 @@ def tile_moe_plb_silu_kernel(
                 stop=True,
             )
 
-        q_win = [tile([P, T], F32, f"q_win{kb}") for kb in range(4)]
-        r_win = [tile([P, T], F32, f"r_win{kb}") for kb in range(4)]
-
-        def scatter(win, idx, lo, hi, src):
-            nc.vector.tensor_copy(win[:].indirect(offsets(idx, lo, hi)), src)
-
-        z = [tile([P, 3, 2 * TC], F32, f"z{h}", tag=f"y1{1 + h}") for h in range(2)]
-        da = [tile([P, 2, T], BF16, f"da{h}") for h in range(2)]
-
-        def silu_neg(h):
-            for g in range(3):
-                nc.scalar.activation(z[h][:, g, :].rearrange("p (e t) -> p e t", e=2), a_sb[h, g], ACT.Silu, scale=-1.0)
-
-        silu_neg(0)
-
-        NA = 256
-        NB = T - NA
-        gB = tile([P, 2, NB], U32, "gB")
-        gA = tile([P, 2, NA], U32, "gA")
-        wB = tile([P, NB, 2], U32, "wB")
-        wA = tile([P, NA, 2], U32, "wA")
-        for h in range(2):
-            nc.vector.tensor_copy(gB[:, h, :], dc_words(h).indirect(offsets(idx2, NA, T)))
-        nc.scalar.copy(wB[:], gB[:].rearrange("p h n -> p n h"))
-        for h in range(2):
-            nc.vector.tensor_copy(gA[:, h, :], dc_words(h).indirect(offsets(idx2, 0, NA)))
-        nc.scalar.copy(wA[:], gA[:].rearrange("p h n -> p n h"))
-        silu_neg(1)
-        cB, sB = quantise(wB[:].rearrange("p n h -> p (n h)").bitcast(BF16), NB, "qB")
-        cA, sA = quantise(wA[:].rearrange("p n h -> p (n h)").bitcast(BF16), NA, "qA")
-        u_first = tile([P, 1, 2 * TC], F32, "u_first")
-        u_rest = tile([P, 5, 2 * TC], F32, "u_rest", tag="wB")
-
-        def u_sb(h, lo, hi):
-            return u_first[:] if (h, lo) == (0, 0) else u_rest[:, 3 * h + lo - 1 : 3 * h + hi - 1, :]
-
-        for h in range(2):
-            for g in range(3):
-                nc.vector.scalar_tensor_tensor(
-                    u_sb(h, g, g + 1)[:, 0, :], z[h][:, g, :], 1.0, dh[h, g][:].rearrange("p e t -> p (e t)"), ALU.subtract, ALU.mult
-                )
-        wa = tile([P, E1, K], U32, "wa", tag="dc0")
-        nc.sync.dma_start(wa[:].bitcast(I32), wat_words.rearrange("e s p k d -> p (e s) (k d)").bitcast(I32))
-
-        banksA = []
-        for b in range(2):
-            bank = ps.tile([P, 2, NA], F32, name=f"qA{b}", tag=f"bank{6 + b}")
-            for u in range(2):
-                for f in range(2):
-                    q_matmul(bank[:, u, f * C2 : (f + 1) * C2], f, 2 * b + u, cA, sA, f * C2)
-            banksA.append(bank)
-        stA = [tile([P, 2, NA], F32, f"stA{b}") for b in range(2)]
-        nc.scalar.copy(stA[0][:], banksA[0][:])
-        for u in range(2):
-            scatter(q_win[u], idx2, 0, NA, stA[0][:, u, :])
-        sg = tile([P, 2, 2 * T], F32, "sg", tag="qA_codes")
-
-        def sigmoid(h):
-            nc.scalar.activation(sg[:, h, :], a_all[:, h, :], ACT.Sigmoid)
-
-        nc.scalar.copy(stA[1][:], banksA[1][:])
-        sigmoid(0)
-        for u in range(2):
-            scatter(q_win[2 + u], idx2, 0, NA, stA[1][:, u, :])
-        sigmoid(1)
-        for h in range(2):
-            mm = tile([P, 2, T], F32, f"mm{h}", tag="wA")
-            for lo, hi in ((0, 1), (1, 2), (2, 3)) if h == 0 else ((0, 3),):
-                nc.gpsimd.tensor_tensor(
-                    mm[:].rearrange("p e (g t) -> p g e t", g=3)[:, lo:hi],
-                    u_sb(h, lo, hi).rearrange("p g (e t) -> p g e t", e=2),
-                    c_sb[h].rearrange("p e (g t) -> p g e t", g=3)[:, lo:hi],
-                    ALU.mult,
-                )
-            for e in range(2):
-                nc.gpsimd.tensor_tensor(
-                    da[h][:, e, :].rearrange("p (g t) -> p g t", g=3),
-                    mm[:, e, :].rearrange("p (g t) -> p g t", g=3),
-                    sg[:, h, :].rearrange("p (g e t) -> p e g t", g=3, e=2)[:, e],
-                    ALU.mult,
-                )
-        banksB = []
-        for kb in range(4):
-            bank = ps.tile([P, T - NA], F32, name=f"qB{kb}", tag=f"bank{6 + kb % 2}")
-            for f in range(2, E2):
-                q_matmul(bank[:, (f - 2) * C2 : (f - 1) * C2], f, kb, cB, sB, (f - 2) * C2)
-            banksB.append(bank)
-            if kb < 3:
-                stB = tile([P, T - NA], F32, f"stB{kb}")
-                nc.scalar.copy(stB[:], bank[:])
-                scatter(q_win[kb], idx2, NA, T, stB[:])
-
-        def r_gather(dst, j, lo, hi):
-            nc.scalar.activation(dst[:, :, j], da[j // 2][:, j % 2, :].indirect(offsets(idx1, lo, hi)), ACT.Copy, scale=-1.0)
-
         def r_matmul(dst, e, kb, codes, scales, lo):
             nc.tensor.matmul_mx(
                 out=dst,
@@ -248,47 +167,118 @@ def tile_moe_plb_silu_kernel(
                 stop=True,
             )
 
-        g1 = tile([P, C1, 4], BF16, "g1")
-        g2 = tile([P, T - C1, 4], BF16, "g2")
-        stB3 = tile([P, T - NA], F32, "stB3", tag="wA")
-        r_gather(g1, 0, 0, C1)
-        r_gather(g1, 1, 0, C1)
-        r_gather(g2, 0, C1, T)
-        r_gather(g2, 1, C1, T)
-        nc.scalar.copy(stB3[:, 0:256], banksB[3][:, 0:256])
-        scatter(q_win[3], idx2, NA, NA + 256, stB3[:, 0:256])
-        r_gather(g1, 2, 0, C1)
-        r_gather(g1, 3, 0, C1)
-        c1, s1 = quantise(g1[:].rearrange("p n j -> p (n j)"), C1, "r1")
-        nc.scalar.copy(stB3[:, 256:512], banksB[3][:, 256:512])
-        scatter(q_win[3], idx2, NA + 256, T, stB3[:, 256:512])
-        st1 = []
-        for b in range(2):
-            bank = ps.tile([P, 2, C1], F32, name=f"r1{b}", tag=f"bank{b}")
-            for u in range(2):
-                r_matmul(bank[:, u, :], 0, 2 * b + u, c1, s1, 0)
-            for u in range(2):
-                st1.append(tile([P, C1], F32, f"st1{2 * b + u}"))
-                nc.scalar.copy(st1[-1][:], bank[:, u, :])
-        scatter(r_win[0], idx1, 0, C1, st1[0][:])
-        r_gather(g2, 2, C1, T)
-        r_gather(g2, 3, C1, T)
-        c2, s2 = quantise(g2[:].rearrange("p n j -> p (n j)"), T - C1, "r2", tag="st10")
-        for kb in range(1, 4):
-            scatter(r_win[kb], idx1, 0, C1, st1[kb][:])
-        for kb in range(4):
-            bank = ps.tile([P, 2, C1], F32, name=f"r2{kb}", tag=f"bank{2 + kb}")
-            for u in range(2):
-                r_matmul(bank[:, u, :], 1 + u, kb, c2, s2, u * C1)
-            st2 = tile([P, T - C1], F32, f"st2{kb}")
-            nc.scalar.copy(st2[:], bank[:].rearrange("p u n -> p (u n)"))
-            scatter(r_win[kb], idx1, C1, T, st2[:])
+        q_win = [tile([P, T], F32, f"q_win{kb}") for kb in range(4)]
+        r_win = [tile([P, T], F32, f"r_win{kb}") for kb in range(4)]
+
+        def scatter_vector(win, idx, lo, hi, src):
+            nc.vector.tensor_copy(win[:].indirect(offsets(idx, lo, hi)), src)
+
+        def scatter_scalar(win, idx, lo, hi, src):
+            nc.scalar.activation(win[:].indirect(offsets(idx, lo, hi)), src, ACT.Copy)
+
+        qgA = tile([P, 2, HEAD], U32, "qgA")
+        qgB = tile([P, 2, REST], U32, "qgB")
+        qwA = tile([P, HEAD, 2], U32, "qwA", tag="w0")
+        qwB = tile([P, REST, 2], U32, "qwB", tag="da0")
+        gather(qgA[:, 0, :], dc[0], idx2, 0, HEAD)
+        gather(qgA[:, 1, :], dc[1], idx2, 0, HEAD)
+        weave_scalar(qwA, qgA)
+        gather(qgB[:, 0, :], dc[0], idx2, HEAD, T)
+        qcA, qsA = quantise(qwA, HEAD, "qA")
+        gather(qgB[:, 1, :], dc[1], idx2, HEAD, T)
+        w = [tile([P, T, 2], F32, "w0", tag="w0"), tile([P, T, 2], F32, "w1", tag="qgB")]
+
+        def make_w(h):
+            nc.vector.scalar_tensor_tensor(
+                w[h][:], z[:, 3 * h : 3 * h + 3].rearrange("p g t e -> p (g t) e"), 1.0, c_sb[h][:].rearrange("p e t -> p t e"), ALU.subtract, ALU.mult
+            )
+
+        make_w(0)
+        weave_vector(qwB, qgB)
+        make_w(1)
+        qcB, qsB = quantise(qwB, REST, "qB")
+        da = [tile([P, T, 2], BF16, f"da{h}") for h in range(2)]
+        for h in range(2):
+            nc.gpsimd.tensor_tensor(da[h][:], pn[h][:], w[h][:], ALU.mult)
+
+        def head_products(matmuls, name, number, blocks):
+            bank = bank_tile([P, 2, HEAD], name, number)
+            for u, kb in enumerate(blocks):
+                matmuls(bank[:, u, :], kb)
+            stage = tile([P, 2, HEAD], F32, name + "_stage")
+            nc.scalar.copy(stage[:], bank[:])
+            return stage
+
+        def q_head(dst, kb):
+            for f in range(2):
+                q_matmul(dst[:, f * C2 : (f + 1) * C2], f, kb, qcA, qsA, f * C2)
+
+        for number, blocks in ((6, (2, 3)), (7, (0, 1))):
+            stage = head_products(q_head, f"qA{number}", number, blocks)
+            for u, kb in enumerate(blocks):
+                scatter_scalar(q_win[kb], idx2, 0, HEAD, stage[:, u, :])
+        q_banks = {}
+        for kb in (2, 0, 3, 1):
+            q_banks[kb] = bank_tile([P, REST], f"qB{kb}", kb)
+            for f in range(2, E2):
+                q_matmul(q_banks[kb][:, (f - 2) * C2 : (f - 1) * C2], f, kb, qcB, qsB, (f - 2) * C2)
+        stq = {kb: tile([P, REST], F32, f"stq{kb}") for kb in range(3)}
+        stq3 = tile([P, 256], F32, "stq3")
+        nc.vector.tensor_copy(stq[2][:], q_banks[2][:])
+        nc.vector.tensor_copy(stq3[:], q_banks[3][:, 0:256])
+        scatter_vector(q_win[2], idx2, HEAD, T, stq[2][:])
+        scatter_vector(q_win[3], idx2, HEAD, HEAD + 256, stq3[:])
+        for kb in range(2):
+            nc.scalar.copy(stq[kb][:], q_banks[kb][:])
+            for lo in (0, 256):
+                scatter_scalar(q_win[kb], idx2, HEAD + lo, HEAD + lo + 256, stq[kb][:, lo : lo + 256])
+
+        rgA = tile([P, 2, HEAD], U32, "rgA")
+        rgB = tile([P, 2, REST], U32, "rgB")
+        rwA = tile([P, HEAD, 2], U32, "rwA")
+        rwB = tile([P, REST, 2], U32, "rwB")
+        gather(rgA[:, 0, :], da[0], idx1, 0, HEAD)
+        gather(rgB[:, 0, :], da[0], idx1, HEAD, T)
+        gather(rgA[:, 1, :], da[1], idx1, 0, HEAD)
+        weave_vector(rwA, rgA)
+        rcA, rsA = quantise(rwA, HEAD, "rA")
+        gather(rgB[:, 1, :], da[1], idx1, HEAD, T)
+        weave_vector(rwB, rgB)
+        rcB, rsB = quantise(rwB, REST, "rB")
+
+        def r_head(dst, kb):
+            r_matmul(dst, 0, kb, rcA, rsA, 0)
+
+        for number, blocks in ((4, (0, 1)), (5, (3, 2))):
+            stage = head_products(r_head, f"rA{number}", number, blocks)
+            for u, kb in enumerate(blocks):
+                scatter_scalar(r_win[kb], idx1, 0, HEAD, stage[:, u, :])
+
+        def finish(kb):
             rows = slice(kb * P, (kb + 1) * P)
-            if kb < 3:
-                nc.gpsimd.tensor_tensor(q_win[kb][:], q_win[kb][:], r_win[kb][:], ALU.add)
-                nc.sync.dma_start(out[rows, :], q_win[kb][:])
+            nc.gpsimd.tensor_tensor(q_win[kb][:], q_win[kb][:], r_win[kb][:], ALU.add)
+            nc.sync.dma_start(out[rows, :], q_win[kb][:])
+
+        for kb, number in ((0, 6), (1, 7), (2, 0), (3, 1)):
+            bank = bank_tile([P, 2, C1], f"rB{kb}", number)
+            for u in range(2):
+                r_matmul(bank[:, u, :], 1 + u, kb, rcB, rsB, u * C1)
+            stage = tile([P, REST], F32, f"str{kb}")
+            if kb == 0:
+                nc.vector.tensor_copy(stage[:], bank[:].rearrange("p u n -> p (u n)"))
             else:
-                for half, queue in enumerate((nc.scalar, nc.scalar)):
-                    cols = slice(half * T // 2, (half + 1) * T // 2)
-                    nc.vector.tensor_tensor(q_win[kb][:, cols], q_win[kb][:, cols], r_win[kb][:, cols], ALU.add)
-                    queue.dma_start(out[rows, cols], q_win[kb][:, cols])
+                nc.scalar.copy(stage[:], bank[:].rearrange("p u n -> p (u n)"))
+            if kb == 2:
+                for lo in (0, 256):
+                    scatter_scalar(r_win[kb], idx1, HEAD + lo, HEAD + lo + 256, stage[:, lo : lo + 256])
+            else:
+                scatter_vector(r_win[kb], idx1, HEAD, T, stage[:])
+            if kb < 3:
+                finish(kb)
+        last = tile([P, 256], F32, "last", tag="str2")
+        nc.scalar.copy(last[:], q_banks[3][:, 256:512])
+        scatter_scalar(q_win[3], idx2, HEAD + 256, T, last[:])
+        for half in range(2):
+            cols = slice(half * T // 2, (half + 1) * T // 2)
+            nc.vector.tensor_tensor(q_win[3][:, cols], q_win[3][:, cols], r_win[3][:, cols], ALU.add)
+            nc.sync.dma_start(out[3 * P : 4 * P, cols], q_win[3][:, cols])

@@ -40,45 +40,42 @@ def tile_moe_plb_silu_kernel(
         dy_sc = tile([P, T], U8, "dy_sc")
         wb_sc = tile([P, E2, K], U8, "wb_sc")
         wa_sc = tile([P, E1, K], U8, "wa_sc")
-        nc.vector.memset(w2_sc_raw[:].bitcast(I32), 0)
-        nc.vector.memset(dy_sc[:].bitcast(I32), 0)
+        blank_w2 = tile([P, H // 4], I32, "blank_w2", tag="dy")
+        blank_dy = tile([P, T // 4], I32, "blank_dy", tag="ac")
+        nc.gpsimd.memset(blank_w2[:], 0)
+        nc.gpsimd.tensor_copy(w2_sc_raw[:].bitcast(I32), blank_w2[:])
+        nc.gpsimd.memset(blank_dy[:], 0)
+        nc.gpsimd.tensor_copy(dy_sc[:].bitcast(I32), blank_dy[:])
         nc.gpsimd.memset(wb_sc[:].rearrange("p f k -> p (f k)").bitcast(I32), 0)
         nc.gpsimd.memset(wa_sc[:].rearrange("p f k -> p (f k)").bitcast(I32), 0)
 
+        idx2 = tile([P, T // 16], U16, "idx2")
+        idx1 = tile([P, T // 16], U16, "idx1")
+        nc.sync.dma_start(idx2[:], offs2)
+        nc.sync.dma_start(idx1[:], offs)
         w2_sc_hbm = w2t_scales.bitcast(I32)
         dy_sc_hbm = dy_scales.bitcast(I32)
-        for q in range(4):
-            nc.sync.dma_start(w2_sc_raw[32 * q : 32 * q + 8, :].bitcast(I32), w2_sc_hbm[:, 4 * q : 4 * q + 4, :])
         w2_raw = tile([P, 2, H], U32, "w2_raw")
         nc.sync.dma_start(w2_raw[:].bitcast(I32), w2t_words.rearrange("s p i d -> p s (i d)").bitcast(I32))
+        for q in range(4):
+            nc.sync.dma_start(w2_sc_raw[32 * q : 32 * q + 8, :].bitcast(I32), w2_sc_hbm[:, 4 * q : 4 * q + 4, :])
         dy = tile([P, 2, T], U32, "dy")
         nc.sync.dma_start(dy[:].bitcast(I32), dy_words.rearrange("s p t d -> p s (t d)").bitcast(I32))
         for q in range(4):
             nc.sync.dma_start(dy_sc[32 * q : 32 * q + 8, :].bitcast(I32), dy_sc_hbm[:, 4 * q : 4 * q + 4, :])
 
-        a_all = tile([P, 6, 2, TC], F32, "a_all")
+        ac = tile([P, 12, 2, TC], F32, "ac")
+        a_all = ac[:, 0:6]
+        c_sb = [ac[:, 6 + 3 * h : 9 + 3 * h].rearrange("p g e t -> p (g e t)").rearrange("p (e t) -> p e t", e=2) for h in range(2)]
         a_v = a.rearrange("(p j) t -> p j t", j=4)
         c_v = c.rearrange("(p j) t -> p j t", j=4)
         for h in range(2):
             for g in range(3):
                 nc.sync.dma_start(a_all[:, 3 * h + g], a_v[:, 2 * h : 2 * h + 2, g * TC : (g + 1) * TC])
-        idx2 = tile([P, T // 16], U16, "idx2")
-        idx1 = tile([P, T // 16], U16, "idx1")
-        nc.sync.dma_start(idx2[:], offs2)
         wb_sc_hbm = wbt_scales.bitcast(I32).rearrange("f s (q r) k -> r q (f s) k", r=4)
         wa_sc_hbm = wat_scales.bitcast(I32).rearrange("f s (q r) k -> r q (f s) k", r=4)
         for r in range(4):
             nc.sync.dma_start(wb_sc[r:P:32, :, :].bitcast(I32), wb_sc_hbm[r])
-        wb = tile([P, E2, 2 * K], U8, "wb")
-        nc.sync.dma_start(wb[:].bitcast(I32), wbt_words.bitcast(I32).rearrange("f s p k -> p (f s) k"))
-        c_sb = [tile([P, 2, T], F32, f"c{h}") for h in range(2)]
-        for h in range(2):
-            nc.sync.dma_start(c_sb[h][:], c_v[:, 2 * h : 2 * h + 2, :])
-        nc.sync.dma_start(idx1[:], offs)
-        for r in range(4):
-            nc.sync.dma_start(wa_sc[r:P:32, :, :].bitcast(I32), wa_sc_hbm[r])
-        wa = tile([P, E1, K], U32, "wa")
-        nc.sync.dma_start(wa[:].bitcast(I32), wat_words.rearrange("e s p k d -> p (e s) (k d)").bitcast(I32))
 
         w2 = tile([P, 2, H], U32, "w2")
         w2_sc = tile([P, H], U8, "w2_sc")
@@ -92,19 +89,22 @@ def tile_moe_plb_silu_kernel(
                 in_=w2_raw[:, s, :].bitcast(I32).rearrange("p (b i j) -> p b j i", j=4, i=4),
             )
 
+        wb = tile([P, E2, 2 * K], U8, "wb", tag="w2_raw")
+        nc.sync.dma_start(wb[:].bitcast(I32), wbt_words.bitcast(I32).rearrange("f s p k -> p (f s) k"))
+        for h in (1, 0):
+            nc.sync.dma_start(c_sb[h], c_v[:, 2 * h : 2 * h + 2, :])
+        for r in range(4):
+            nc.sync.dma_start(wa_sc[r:P:32, :, :].bitcast(I32), wa_sc_hbm[r])
+        wa = tile([P, E1, K], U32, "wa", tag="w2_sc_raw")
+        nc.sync.dma_start(wa[:].bitcast(I32), wat_words.rearrange("e s p k d -> p (e s) (k d)").bitcast(I32))
+
         dc = [tile([P, T, 2], BF16, f"dc{h}") for h in range(2)]
-        pn = [tile([P, T, 2], F32, f"pn{h}") for h in range(2)]
-
-        def make_dc(h):
-            for g in range(3):
-                cols = slice(g * TC, (g + 1) * TC)
-                nc.vector.scalar_tensor_tensor(
-                    dc[h][:, cols, :], pn[h][:, cols, :], -1.0, a_all[:, 3 * h + g].rearrange("p e t -> p t e"), ALU.mult, ALU.mult
-                )
-
+        dh = {}
+        t_sb = {}
         for h in range(2):
             for g in range(3):
                 bank = bank_tile([P, 2, TC], f"dh{h}{g}", 3 * h + g)
+                dh[h, g] = bank
                 cols = slice(g * TC, (g + 1) * TC)
                 for e in range(2):
                     j = 2 * h + e
@@ -118,12 +118,14 @@ def tile_moe_plb_silu_kernel(
                             start=(s == 0),
                             stop=(s == 1),
                         )
-                sg = tile([P, TC, 2], F32, f"sg{h}{g}")
-                nc.scalar.activation(sg[:], a_all[:, 3 * h + g].rearrange("p e t -> p t e"), ACT.Sigmoid)
-                nc.vector.scalar_tensor_tensor(pn[h][:, cols, :], bank[:].rearrange("p e t -> p t e"), -1.0, sg[:], ALU.mult, ALU.mult)
-            make_dc(h)
-        z = tile([P, 6, TC, 2], F32, "z")
-        nc.scalar.activation(z[:], a_all[:].rearrange("p k e t -> p k t e"), ACT.Silu, scale=-1.0)
+                y = tile([P, 2, TC], F32, f"y{h}{g}")
+                nc.scalar.activation(y[:], a_all[:, 3 * h + g], ACT.Silu)
+                nc.vector.tensor_tensor(dc[h][:, cols, :], bank[:].rearrange("p e t -> p t e"), y[:].rearrange("p e t -> p t e"), ALU.mult)
+                t_sb[h, g] = tile([P, 2, TC], F32, f"t{h}{g}")
+                nc.gpsimd.tensor_tensor(t_sb[h, g][:], a_all[:, 3 * h + g], y[:], ALU.subtract)
+        sg = {1: tile([P, 2, T], F32, "sg1"), 0: tile([P, 2, T], F32, "sg0", tag="y11")}
+        for h in (1, 0):
+            nc.scalar.activation(sg[h][:].rearrange("p e (g t) -> p g e t", g=3), a_all[:, 3 * h : 3 * h + 3], ACT.Sigmoid)
 
         def offsets(idx, lo, hi):
             return idx[:, lo // 16 : hi // 16]
@@ -133,16 +135,13 @@ def tile_moe_plb_silu_kernel(
 
         def weave_vector(dst, src):
             nc.vector.tensor_copy(
-                dst[:].bitcast(I32).rearrange("p (b i) h -> p b h i", i=4), src[:].bitcast(I32).rearrange("p h (b i) -> p b h i", i=4)
+                dst.bitcast(I32).rearrange("p (b i) h -> p b h i", i=4), src.bitcast(I32).rearrange("p h (b i) -> p b h i", i=4)
             )
-
-        def weave_scalar(dst, src):
-            nc.scalar.copy(dst[:], src[:].rearrange("p h n -> p n h"))
 
         def quantise(src, n, name):
             codes = tile([P, n], U32, name + "_codes")
             scales = tile([P, n], U8, name + "_scales")
-            nc.vector.quantize_mx(out=codes[:].bitcast(FP8X4), scales=scales[:], in_=src[:].rearrange("p n h -> p (n h)").bitcast(BF16))
+            nc.vector.quantize_mx(out=codes[:].bitcast(FP8X4), scales=scales[:], in_=src.rearrange("p n h -> p (n h)").bitcast(BF16))
             return codes, scales
 
         def q_matmul(dst, f, kb, codes, scales, lo):
@@ -176,109 +175,111 @@ def tile_moe_plb_silu_kernel(
         def scatter_scalar(win, idx, lo, hi, src):
             nc.scalar.activation(win[:].indirect(offsets(idx, lo, hi)), src, ACT.Copy)
 
-        qgA = tile([P, 2, HEAD], U32, "qgA")
-        qgB = tile([P, 2, REST], U32, "qgB")
-        qwA = tile([P, HEAD, 2], U32, "qwA", tag="w0")
-        qwB = tile([P, REST, 2], U32, "qwB", tag="da0")
-        gather(qgA[:, 0, :], dc[0], idx2, 0, HEAD)
-        gather(qgA[:, 1, :], dc[1], idx2, 0, HEAD)
-        weave_scalar(qwA, qgA)
-        gather(qgB[:, 0, :], dc[0], idx2, HEAD, T)
-        qcA, qsA = quantise(qwA, HEAD, "qA")
-        gather(qgB[:, 1, :], dc[1], idx2, HEAD, T)
-        w = [tile([P, T, 2], F32, "w0", tag="w0"), tile([P, T, 2], F32, "w1", tag="qgB")]
+        qwA = tile([P, HEAD, 2], U32, "qwA")
+        qwB = tile([P, REST, 2], U32, "qwB")
+        u = [tile([P, T, 2], F32, f"u{h}") for h in range(2)]
 
-        def make_w(h):
+        def make_u(h, g):
             nc.vector.scalar_tensor_tensor(
-                w[h][:], z[:, 3 * h : 3 * h + 3].rearrange("p g t e -> p (g t) e"), 1.0, c_sb[h][:].rearrange("p e t -> p t e"), ALU.subtract, ALU.mult
+                u[h][:, g * TC : (g + 1) * TC, :],
+                t_sb[h, g][:].rearrange("p e t -> p t e"),
+                1.0,
+                dh[h, g][:].rearrange("p e t -> p t e"),
+                ALU.add,
+                ALU.mult,
             )
 
-        make_w(0)
-        weave_vector(qwB, qgB)
-        make_w(1)
-        qcB, qsB = quantise(qwB, REST, "qB")
+        gather(qwA[:, :, 0], dc[0], idx2, 0, HEAD)
+        gather(qwA[:, :, 1], dc[1], idx2, 0, HEAD)
+        make_u(0, 0)
+        make_u(0, 1)
+        qcA, qsA = quantise(qwA[:], HEAD, "qA")
+        gather(qwB[:, :, 0], dc[0], idx2, HEAD, T)
+        gather(qwB[:, :, 1], dc[1], idx2, HEAD, T)
+        qcB, qsB = quantise(qwB[:], REST, "qB")
+        for g in range(3):
+            make_u(1, g)
+        make_u(0, 2)
         da = [tile([P, T, 2], BF16, f"da{h}") for h in range(2)]
-        for h in range(2):
-            nc.gpsimd.tensor_tensor(da[h][:], pn[h][:], w[h][:], ALU.mult)
+        m = {1: tile([P, 2, T], F32, "m1", tag="qwA"), 0: tile([P, 2, T], F32, "m0", tag="qwB")}
+        for h in (1, 0):
+            for e in range(2):
+                nc.gpsimd.tensor_tensor(m[h][:, e, :], sg[h][:, e, :], c_sb[h][:, e, :], ALU.mult)
+        for h in (1, 0):
+            nc.gpsimd.tensor_tensor(da[h][:], u[h][:], m[h][:].rearrange("p e t -> p t e"), ALU.mult)
 
-        def head_products(matmuls, name, number, blocks):
-            bank = bank_tile([P, 2, HEAD], name, number)
-            for u, kb in enumerate(blocks):
-                matmuls(bank[:, u, :], kb)
-            stage = tile([P, 2, HEAD], F32, name + "_stage")
-            nc.scalar.copy(stage[:], bank[:])
-            return stage
+        def q_products(dst, kb, lo, hi):
+            for f in range(lo // C2, hi // C2):
+                codes, scales, first = (qcA, qsA, 0) if f * C2 < HEAD else (qcB, qsB, HEAD)
+                q_matmul(dst[:, f * C2 - lo : (f + 1) * C2 - lo], f, kb, codes, scales, f * C2 - first)
 
-        def q_head(dst, kb):
-            for f in range(2):
-                q_matmul(dst[:, f * C2 : (f + 1) * C2], f, kb, qcA, qsA, f * C2)
+        def r_products(dst, kb, lo, hi):
+            for e in range(lo // C1, hi // C1):
+                codes, scales, first = (rcA, rsA, 0) if e * C1 < HEAD else (rcB, rsB, HEAD)
+                r_matmul(dst[:, e * C1 - lo : (e + 1) * C1 - lo], e, kb, codes, scales, e * C1 - first)
 
-        for number, blocks in ((6, (2, 3)), (7, (0, 1))):
-            stage = head_products(q_head, f"qA{number}", number, blocks)
-            for u, kb in enumerate(blocks):
-                scatter_scalar(q_win[kb], idx2, 0, HEAD, stage[:, u, :])
-        q_banks = {}
-        for kb in (2, 0, 3, 1):
-            q_banks[kb] = bank_tile([P, REST], f"qB{kb}", kb)
-            for f in range(2, E2):
-                q_matmul(q_banks[kb][:, (f - 2) * C2 : (f - 1) * C2], f, kb, qcB, qsB, (f - 2) * C2)
-        stq = {kb: tile([P, REST], F32, f"stq{kb}") for kb in range(3)}
-        stq3 = tile([P, 256], F32, "stq3")
-        nc.vector.tensor_copy(stq[2][:], q_banks[2][:])
-        nc.vector.tensor_copy(stq3[:], q_banks[3][:, 0:256])
-        scatter_vector(q_win[2], idx2, HEAD, T, stq[2][:])
-        scatter_vector(q_win[3], idx2, HEAD, HEAD + 256, stq3[:])
-        for kb in range(2):
-            nc.scalar.copy(stq[kb][:], q_banks[kb][:])
-            for lo in (0, 256):
-                scatter_scalar(q_win[kb], idx2, HEAD + lo, HEAD + lo + 256, stq[kb][:, lo : lo + 256])
+        staged = []
 
-        rgA = tile([P, 2, HEAD], U32, "rgA")
-        rgB = tile([P, 2, REST], U32, "rgB")
-        rwA = tile([P, HEAD, 2], U32, "rwA")
+        def fill(products, name, number, runs):
+            bank = bank_tile([P, sum(hi - lo for kb, lo, hi in runs)], name, number)
+            at = 0
+            parts = []
+            for kb, lo, hi in runs:
+                parts.append(bank[:, at : at + hi - lo])
+                products(parts[-1], kb, lo, hi)
+                at += hi - lo
+            return parts
+
+        def scalar_unit(products, wins, idx, name, number, runs):
+            for part, (kb, lo, hi) in zip(fill(products, name, number, runs), runs):
+                for x in range(0, hi - lo, 256):
+                    stage = tile([P, 256], F32, f"{name}_{kb}_{x}", tag=f"stage{len(staged) % 3}")
+                    staged.append(stage)
+                    nc.scalar.copy(stage[:], part[:, x : x + 256])
+                    scatter_scalar(wins[kb], idx, lo + x, lo + x + 256, stage[:])
+
+        def vector_unit(products, wins, idx, name, number, runs, tag=None):
+            for part, (kb, lo, hi) in zip(fill(products, name, number, runs), runs):
+                stage = tile([P, hi - lo], F32, f"{name}_{kb}", tag=tag)
+                nc.vector.tensor_copy(stage[:], part)
+                scatter_vector(wins[kb], idx, lo, hi, stage[:])
+
+        scalar_unit(q_products, q_win, idx2, "qa", 6, [(3, 0, 256), (2, 0, 256)])
+        scalar_unit(q_products, q_win, idx2, "qb", 7, [(0, 0, 256), (1, 0, 256)])
+        scalar_unit(q_products, q_win, idx2, "qc", 0, [(0, 256, 768)])
+        vector_unit(q_products, q_win, idx2, "qe", 1, [(3, 256, 768)])
+        scalar_unit(q_products, q_win, idx2, "qf", 2, [(2, 256, 768)])
+        vector_unit(q_products, q_win, idx2, "qh", 3, [(1, 256, 512)])
+
+        rg = tile([P, 2 * REST], U32, "rg")
+        rgB = rg[:].rearrange("p (h n) -> p h n", h=2)
+        rwA = rg[:, 0 : 2 * HEAD].rearrange("p (n h) -> p n h", h=2)
         rwB = tile([P, REST, 2], U32, "rwB")
-        gather(rgA[:, 0, :], da[0], idx1, 0, HEAD)
-        gather(rgB[:, 0, :], da[0], idx1, HEAD, T)
-        gather(rgA[:, 1, :], da[1], idx1, 0, HEAD)
-        weave_vector(rwA, rgA)
-        rcA, rsA = quantise(rwA, HEAD, "rA")
+        gather(rwA[:, :, 1], da[1], idx1, 0, HEAD)
         gather(rgB[:, 1, :], da[1], idx1, HEAD, T)
-        weave_vector(rwB, rgB)
-        rcB, rsB = quantise(rwB, REST, "rB")
-
-        def r_head(dst, kb):
-            r_matmul(dst, 0, kb, rcA, rsA, 0)
-
-        for number, blocks in ((4, (0, 1)), (5, (3, 2))):
-            stage = head_products(r_head, f"rA{number}", number, blocks)
-            for u, kb in enumerate(blocks):
-                scatter_scalar(r_win[kb], idx1, 0, HEAD, stage[:, u, :])
+        gather(rwA[:, :, 0], da[0], idx1, 0, HEAD)
+        rcA, rsA = quantise(rwA, HEAD, "rA")
+        gather(rgB[:, 0, :], da[0], idx1, HEAD, T)
+        weave_vector(rwB[:], rgB)
+        rcB, rsB = quantise(rwB[:], REST, "rB")
 
         def finish(kb):
             rows = slice(kb * P, (kb + 1) * P)
             nc.gpsimd.tensor_tensor(q_win[kb][:], q_win[kb][:], r_win[kb][:], ALU.add)
             nc.sync.dma_start(out[rows, :], q_win[kb][:])
 
-        for kb, number in ((0, 6), (1, 7), (2, 0), (3, 1)):
-            bank = bank_tile([P, 2, C1], f"rB{kb}", number)
-            for u in range(2):
-                r_matmul(bank[:, u, :], 1 + u, kb, rcB, rsB, u * C1)
-            stage = tile([P, REST], F32, f"str{kb}")
-            if kb == 0:
-                nc.vector.tensor_copy(stage[:], bank[:].rearrange("p u n -> p (u n)"))
-            else:
-                nc.scalar.copy(stage[:], bank[:].rearrange("p u n -> p (u n)"))
-            if kb == 2:
-                for lo in (0, 256):
-                    scatter_scalar(r_win[kb], idx1, HEAD + lo, HEAD + lo + 256, stage[:, lo : lo + 256])
-            else:
-                scatter_vector(r_win[kb], idx1, HEAD, T, stage[:])
-            if kb < 3:
-                finish(kb)
-        last = tile([P, 256], F32, "last", tag="str2")
-        nc.scalar.copy(last[:], q_banks[3][:, 256:512])
-        scatter_scalar(q_win[3], idx2, HEAD + 256, T, last[:])
+        scalar_unit(r_products, r_win, idx1, "ra", 4, [(2, 0, 256), (3, 0, 256)])
+        vector_unit(r_products, r_win, idx1, "rb", 5, [(0, 0, 256)])
+        scalar_unit(r_products, r_win, idx1, "rc", 6, [(2, 256, 768)])
+        finish(2)
+        vector_unit(r_products, r_win, idx1, "rd", 7, [(0, 256, 768)])
+        finish(0)
+        scalar_unit(r_products, r_win, idx1, "re", 0, [(3, 256, 768)])
+        finish(3)
+        vector_unit(r_products, r_win, idx1, "rf", 1, [(1, 0, 512)])
+        vector_unit(r_products, r_win, idx1, "rg", 3, [(1, 512, 768)])
+        scalar_unit(q_products, q_win, idx2, "qg", 2, [(1, 512, 768)])
         for half in range(2):
             cols = slice(half * T // 2, (half + 1) * T // 2)
-            nc.vector.tensor_tensor(q_win[3][:, cols], q_win[3][:, cols], r_win[3][:, cols], ALU.add)
-            nc.sync.dma_start(out[3 * P : 4 * P, cols], q_win[3][:, cols])
+            nc.vector.tensor_tensor(q_win[1][:, cols], q_win[1][:, cols], r_win[1][:, cols], ALU.add)
+            nc.scalar.dma_start(out[P : 2 * P, cols], q_win[1][:, cols])

@@ -99,12 +99,10 @@ def tile_moe_plb_silu_kernel(
         nc.sync.dma_start(wa[:].bitcast(I32), wat_words.rearrange("e s p k d -> p (e s) (k d)").bitcast(I32))
 
         dc = [tile([P, T, 2], BF16, f"dc{h}") for h in range(2)]
-        dh = {}
-        t_sb = {}
+        p_sb = tile([P, 6, TC, 2], F32, "p_sb")
         for h in range(2):
             for g in range(3):
                 bank = bank_tile([P, 2, TC], f"dh{h}{g}", 3 * h + g)
-                dh[h, g] = bank
                 cols = slice(g * TC, (g + 1) * TC)
                 for e in range(2):
                     j = 2 * h + e
@@ -118,24 +116,35 @@ def tile_moe_plb_silu_kernel(
                             start=(s == 0),
                             stop=(s == 1),
                         )
-                y = tile([P, 2, TC], F32, f"y{h}{g}")
-                nc.scalar.activation(y[:], a_all[:, 3 * h + g], ACT.Silu)
-                nc.vector.tensor_tensor(dc[h][:, cols, :], bank[:].rearrange("p e t -> p t e"), y[:].rearrange("p e t -> p t e"), ALU.mult)
-                t_sb[h, g] = tile([P, 2, TC], F32, f"t{h}{g}")
-                nc.gpsimd.tensor_tensor(t_sb[h, g][:], a_all[:, 3 * h + g], y[:], ALU.subtract)
-        sg = {1: tile([P, 2, T], F32, "sg1"), 0: tile([P, 2, T], F32, "sg0", tag="y11")}
-        for h in (1, 0):
-            nc.scalar.activation(sg[h][:].rearrange("p e (g t) -> p g e t", g=3), a_all[:, 3 * h : 3 * h + 3], ACT.Sigmoid)
+                sg = tile([P, TC, 2], F32, f"sg{h}{g}")
+                nc.scalar.activation(sg[:], a_all[:, 3 * h + g].rearrange("p e t -> p t e"), ACT.Sigmoid)
+                nc.vector.tensor_tensor(p_sb[:, 3 * h + g], bank[:].rearrange("p e t -> p t e"), sg[:], ALU.mult)
+                if h == 0:
+                    nc.gpsimd.tensor_tensor(dc[0][:, cols, :], p_sb[:, g], a_all[:, g].rearrange("p e t -> p t e"), ALU.mult)
+        nc.vector.tensor_tensor(
+            dc[1][:].rearrange("p (g t) e -> p g t e", g=3), p_sb[:, 3:6], a_all[:, 3:6].rearrange("p g e t -> p g t e"), ALU.mult
+        )
+        z = tile([P, 6, TC, 2], F32, "z")
+        nc.scalar.activation(z[:], a_all.rearrange("p k e t -> p k t e"), ACT.Silu, scale=-1.0)
 
         def offsets(idx, lo, hi):
             return idx[:, lo // 16 : hi // 16]
 
         def gather(dst, src, idx, lo, hi):
-            nc.vector.tensor_copy(dst, src[:].rearrange("p t e -> p (t e)").bitcast(U32).indirect(offsets(idx, lo, hi)))
+            nc.vector.tensor_copy(dst, src.rearrange("p t e -> p (t e)").bitcast(U32).indirect(offsets(idx, lo, hi)))
 
         def weave_vector(dst, src):
             nc.vector.tensor_copy(
                 dst.bitcast(I32).rearrange("p (b i) h -> p b h i", i=4), src.bitcast(I32).rearrange("p h (b i) -> p b h i", i=4)
+            )
+
+        def weave_negated(dst, src):
+            nc.vector.tensor_scalar(
+                dst.bitcast(BF16).rearrange("p n (h e) -> p n h e", e=2),
+                src.bitcast(BF16).rearrange("p h (n e) -> p n h e", e=2),
+                -1.0,
+                None,
+                ALU.mult,
             )
 
         def quantise(src, n, name):
@@ -155,13 +164,13 @@ def tile_moe_plb_silu_kernel(
                 stop=True,
             )
 
-        def r_matmul(dst, e, kb, codes, scales, lo):
+        def r_matmul(dst, e, kb, codes, scales, lo, hi):
             nc.tensor.matmul_mx(
                 out=dst,
                 lhsT=wa[:, e, P * kb : P * (kb + 1)].bitcast(FP8X4),
                 lhsT_scale=wa_sc[:, e, P * kb : P * (kb + 1)],
-                rhs=codes[:, lo : lo + C1].bitcast(FP8X4),
-                rhs_scale=scales[:, lo : lo + C1],
+                rhs=codes[:, lo:hi].bitcast(FP8X4),
+                rhs_scale=scales[:, lo:hi],
                 start=True,
                 stop=True,
             )
@@ -175,38 +184,31 @@ def tile_moe_plb_silu_kernel(
         def scatter_scalar(win, idx, lo, hi, src):
             nc.scalar.activation(win[:].indirect(offsets(idx, lo, hi)), src, ACT.Copy)
 
+        qgA = tile([P, 2, HEAD], U32, "qgA")
         qwA = tile([P, HEAD, 2], U32, "qwA")
-        qwB = tile([P, REST, 2], U32, "qwB")
-        u = [tile([P, T, 2], F32, f"u{h}") for h in range(2)]
+        qgB = tile([P, 2, REST], U32, "qgB", tag="qwA")
+        gather(qgA[:, 0, :], dc[0][:], idx2, 0, HEAD)
+        gather(qgA[:, 1, :], dc[1][:], idx2, 0, HEAD)
+        weave_vector(qwA[:], qgA[:])
+        qcA, qsA = quantise(qwA[:], HEAD, "qA")
+        gather(qgB[:, 0, :], dc[0][:], idx2, HEAD, T)
+        gather(qgB[:, 1, :], dc[1][:], idx2, HEAD, T)
+        w = tile([P, 2, T, 2], F32, "w", tag="dc0")
+        qwB = w[:, 0, 0:REST, :].bitcast(U32)
 
-        def make_u(h, g):
+        def make_w(h):
             nc.vector.scalar_tensor_tensor(
-                u[h][:, g * TC : (g + 1) * TC, :],
-                t_sb[h, g][:].rearrange("p e t -> p t e"),
-                1.0,
-                dh[h, g][:].rearrange("p e t -> p t e"),
-                ALU.add,
-                ALU.mult,
+                w[:, h], z[:, 3 * h : 3 * h + 3].rearrange("p g t e -> p (g t) e"), 1.0, c_sb[h].rearrange("p e t -> p t e"), ALU.subtract, ALU.mult
             )
 
-        gather(qwA[:, :, 0], dc[0], idx2, 0, HEAD)
-        gather(qwA[:, :, 1], dc[1], idx2, 0, HEAD)
-        make_u(0, 0)
-        make_u(0, 1)
-        qcA, qsA = quantise(qwA[:], HEAD, "qA")
-        gather(qwB[:, :, 0], dc[0], idx2, HEAD, T)
-        gather(qwB[:, :, 1], dc[1], idx2, HEAD, T)
-        qcB, qsB = quantise(qwB[:], REST, "qB")
-        for g in range(3):
-            make_u(1, g)
-        make_u(0, 2)
-        da = [tile([P, T, 2], BF16, f"da{h}") for h in range(2)]
-        m = {1: tile([P, 2, T], F32, "m1", tag="qwA"), 0: tile([P, 2, T], F32, "m0", tag="qwB")}
-        for h in (1, 0):
-            for e in range(2):
-                nc.gpsimd.tensor_tensor(m[h][:, e, :], sg[h][:, e, :], c_sb[h][:, e, :], ALU.mult)
-        for h in (1, 0):
-            nc.gpsimd.tensor_tensor(da[h][:], u[h][:], m[h][:].rearrange("p e t -> p t e"), ALU.mult)
+        make_w(1)
+        weave_vector(qwB, qgB[:])
+        qcB, qsB = quantise(qwB, REST, "qB")
+        make_w(0)
+        da = tile([P, 2, T, 2], BF16, "da")
+        nc.gpsimd.tensor_tensor(
+            da[:].rearrange("p h t e -> p (h t e)"), p_sb[:].rearrange("p k t e -> p (k t e)"), w[:].rearrange("p h t e -> p (h t e)"), ALU.mult
+        )
 
         def q_products(dst, kb, lo, hi):
             for f in range(lo // C2, hi // C2):
@@ -214,9 +216,11 @@ def tile_moe_plb_silu_kernel(
                 q_matmul(dst[:, f * C2 - lo : (f + 1) * C2 - lo], f, kb, codes, scales, f * C2 - first)
 
         def r_products(dst, kb, lo, hi):
-            for e in range(lo // C1, hi // C1):
-                codes, scales, first = (rcA, rsA, 0) if e * C1 < HEAD else (rcB, rsB, HEAD)
-                r_matmul(dst[:, e * C1 - lo : (e + 1) * C1 - lo], e, kb, codes, scales, e * C1 - first)
+            for e in range(E1):
+                x, y = max(lo, e * C1), min(hi, (e + 1) * C1)
+                if x < y:
+                    codes, scales, first = (rcA, rsA, 0) if x < HEAD else (rcB, rsB, HEAD)
+                    r_matmul(dst[:, x - lo : y - lo], e, kb, codes, scales, x - first, y - first)
 
         staged = []
 
@@ -232,11 +236,12 @@ def tile_moe_plb_silu_kernel(
 
         def scalar_unit(products, wins, idx, name, number, runs):
             for part, (kb, lo, hi) in zip(fill(products, name, number, runs), runs):
-                for x in range(0, hi - lo, 256):
-                    stage = tile([P, 256], F32, f"{name}_{kb}_{x}", tag=f"stage{len(staged) % 3}")
+                step = 256 if hi - lo > 384 else hi - lo
+                for x in range(0, hi - lo, step):
+                    stage = tile([P, step], F32, f"{name}_{kb}_{x}", tag=f"stage{len(staged) % 3}")
                     staged.append(stage)
-                    nc.scalar.copy(stage[:], part[:, x : x + 256])
-                    scatter_scalar(wins[kb], idx, lo + x, lo + x + 256, stage[:])
+                    nc.scalar.copy(stage[:], part[:, x : x + step])
+                    scatter_scalar(wins[kb], idx, lo + x, lo + x + step, stage[:])
 
         def vector_unit(products, wins, idx, name, number, runs, tag=None):
             for part, (kb, lo, hi) in zip(fill(products, name, number, runs), runs):
@@ -246,21 +251,22 @@ def tile_moe_plb_silu_kernel(
 
         scalar_unit(q_products, q_win, idx2, "qa", 6, [(3, 0, 256), (2, 0, 256)])
         scalar_unit(q_products, q_win, idx2, "qb", 7, [(0, 0, 256), (1, 0, 256)])
-        scalar_unit(q_products, q_win, idx2, "qc", 0, [(0, 256, 768)])
         vector_unit(q_products, q_win, idx2, "qe", 1, [(3, 256, 768)])
+        scalar_unit(q_products, q_win, idx2, "qc", 0, [(0, 256, 768)])
         scalar_unit(q_products, q_win, idx2, "qf", 2, [(2, 256, 768)])
-        vector_unit(q_products, q_win, idx2, "qh", 3, [(1, 256, 512)])
+        vector_unit(q_products, q_win, idx2, "qh", 3, [(1, 256, 640)])
 
-        rg = tile([P, 2 * REST], U32, "rg")
-        rgB = rg[:].rearrange("p (h n) -> p h n", h=2)
-        rwA = rg[:, 0 : 2 * HEAD].rearrange("p (n h) -> p n h", h=2)
+        rgA = tile([P, 2, HEAD], U32, "rgA")
+        rwA = tile([P, HEAD, 2], U32, "rwA")
+        rgB = tile([P, 2, REST], U32, "rgB", tag="rwA")
         rwB = tile([P, REST, 2], U32, "rwB")
-        gather(rwA[:, :, 1], da[1], idx1, 0, HEAD)
-        gather(rgB[:, 1, :], da[1], idx1, HEAD, T)
-        gather(rwA[:, :, 0], da[0], idx1, 0, HEAD)
-        rcA, rsA = quantise(rwA, HEAD, "rA")
-        gather(rgB[:, 0, :], da[0], idx1, HEAD, T)
-        weave_vector(rwB[:], rgB)
+        gather(rgA[:, 0, :], da[:, 0], idx1, 0, HEAD)
+        gather(rgA[:, 1, :], da[:, 1], idx1, 0, HEAD)
+        weave_negated(rwA[:], rgA[:])
+        rcA, rsA = quantise(rwA[:], HEAD, "rA")
+        gather(rgB[:, 0, :], da[:, 0], idx1, HEAD, T)
+        gather(rgB[:, 1, :], da[:, 1], idx1, HEAD, T)
+        weave_negated(rwB[:], rgB[:])
         rcB, rsB = quantise(rwB[:], REST, "rB")
 
         def finish(kb):
@@ -269,16 +275,17 @@ def tile_moe_plb_silu_kernel(
             nc.sync.dma_start(out[rows, :], q_win[kb][:])
 
         scalar_unit(r_products, r_win, idx1, "ra", 4, [(2, 0, 256), (3, 0, 256)])
-        vector_unit(r_products, r_win, idx1, "rb", 5, [(0, 0, 256)])
+        scalar_unit(r_products, r_win, idx1, "rh", 3, [(1, 0, 128)])
+        vector_unit(r_products, r_win, idx1, "rb", 5, [(0, 0, 256)], tag="rwB")
         scalar_unit(r_products, r_win, idx1, "rc", 6, [(2, 256, 768)])
         finish(2)
         vector_unit(r_products, r_win, idx1, "rd", 7, [(0, 256, 768)])
         finish(0)
         scalar_unit(r_products, r_win, idx1, "re", 0, [(3, 256, 768)])
         finish(3)
-        vector_unit(r_products, r_win, idx1, "rf", 1, [(1, 0, 512)])
-        vector_unit(r_products, r_win, idx1, "rg", 3, [(1, 512, 768)])
-        scalar_unit(q_products, q_win, idx2, "qg", 2, [(1, 512, 768)])
+        vector_unit(r_products, r_win, idx1, "rf", 1, [(1, 128, 512)])
+        vector_unit(r_products, r_win, idx1, "rg", 4, [(1, 512, 768)])
+        scalar_unit(q_products, q_win, idx2, "qg", 2, [(1, 640, 768)])
         for half in range(2):
             cols = slice(half * T // 2, (half + 1) * T // 2)
             nc.vector.tensor_tensor(q_win[1][:, cols], q_win[1][:, cols], r_win[1][:, cols], ALU.add)

@@ -19,6 +19,8 @@ P = 128
 TC = 256
 HEAD = 256
 REST = T - HEAD
+DA_SPLIT = 2048
+DC_GPSIMD = 2
 FLOPS = 2 * N * H * T + 2 * 2 * H * K * T
 
 
@@ -40,29 +42,27 @@ def tile_moe_plb_silu_kernel(
         dy_sc = tile([P, T], U8, "dy_sc")
         wb_sc = tile([P, E2, K], U8, "wb_sc")
         wa_sc = tile([P, E1, K], U8, "wa_sc")
-        blank_w2 = tile([P, H // 4], I32, "blank_w2", tag="dy")
-        blank_dy = tile([P, T // 4], I32, "blank_dy", tag="ac")
-        nc.gpsimd.memset(blank_w2[:], 0)
-        nc.gpsimd.tensor_copy(w2_sc_raw[:].bitcast(I32), blank_w2[:])
-        nc.gpsimd.memset(blank_dy[:], 0)
-        nc.gpsimd.tensor_copy(dy_sc[:].bitcast(I32), blank_dy[:])
+        nc.gpsimd.memset(w2_sc_raw[:].bitcast(I32), 0)
+        nc.gpsimd.memset(dy_sc[:].bitcast(I32), 0)
         nc.gpsimd.memset(wb_sc[:].rearrange("p f k -> p (f k)").bitcast(I32), 0)
         nc.gpsimd.memset(wa_sc[:].rearrange("p f k -> p (f k)").bitcast(I32), 0)
 
-        idx2 = tile([P, T // 16], U16, "idx2")
-        idx1 = tile([P, T // 16], U16, "idx1")
-        nc.sync.dma_start(idx2[:], offs2)
-        nc.sync.dma_start(idx1[:], offs)
         w2_sc_hbm = w2t_scales.bitcast(I32)
         dy_sc_hbm = dy_scales.bitcast(I32)
-        w2_raw = tile([P, 2, H], U32, "w2_raw")
-        nc.sync.dma_start(w2_raw[:].bitcast(I32), w2t_words.rearrange("s p i d -> p s (i d)").bitcast(I32))
+
+        def load_dy_scales(q):
+            nc.sync.dma_start(dy_sc[32 * q : 32 * q + 8, :].bitcast(I32), dy_sc_hbm[:, 4 * q : 4 * q + 4, :])
+
         for q in range(4):
             nc.sync.dma_start(w2_sc_raw[32 * q : 32 * q + 8, :].bitcast(I32), w2_sc_hbm[:, 4 * q : 4 * q + 4, :])
+        load_dy_scales(0)
+        load_dy_scales(1)
+        w2_raw = tile([P, 2, H], U32, "w2_raw")
+        nc.sync.dma_start(w2_raw[:].bitcast(I32), w2t_words.rearrange("s p i d -> p s (i d)").bitcast(I32))
         dy = tile([P, 2, T], U32, "dy")
         nc.sync.dma_start(dy[:].bitcast(I32), dy_words.rearrange("s p t d -> p s (t d)").bitcast(I32))
-        for q in range(4):
-            nc.sync.dma_start(dy_sc[32 * q : 32 * q + 8, :].bitcast(I32), dy_sc_hbm[:, 4 * q : 4 * q + 4, :])
+        load_dy_scales(2)
+        load_dy_scales(3)
 
         ac = tile([P, 12, 2, TC], F32, "ac")
         a_all = ac[:, 0:6]
@@ -72,6 +72,10 @@ def tile_moe_plb_silu_kernel(
         for h in range(2):
             for g in range(3):
                 nc.sync.dma_start(a_all[:, 3 * h + g], a_v[:, 2 * h : 2 * h + 2, g * TC : (g + 1) * TC])
+        idx2 = tile([P, T // 16], U16, "idx2")
+        idx1 = tile([P, T // 16], U16, "idx1")
+        nc.sync.dma_start(idx2[:], offs2)
+        nc.sync.dma_start(idx1[:], offs)
         wb_sc_hbm = wbt_scales.bitcast(I32).rearrange("f s (q r) k -> r q (f s) k", r=4)
         wa_sc_hbm = wat_scales.bitcast(I32).rearrange("f s (q r) k -> r q (f s) k", r=4)
         for r in range(4):
@@ -98,7 +102,8 @@ def tile_moe_plb_silu_kernel(
         wa = tile([P, E1, K], U32, "wa", tag="w2_sc_raw")
         nc.sync.dma_start(wa[:].bitcast(I32), wat_words.rearrange("e s p k d -> p (e s) (k d)").bitcast(I32))
 
-        dc = [tile([P, T, 2], BF16, f"dc{h}") for h in range(2)]
+        dc_all = tile([P, 6, TC, 2], BF16, "dc")
+        dc = [dc_all[:, 3 * h : 3 * h + 3].rearrange("p g t e -> p (g t) e") for h in range(2)]
         p_sb = tile([P, 6, TC, 2], F32, "p_sb")
         for h in range(2):
             for g in range(3):
@@ -119,10 +124,10 @@ def tile_moe_plb_silu_kernel(
                 sg = tile([P, TC, 2], F32, f"sg{h}{g}")
                 nc.scalar.activation(sg[:], a_all[:, 3 * h + g].rearrange("p e t -> p t e"), ACT.Sigmoid)
                 nc.vector.tensor_tensor(p_sb[:, 3 * h + g], bank[:].rearrange("p e t -> p t e"), sg[:], ALU.mult)
-                if h == 0:
-                    nc.gpsimd.tensor_tensor(dc[0][:, cols, :], p_sb[:, g], a_all[:, g].rearrange("p e t -> p t e"), ALU.mult)
+                if 3 * h + g < DC_GPSIMD:
+                    nc.gpsimd.tensor_tensor(dc_all[:, g], p_sb[:, g], a_all[:, g].rearrange("p e t -> p t e"), ALU.mult)
         nc.vector.tensor_tensor(
-            dc[1][:].rearrange("p (g t) e -> p g t e", g=3), p_sb[:, 3:6], a_all[:, 3:6].rearrange("p g e t -> p g t e"), ALU.mult
+            dc_all[:, DC_GPSIMD:6], p_sb[:, DC_GPSIMD:6], a_all[:, DC_GPSIMD:6].rearrange("p g e t -> p g t e"), ALU.mult
         )
         z = tile([P, 6, TC, 2], F32, "z")
         nc.scalar.activation(z[:], a_all.rearrange("p k e t -> p k t e"), ACT.Silu, scale=-1.0)
@@ -185,16 +190,17 @@ def tile_moe_plb_silu_kernel(
             nc.scalar.activation(win[:].indirect(offsets(idx, lo, hi)), src, ACT.Copy)
 
         qgA = tile([P, 2, HEAD], U32, "qgA")
-        qwA = tile([P, HEAD, 2], U32, "qwA")
-        qgB = tile([P, 2, REST], U32, "qgB", tag="qwA")
-        gather(qgA[:, 0, :], dc[0][:], idx2, 0, HEAD)
-        gather(qgA[:, 1, :], dc[1][:], idx2, 0, HEAD)
-        weave_vector(qwA[:], qgA[:])
-        qcA, qsA = quantise(qwA[:], HEAD, "qA")
-        gather(qgB[:, 0, :], dc[0][:], idx2, HEAD, T)
-        gather(qgB[:, 1, :], dc[1][:], idx2, HEAD, T)
-        w = tile([P, 2, T, 2], F32, "w", tag="dc0")
-        qwB = w[:, 0, 0:REST, :].bitcast(U32)
+        w = tile([P, 2, T, 2], F32, "w", tag="sg12")
+        w_words = w[:].rearrange("p h t e -> p (h t e)").bitcast(U32)
+        qwA = w_words[:, 2 * T - HEAD : 2 * T + HEAD].rearrange("p (n h) -> p n h", h=2)
+        qgB = w_words[:, 2 * T - 2 * REST : 2 * T].rearrange("p (h n) -> p h n", h=2)
+        qwB = tile([P, REST, 2], U32, "qwB")[:]
+        gather(qgA[:, 0, :], dc[0], idx2, 0, HEAD)
+        gather(qgA[:, 1, :], dc[1], idx2, 0, HEAD)
+        nc.scalar.copy(qwA, qgA[:].rearrange("p h n -> p n h"))
+        gather(qgB[:, 0, :], dc[0], idx2, HEAD, T)
+        qcA, qsA = quantise(qwA, HEAD, "qA")
+        gather(qgB[:, 1, :], dc[1], idx2, HEAD, T)
 
         def make_w(h):
             nc.vector.scalar_tensor_tensor(
@@ -202,13 +208,21 @@ def tile_moe_plb_silu_kernel(
             )
 
         make_w(1)
-        weave_vector(qwB, qgB[:])
+        weave_vector(qwB, qgB)
+        da = tile([P, 2, T, 2], BF16, "da")
+
+        def make_da(engine, lo, hi):
+            engine.tensor_tensor(
+                da[:].rearrange("p h t e -> p (h t e)")[:, lo:hi],
+                p_sb[:].rearrange("p k t e -> p (k t e)")[:, lo:hi],
+                w[:].rearrange("p h t e -> p (h t e)")[:, lo:hi],
+                ALU.mult,
+            )
+
+        make_da(nc.vector, DA_SPLIT, 4 * T)
         qcB, qsB = quantise(qwB, REST, "qB")
         make_w(0)
-        da = tile([P, 2, T, 2], BF16, "da")
-        nc.gpsimd.tensor_tensor(
-            da[:].rearrange("p h t e -> p (h t e)"), p_sb[:].rearrange("p k t e -> p (k t e)"), w[:].rearrange("p h t e -> p (h t e)"), ALU.mult
-        )
+        make_da(nc.gpsimd, 0, DA_SPLIT)
 
         def q_products(dst, kb, lo, hi):
             for f in range(lo // C2, hi // C2):
@@ -249,43 +263,46 @@ def tile_moe_plb_silu_kernel(
                 nc.vector.tensor_copy(stage[:], part)
                 scatter_vector(wins[kb], idx, lo, hi, stage[:])
 
-        scalar_unit(q_products, q_win, idx2, "qa", 6, [(3, 0, 256), (2, 0, 256)])
-        scalar_unit(q_products, q_win, idx2, "qb", 7, [(0, 0, 256), (1, 0, 256)])
+        for kb, number in ((3, 6), (2, 7), (0, 4), (1, 5)):
+            scalar_unit(q_products, q_win, idx2, f"qa{kb}", number, [(kb, 0, 256)])
         vector_unit(q_products, q_win, idx2, "qe", 1, [(3, 256, 768)])
+        vector_unit(q_products, q_win, idx2, "qh", 3, [(2, 640, 768)])
         scalar_unit(q_products, q_win, idx2, "qc", 0, [(0, 256, 768)])
-        scalar_unit(q_products, q_win, idx2, "qf", 2, [(2, 256, 768)])
-        vector_unit(q_products, q_win, idx2, "qh", 3, [(1, 256, 640)])
+        scalar_unit(q_products, q_win, idx2, "qf", 2, [(2, 256, 640)])
+        scalar_unit(q_products, q_win, idx2, "qi", 6, [(1, 256, 512)])
 
         rgA = tile([P, 2, HEAD], U32, "rgA")
         rwA = tile([P, HEAD, 2], U32, "rwA")
-        rgB = tile([P, 2, REST], U32, "rgB", tag="rwA")
+        rgB = tile([P, 2, REST], U32, "rgB")
         rwB = tile([P, REST, 2], U32, "rwB")
         gather(rgA[:, 0, :], da[:, 0], idx1, 0, HEAD)
         gather(rgA[:, 1, :], da[:, 1], idx1, 0, HEAD)
-        weave_negated(rwA[:], rgA[:])
-        rcA, rsA = quantise(rwA[:], HEAD, "rA")
         gather(rgB[:, 0, :], da[:, 0], idx1, HEAD, T)
+        weave_negated(rwA[:], rgA[:])
         gather(rgB[:, 1, :], da[:, 1], idx1, HEAD, T)
+        rcA, rsA = quantise(rwA[:], HEAD, "rA")
         weave_negated(rwB[:], rgB[:])
         rcB, rsB = quantise(rwB[:], REST, "rB")
 
-        def finish(kb):
+        def finish(kb, pieces):
             rows = slice(kb * P, (kb + 1) * P)
-            nc.gpsimd.tensor_tensor(q_win[kb][:], q_win[kb][:], r_win[kb][:], ALU.add)
-            nc.sync.dma_start(out[rows, :], q_win[kb][:])
+            for x in range(pieces):
+                cols = slice(x * T // pieces, (x + 1) * T // pieces)
+                nc.gpsimd.tensor_tensor(q_win[kb][:, cols], q_win[kb][:, cols], r_win[kb][:, cols], ALU.add)
+                nc.sync.dma_start(out[rows, cols], q_win[kb][:, cols])
 
-        scalar_unit(r_products, r_win, idx1, "ra", 4, [(2, 0, 256), (3, 0, 256)])
-        scalar_unit(r_products, r_win, idx1, "rh", 3, [(1, 0, 128)])
+        scalar_unit(r_products, r_win, idx1, "ra", 3, [(2, 0, 256)])
+        scalar_unit(r_products, r_win, idx1, "rj", 0, [(3, 0, 256)])
         vector_unit(r_products, r_win, idx1, "rb", 5, [(0, 0, 256)], tag="rwB")
-        scalar_unit(r_products, r_win, idx1, "rc", 6, [(2, 256, 768)])
-        finish(2)
         vector_unit(r_products, r_win, idx1, "rd", 7, [(0, 256, 768)])
-        finish(0)
-        scalar_unit(r_products, r_win, idx1, "re", 0, [(3, 256, 768)])
-        finish(3)
-        vector_unit(r_products, r_win, idx1, "rf", 1, [(1, 128, 512)])
+        scalar_unit(r_products, r_win, idx1, "rc", 6, [(2, 256, 768)])
+        finish(0, 1)
+        finish(2, 1)
+        vector_unit(r_products, r_win, idx1, "rf", 1, [(1, 0, 512)])
         vector_unit(r_products, r_win, idx1, "rg", 4, [(1, 512, 768)])
-        scalar_unit(q_products, q_win, idx2, "qg", 2, [(1, 640, 768)])
+        scalar_unit(r_products, r_win, idx1, "re", 3, [(3, 256, 768)])
+        finish(3, 2)
+        scalar_unit(q_products, q_win, idx2, "qg", 2, [(1, 512, 768)])
         for half in range(2):
             cols = slice(half * T // 2, (half + 1) * T // 2)
             nc.vector.tensor_tensor(q_win[1][:, cols], q_win[1][:, cols], r_win[1][:, cols], ALU.add)

@@ -291,15 +291,16 @@ def tile_moe_plb_silu_kernel(
                 nc.gpsimd.tensor_tensor(q_win[kb][:, cols], q_win[kb][:, cols], r_win[kb][:, cols], ALU.add)
                 nc.sync.dma_start(out[rows, cols], q_win[kb][:, cols])
 
+        vector_unit(r_products, r_win, idx1, "rb", 5, [(0, 0, 256)])
         scalar_unit(r_products, r_win, idx1, "ra", 3, [(2, 0, 256)])
         scalar_unit(r_products, r_win, idx1, "rj", 0, [(3, 0, 256)])
-        vector_unit(r_products, r_win, idx1, "rb", 5, [(0, 0, 256)], tag="rwB")
+        vector_unit(r_products, r_win, idx1, "ri", 5, [(2, 640, 768)])
         vector_unit(r_products, r_win, idx1, "rd", 7, [(0, 256, 768)])
-        scalar_unit(r_products, r_win, idx1, "rc", 6, [(2, 256, 768)])
+        vector_unit(r_products, r_win, idx1, "rg", 4, [(1, 512, 768)])
+        vector_unit(r_products, r_win, idx1, "rf", 1, [(1, 0, 512)])
+        scalar_unit(r_products, r_win, idx1, "rc", 6, [(2, 256, 640)])
         finish(0, 1)
         finish(2, 1)
-        vector_unit(r_products, r_win, idx1, "rf", 1, [(1, 0, 512)])
-        vector_unit(r_products, r_win, idx1, "rg", 4, [(1, 512, 768)])
         scalar_unit(r_products, r_win, idx1, "re", 3, [(3, 256, 768)])
         finish(3, 2)
         scalar_unit(q_products, q_win, idx2, "qg", 2, [(1, 512, 768)])

@@ -42,8 +42,12 @@ def tile_moe_plb_silu_kernel(
         dy_sc = tile([P, T], U8, "dy_sc")
         wb_sc = tile([P, E2, K], U8, "wb_sc")
         wa_sc = tile([P, E1, K], U8, "wa_sc")
-        nc.gpsimd.memset(w2_sc_raw[:].bitcast(I32), 0)
-        nc.gpsimd.memset(dy_sc[:].bitcast(I32), 0)
+        blank_w2 = tile([P, H // 4], I32, "blank_w2", tag="dy")
+        blank_dy = tile([P, T // 4], I32, "blank_dy", tag="ac")
+        nc.gpsimd.memset(blank_w2[:], 0)
+        nc.gpsimd.tensor_copy(w2_sc_raw[:].bitcast(I32), blank_w2[:])
+        nc.gpsimd.memset(blank_dy[:], 0)
+        nc.gpsimd.tensor_copy(dy_sc[:].bitcast(I32), blank_dy[:])
         nc.gpsimd.memset(wb_sc[:].rearrange("p f k -> p (f k)").bitcast(I32), 0)
         nc.gpsimd.memset(wa_sc[:].rearrange("p f k -> p (f k)").bitcast(I32), 0)
 
@@ -53,29 +57,29 @@ def tile_moe_plb_silu_kernel(
         def load_dy_scales(q):
             nc.sync.dma_start(dy_sc[32 * q : 32 * q + 8, :].bitcast(I32), dy_sc_hbm[:, 4 * q : 4 * q + 4, :])
 
-        for q in range(4):
-            nc.sync.dma_start(w2_sc_raw[32 * q : 32 * q + 8, :].bitcast(I32), w2_sc_hbm[:, 4 * q : 4 * q + 4, :])
-        load_dy_scales(0)
-        load_dy_scales(1)
-        w2_raw = tile([P, 2, H], U32, "w2_raw")
-        nc.sync.dma_start(w2_raw[:].bitcast(I32), w2t_words.rearrange("s p i d -> p s (i d)").bitcast(I32))
-        dy = tile([P, 2, T], U32, "dy")
-        nc.sync.dma_start(dy[:].bitcast(I32), dy_words.rearrange("s p t d -> p s (t d)").bitcast(I32))
-        load_dy_scales(2)
-        load_dy_scales(3)
-
         ac = tile([P, 12, 2, TC], F32, "ac")
         a_all = ac[:, 0:6]
         c_sb = [ac[:, 6 + 3 * h : 9 + 3 * h].rearrange("p g e t -> p (g e t)").rearrange("p (e t) -> p e t", e=2) for h in range(2)]
         a_v = a.rearrange("(p j) t -> p j t", j=4)
         c_v = c.rearrange("(p j) t -> p j t", j=4)
-        for h in range(2):
-            for g in range(3):
-                nc.sync.dma_start(a_all[:, 3 * h + g], a_v[:, 2 * h : 2 * h + 2, g * TC : (g + 1) * TC])
+
+        def load_a(h, g):
+            nc.sync.dma_start(a_all[:, 3 * h + g], a_v[:, 2 * h : 2 * h + 2, g * TC : (g + 1) * TC])
+
         idx2 = tile([P, T // 16], U16, "idx2")
         idx1 = tile([P, T // 16], U16, "idx1")
         nc.sync.dma_start(idx2[:], offs2)
         nc.sync.dma_start(idx1[:], offs)
+        w2_raw = tile([P, 2, H], U32, "w2_raw")
+        nc.sync.dma_start(w2_raw[:].bitcast(I32), w2t_words.rearrange("s p i d -> p s (i d)").bitcast(I32))
+        for q in range(4):
+            nc.sync.dma_start(w2_sc_raw[32 * q : 32 * q + 8, :].bitcast(I32), w2_sc_hbm[:, 4 * q : 4 * q + 4, :])
+        dy = tile([P, 2, T], U32, "dy")
+        nc.sync.dma_start(dy[:].bitcast(I32), dy_words.rearrange("s p t d -> p s (t d)").bitcast(I32))
+        for q in range(4):
+            load_dy_scales(q)
+        for k in range(6):
+            load_a(k // 3, k % 3)
         wb_sc_hbm = wbt_scales.bitcast(I32).rearrange("f s (q r) k -> r q (f s) k", r=4)
         wa_sc_hbm = wat_scales.bitcast(I32).rearrange("f s (q r) k -> r q (f s) k", r=4)
         for r in range(4):

@@ -85,6 +85,18 @@ def tile_moe_plb_silu_kernel(
         for r in range(4):
             nc.sync.dma_start(wb_sc[r:P:32, :, :].bitcast(I32), wb_sc_hbm[r])
 
+        for number in (6, 7):
+            warm = bank_tile([P, H], f"warm{number}", number)
+            nc.tensor.matmul_mx(
+                out=warm[:],
+                lhsT=w2_raw[:, 0, 0:P].bitcast(FP8X4),
+                lhsT_scale=w2_sc_raw[:, 0:P],
+                rhs=w2_raw[:, 0, :].bitcast(FP8X4),
+                rhs_scale=w2_sc_raw[:],
+                start=True,
+                stop=True,
+            )
+
         w2 = tile([P, 2, H], U32, "w2")
         w2_sc = tile([P, H], U8, "w2_sc")
         nc.vector.tensor_copy(

@@ -19,8 +19,8 @@ P = 128
 TC = 256
 HEAD = 256
 REST = T - HEAD
-DA_SPLIT = 2048
 DC_GPSIMD = 2
+LATE = T - 128
 FLOPS = 2 * N * H * T + 2 * 2 * H * K * T
 
 
@@ -142,9 +142,8 @@ def tile_moe_plb_silu_kernel(
                 nc.vector.tensor_tensor(p_sb[:, 3 * h + g], bank[:].rearrange("p e t -> p t e"), sg[:], ALU.mult)
                 if 3 * h + g < DC_GPSIMD:
                     nc.gpsimd.tensor_tensor(dc_all[:, g], p_sb[:, g], a_all[:, g].rearrange("p e t -> p t e"), ALU.mult)
-        nc.vector.tensor_tensor(
-            dc_all[:, DC_GPSIMD:6], p_sb[:, DC_GPSIMD:6], a_all[:, DC_GPSIMD:6].rearrange("p g e t -> p g t e"), ALU.mult
-        )
+        for part in (slice(DC_GPSIMD, 5), slice(5, 6)):
+            nc.vector.tensor_tensor(dc_all[:, part], p_sb[:, part], a_all[:, part].rearrange("p g e t -> p g t e"), ALU.mult)
         z = tile([P, 6, TC, 2], F32, "z")
         nc.scalar.activation(z[:], a_all.rearrange("p k e t -> p k t e"), ACT.Silu, scale=-1.0)
 
@@ -157,15 +156,6 @@ def tile_moe_plb_silu_kernel(
         def weave_vector(dst, src):
             nc.vector.tensor_copy(
                 dst.bitcast(I32).rearrange("p (b i) h -> p b h i", i=4), src.bitcast(I32).rearrange("p h (b i) -> p b h i", i=4)
-            )
-
-        def weave_negated(dst, src):
-            nc.vector.tensor_scalar(
-                dst.bitcast(BF16).rearrange("p n (h e) -> p n h e", e=2),
-                src.bitcast(BF16).rearrange("p h (n e) -> p n h e", e=2),
-                -1.0,
-                None,
-                ALU.mult,
             )
 
         def quantise(src, n, name):
@@ -205,40 +195,45 @@ def tile_moe_plb_silu_kernel(
         def scatter_scalar(win, idx, lo, hi, src):
             nc.scalar.activation(win[:].indirect(offsets(idx, lo, hi)), src, ACT.Copy)
 
-        qgA = tile([P, 2, HEAD], U32, "qgA")
-        w = tile([P, 2, T, 2], F32, "w", tag="sg12")
-        w_words = w[:].rearrange("p h t e -> p (h t e)").bitcast(U32)
-        qwA = w_words[:, 2 * T - HEAD : 2 * T + HEAD].rearrange("p (n h) -> p n h", h=2)
-        qgB = w_words[:, 2 * T - 2 * REST : 2 * T].rearrange("p (h n) -> p h n", h=2)
-        qwB = tile([P, REST, 2], U32, "qwB")[:]
+        w_both = tile([P, 2, T, 2], F32, "w", tag="sg12")
+        w = [w_both[:, 1], w_both[:, 0]]
+        w_words = w_both[:].rearrange("p h t e -> p (h t e)").bitcast(U32)
+        qgA = w_words[:, 2 * T - HEAD : 2 * T + HEAD].rearrange("p (h n) -> p h n", h=2)
+        qgB = w_words[:, 2 * T : 2 * T + 2 * REST].rearrange("p (h n) -> p h n", h=2)
+        qwA = tile([P, HEAD, 2], U32, "qwA")[:]
+        qwB = tile([P, REST, 2], U32, "qwB")
         gather(qgA[:, 0, :], dc[0], idx2, 0, HEAD)
         gather(qgA[:, 1, :], dc[1], idx2, 0, HEAD)
-        nc.scalar.copy(qwA, qgA[:].rearrange("p h n -> p n h"))
-        gather(qgB[:, 0, :], dc[0], idx2, HEAD, T)
-        qcA, qsA = quantise(qwA, HEAD, "qA")
+        nc.scalar.copy(qwA, qgA.rearrange("p h n -> p n h"))
         gather(qgB[:, 1, :], dc[1], idx2, HEAD, T)
+        qcA, qsA = quantise(qwA, HEAD, "qA")
+        gather(qgB[:, 0, :], dc[0], idx2, HEAD, T)
 
-        def make_w(h):
+        def make_w(h, lo, hi):
             nc.vector.scalar_tensor_tensor(
-                w[:, h], z[:, 3 * h : 3 * h + 3].rearrange("p g t e -> p (g t) e"), 1.0, c_sb[h].rearrange("p e t -> p t e"), ALU.subtract, ALU.mult
-            )
-
-        make_w(1)
-        weave_vector(qwB, qgB)
-        da = tile([P, 2, T, 2], BF16, "da")
-
-        def make_da(engine, lo, hi):
-            engine.tensor_tensor(
-                da[:].rearrange("p h t e -> p (h t e)")[:, lo:hi],
-                p_sb[:].rearrange("p k t e -> p (k t e)")[:, lo:hi],
-                w[:].rearrange("p h t e -> p (h t e)")[:, lo:hi],
+                w[h][:, lo:hi],
+                z[:, 3 * h : 3 * h + 3].rearrange("p g t e -> p (g t) e")[:, lo:hi],
+                1.0,
+                c_sb[h][:, :, lo:hi].rearrange("p e t -> p t e"),
+                ALU.subtract,
                 ALU.mult,
             )
 
-        make_da(nc.vector, DA_SPLIT, 4 * T)
-        qcB, qsB = quantise(qwB, REST, "qB")
-        make_w(0)
-        make_da(nc.gpsimd, 0, DA_SPLIT)
+        da = [tile([P, T, 2], BF16, "da0")]
+
+        def make_da(engine, h, lo, hi):
+            p_pair = p_sb[:, 3 * h : 3 * h + 3].rearrange("p g t e -> p (g t) e")
+            engine.tensor_tensor(da[h][:, lo:hi], p_pair[:, lo:hi], w[h][:, lo:hi], ALU.mult)
+
+        make_w(0, LATE, T)
+        make_w(1, 0, T)
+        weave_vector(qwB[:], qgB)
+        qcB, qsB = quantise(qwB[:], REST, "qB")
+        make_da(nc.vector, 0, LATE, T)
+        make_w(0, 0, LATE)
+        da.append(tile([P, T, 2], BF16, "da1", tag="z"))
+        make_da(nc.gpsimd, 1, 0, T)
+        make_da(nc.gpsimd, 0, 0, LATE)
 
         def q_products(dst, kb, lo, hi):
             for f in range(lo // C2, hi // C2):
@@ -291,20 +286,20 @@ def tile_moe_plb_silu_kernel(
         rwA = tile([P, HEAD, 2], U32, "rwA")
         rgB = tile([P, 2, REST], U32, "rgB")
         rwB = tile([P, REST, 2], U32, "rwB")
-        gather(rgA[:, 0, :], da[:, 0], idx1, 0, HEAD)
-        gather(rgA[:, 1, :], da[:, 1], idx1, 0, HEAD)
-        gather(rgB[:, 0, :], da[:, 0], idx1, HEAD, T)
-        weave_negated(rwA[:], rgA[:])
-        gather(rgB[:, 1, :], da[:, 1], idx1, HEAD, T)
+        for h in (1, 0):
+            gather(rgA[:, h, :], da[h][:], idx1, 0, HEAD)
+        weave_vector(rwA[:], rgA[:])
         rcA, rsA = quantise(rwA[:], HEAD, "rA")
-        weave_negated(rwB[:], rgB[:])
+        for h in (1, 0):
+            gather(rgB[:, h, :], da[h][:], idx1, HEAD, T)
+        weave_vector(rwB[:], rgB[:])
         rcB, rsB = quantise(rwB[:], REST, "rB")
 
         def finish(kb, pieces):
             rows = slice(kb * P, (kb + 1) * P)
             for x in range(pieces):
                 cols = slice(x * T // pieces, (x + 1) * T // pieces)
-                nc.gpsimd.tensor_tensor(q_win[kb][:, cols], q_win[kb][:, cols], r_win[kb][:, cols], ALU.add)
+                nc.gpsimd.tensor_tensor(q_win[kb][:, cols], q_win[kb][:, cols], r_win[kb][:, cols], ALU.subtract)
                 nc.sync.dma_start(out[rows, cols], q_win[kb][:, cols])
 
         vector_unit(r_products, r_win, idx1, "rb", 5, [(0, 0, 256)])
@@ -322,5 +317,5 @@ def tile_moe_plb_silu_kernel(
         scalar_unit(q_products, q_win, idx2, "qg", 2, [(1, 512, 768)])
         for half in range(2):
             cols = slice(half * T // 2, (half + 1) * T // 2)
-            nc.vector.tensor_tensor(q_win[1][:, cols], q_win[1][:, cols], r_win[1][:, cols], ALU.add)
+            nc.vector.tensor_tensor(q_win[1][:, cols], q_win[1][:, cols], r_win[1][:, cols], ALU.subtract)
             nc.scalar.dma_start(out[P : 2 * P, cols], q_win[1][:, cols])

@@ -17,10 +17,10 @@ K, T, H, N = 512, 768, 512, 1024
 E1, C1, E2, C2 = 3, 256, 6, 128
 P = 128
 TC = 256
+G = T // TC
 HEAD = 256
 REST = T - HEAD
-DC_GPSIMD = 2
-LATE = T - 128
+WIDE = 1024
 FLOPS = 2 * N * H * T + 2 * 2 * H * K * T
 
 
@@ -38,12 +38,15 @@ def tile_moe_plb_silu_kernel(
         def bank_tile(shape, name, number):
             return ps.tile(shape, F32, name=name, tag=f"bank{number}")
 
+        def tokens(g):
+            return slice(g * TC, (g + 1) * TC)
+
         w2_sc_raw = tile([P, H], U8, "w2_sc_raw")
         dy_sc = tile([P, T], U8, "dy_sc")
         wb_sc = tile([P, E2, K], U8, "wb_sc")
         wa_sc = tile([P, E1, K], U8, "wa_sc")
-        blank_w2 = tile([P, H // 4], I32, "blank_w2", tag="dy")
-        blank_dy = tile([P, T // 4], I32, "blank_dy", tag="ac")
+        blank_w2 = tile([P, H // 4], I32, "blank_w2", tag="ac")
+        blank_dy = tile([P, T // 4], I32, "blank_dy", tag="dy")
         nc.gpsimd.memset(blank_w2[:], 0)
         nc.gpsimd.tensor_copy(w2_sc_raw[:].bitcast(I32), blank_w2[:])
         nc.gpsimd.memset(blank_dy[:], 0)
@@ -53,35 +56,45 @@ def tile_moe_plb_silu_kernel(
 
         w2_sc_hbm = w2t_scales.bitcast(I32)
         dy_sc_hbm = dy_scales.bitcast(I32)
-
-        def load_dy_scales(q):
-            nc.sync.dma_start(dy_sc[32 * q : 32 * q + 8, :].bitcast(I32), dy_sc_hbm[:, 4 * q : 4 * q + 4, :])
-
-        ac = tile([P, 12, 2, TC], F32, "ac")
-        a_all = ac[:, 0:6]
-        c_sb = [ac[:, 6 + 3 * h : 9 + 3 * h].rearrange("p g e t -> p (g e t)").rearrange("p (e t) -> p e t", e=2) for h in range(2)]
         a_v = a.rearrange("(p j) t -> p j t", j=4)
         c_v = c.rearrange("(p j) t -> p j t", j=4)
-
-        def load_a(h, g):
-            nc.sync.dma_start(a_all[:, 3 * h + g], a_v[:, 2 * h : 2 * h + 2, g * TC : (g + 1) * TC])
+        dy_v = dy_words.rearrange("s p t d -> p s (t d)").bitcast(I32)
+        wb_v = wbt_words.bitcast(I32).rearrange("f s p k -> p (f s) k")
+        wb_sc_hbm = wbt_scales.bitcast(I32).rearrange("f s (q r) k -> r q (f s) k", r=4)
+        wa_sc_hbm = wat_scales.bitcast(I32).rearrange("f s (q r) k -> r q (f s) k", r=4)
 
         idx2 = tile([P, T // 16], U16, "idx2")
         idx1 = tile([P, T // 16], U16, "idx1")
+        w2_raw = tile([P, 2, H], U32, "w2_raw")
+        ac = tile([P, 8, T], F32, "ac")
+        a_plane = [ac[:, 0], ac[:, 1]]
+        a_pair = ac[:, 2:4]
+        c_sb = [ac[:, 4:6], ac[:, 6:8]]
+        dy_all = tile([P, G, 2, TC], U32, "dy")
+        dy = [dy_all[:, g] for g in range(G)]
+
+        def load_a(j):
+            nc.sync.dma_start(a_plane[j], a_v[:, j])
+
+        def load_dy(g):
+            nc.sync.dma_start(dy[g].bitcast(I32), dy_v[:, :, tokens(g)])
+
         nc.sync.dma_start(idx2[:], offs2)
         nc.sync.dma_start(idx1[:], offs)
-        w2_raw = tile([P, 2, H], U32, "w2_raw")
         nc.sync.dma_start(w2_raw[:].bitcast(I32), w2t_words.rearrange("s p i d -> p s (i d)").bitcast(I32))
         for q in range(4):
             nc.sync.dma_start(w2_sc_raw[32 * q : 32 * q + 8, :].bitcast(I32), w2_sc_hbm[:, 4 * q : 4 * q + 4, :])
-        dy = tile([P, 2, T], U32, "dy")
-        nc.sync.dma_start(dy[:].bitcast(I32), dy_words.rearrange("s p t d -> p s (t d)").bitcast(I32))
+        load_a(0)
+        load_a(1)
+        load_dy(0)
         for q in range(4):
-            load_dy_scales(q)
-        for k in range(6):
-            load_a(k // 3, k % 3)
-        wb_sc_hbm = wbt_scales.bitcast(I32).rearrange("f s (q r) k -> r q (f s) k", r=4)
-        wa_sc_hbm = wat_scales.bitcast(I32).rearrange("f s (q r) k -> r q (f s) k", r=4)
+            nc.sync.dma_start(dy_sc[32 * q : 32 * q + 8, :].bitcast(I32), dy_sc_hbm[:, 4 * q : 4 * q + 4, :])
+        load_dy(1)
+        load_dy(2)
+        for g in range(G):
+            nc.sync.dma_start(a_pair[:, :, tokens(g)], a_v[:, 2:4, tokens(g)])
+        nc.sync.dma_start(c_sb[0][:, :, 0:TC], c_v[:, 0:2, 0:TC])
+        nc.sync.dma_start(c_sb[0][:, :, TC:T], c_v[:, 0:2, TC:T])
         for r in range(4):
             nc.sync.dma_start(wb_sc[r:P:32, :, :].bitcast(I32), wb_sc_hbm[r])
 
@@ -99,32 +112,46 @@ def tile_moe_plb_silu_kernel(
 
         w2 = tile([P, 2, H], U32, "w2")
         w2_sc = tile([P, H], U8, "w2_sc")
-        nc.vector.tensor_copy(
-            out=w2_sc[:].rearrange("p (j m) -> p m j", j=4),
-            in_=w2_sc_raw[:].rearrange("p (m j) -> p m j", j=4),
-        )
         for s in range(2):
             nc.vector.tensor_copy(
                 out=w2[:, s, :].bitcast(I32).rearrange("p (j b i) -> p b j i", j=4, i=4),
                 in_=w2_raw[:, s, :].bitcast(I32).rearrange("p (b i j) -> p b j i", j=4, i=4),
             )
+        nc.vector.tensor_copy(
+            out=w2_sc[:].rearrange("p (j m) -> p m j", j=4),
+            in_=w2_sc_raw[:].rearrange("p (m j) -> p m j", j=4),
+        )
 
         wb = tile([P, E2, 2 * K], U8, "wb", tag="w2_raw")
-        nc.sync.dma_start(wb[:].bitcast(I32), wbt_words.bitcast(I32).rearrange("f s p k -> p (f s) k"))
-        for h in (1, 0):
-            nc.sync.dma_start(c_sb[h], c_v[:, 2 * h : 2 * h + 2, :])
+        wa = tile([P, E1, K], U32, "wa", tag="w2_sc_raw")
+        nc.sync.dma_start(wb[:, 0 : HEAD // C2].bitcast(I32), wb_v[:, 0 : HEAD // C2])
+        nc.sync.dma_start(c_sb[1], c_v[:, 2:4, :])
+        nc.sync.dma_start(wb[:, HEAD // C2 : E2].bitcast(I32), wb_v[:, HEAD // C2 : E2])
         for r in range(4):
             nc.sync.dma_start(wa_sc[r:P:32, :, :].bitcast(I32), wa_sc_hbm[r])
-        wa = tile([P, E1, K], U32, "wa", tag="w2_sc_raw")
         nc.sync.dma_start(wa[:].bitcast(I32), wat_words.rearrange("e s p k d -> p (e s) (k d)").bitcast(I32))
 
-        dc_all = tile([P, 6, TC, 2], BF16, "dc")
-        dc = [dc_all[:, 3 * h : 3 * h + 3].rearrange("p g t e -> p (g t) e") for h in range(2)]
-        p_sb = tile([P, 6, TC, 2], F32, "p_sb")
+        s_first = tile([P, 2, T], F32, "s_first")
+        s_sb = {(0, g): s_first[:, :, tokens(g)] for g in range(G)}
+        e_sb = tile([P, 2, T], F32, "e")
+        th = [tile([P, 2, T], F32, f"th{h}") for h in range(2)]
+        da_words = tile([P, 2 * T], U32, "da")
+        z = [tile([P, T], F32, "z")[:], da_words[:, T : 2 * T].bitcast(F32)]
+        for e in range(2):
+            nc.scalar.activation(s_first[:, e], a_plane[e], ACT.Silu)
+            nc.vector.scalar_tensor_tensor(e_sb[:, e], s_first[:, e], 1.0, a_plane[e], ALU.subtract, ALU.subtract)
+        for g in range(G):
+            s_sb[1, g] = tile([P, 2, TC], F32, f"s{g}")[:]
+            nc.scalar.activation(s_sb[1, g], a_pair[:, :, tokens(g)], ACT.Silu)
+        nc.scalar.activation(th[0][:], ac[:, 0:2], ACT.Tanh, scale=0.5)
+        nc.scalar.activation(th[1][:], a_pair, ACT.Tanh, scale=0.5)
+
+        dc = [tile([P, T, 2], BF16, f"dc{h}") for h in range(2)]
+        dh = {}
         for h in range(2):
-            for g in range(3):
-                bank = bank_tile([P, 2, TC], f"dh{h}{g}", 3 * h + g)
-                cols = slice(g * TC, (g + 1) * TC)
+            for g in range(G):
+                bank = bank_tile([P, 2, TC], f"dh{h}{g}", G * h + g)
+                dh[h, g] = bank
                 for e in range(2):
                     j = 2 * h + e
                     for s in range(2):
@@ -132,20 +159,17 @@ def tile_moe_plb_silu_kernel(
                             out=bank[:, e, :],
                             lhsT=w2[:, s, j * P : (j + 1) * P].bitcast(FP8X4),
                             lhsT_scale=w2_sc[4 * s : P, j * P : (j + 1) * P],
-                            rhs=dy[:, s, cols].bitcast(FP8X4),
-                            rhs_scale=dy_sc[4 * s : P, cols],
+                            rhs=dy[g][:, s, :].bitcast(FP8X4),
+                            rhs_scale=dy_sc[4 * s : P, tokens(g)],
                             start=(s == 0),
                             stop=(s == 1),
                         )
-                sg = tile([P, TC, 2], F32, f"sg{h}{g}")
-                nc.scalar.activation(sg[:], a_all[:, 3 * h + g].rearrange("p e t -> p t e"), ACT.Sigmoid)
-                nc.vector.tensor_tensor(p_sb[:, 3 * h + g], bank[:].rearrange("p e t -> p t e"), sg[:], ALU.mult)
-                if 3 * h + g < DC_GPSIMD:
-                    nc.gpsimd.tensor_tensor(dc_all[:, g], p_sb[:, g], a_all[:, g].rearrange("p e t -> p t e"), ALU.mult)
-        for part in (slice(DC_GPSIMD, 5), slice(5, 6)):
-            nc.vector.tensor_tensor(dc_all[:, part], p_sb[:, part], a_all[:, part].rearrange("p g e t -> p g t e"), ALU.mult)
-        z = tile([P, 6, TC, 2], F32, "z")
-        nc.scalar.activation(z[:], a_all.rearrange("p k e t -> p k t e"), ACT.Silu, scale=-1.0)
+                nc.vector.tensor_tensor(
+                    dc[h][:, tokens(g), :],
+                    bank[:].rearrange("p e t -> p t e"),
+                    s_sb[h, g].rearrange("p e t -> p t e"),
+                    ALU.mult,
+                )
 
         def offsets(idx, lo, hi):
             return idx[:, lo // 16 : hi // 16]
@@ -163,6 +187,63 @@ def tile_moe_plb_silu_kernel(
             scales = tile([P, n], U8, name + "_scales")
             nc.vector.quantize_mx(out=codes[:].bitcast(FP8X4), scales=scales[:], in_=src.rearrange("p n h -> p (n h)").bitcast(BF16))
             return codes, scales
+
+        order = [(h, g) for h in range(2) for g in range(G)]
+        p_words = tile([P, 2 * G * 2 * TC], U32, "p")
+        p_all = p_words[:].bitcast(F32).rearrange("p (k e t) -> p k e t", e=2, t=TC)
+        p_sb = {piece: p_all[:, k] for k, piece in enumerate(order)}
+        qgA = p_words[:, 0:3072].rearrange("p (h n) -> p h n", h=2)[:, :, 384 : 384 + HEAD]
+        qgB = p_words[:, 2048:3072].rearrange("p (h n) -> p h n", h=2)
+        qwA = tile([P, HEAD, 2], U32, "qwA")
+        gather(qgA[:, 0, :], dc[0][:], idx2, 0, HEAD)
+        gather(qgA[:, 1, :], dc[1][:], idx2, 0, HEAD)
+        nc.scalar.copy(qwA[:], qgA.rearrange("p h n -> p n h"))
+        for e in range(2):
+            nc.scalar.activation(z[e], a_pair[:, e], ACT.Silu, scale=-1.0)
+        qcA, qsA = quantise(qwA[:], HEAD, "qA")
+        gather(qgB[:, 1, :], dc[1][:], idx2, HEAD, T)
+
+        def make_p(h, g):
+            nc.vector.scalar_tensor_tensor(p_sb[h, g], th[h][:, :, tokens(g)], 1.0, dh[h, g][:], ALU.add, ALU.mult)
+
+        m = {}
+        for g in range(G):
+            m[0, g] = tile([P, 2, TC], F32, f"m{g}")[:]
+            nc.gpsimd.tensor_tensor(m[0, g], e_sb[:, :, tokens(g)], c_sb[0][:, :, tokens(g)], ALU.mult)
+
+        da = [da_words[:, h * T : (h + 1) * T].bitcast(BF16).rearrange("p (t e) -> p t e", e=2) for h in range(2)]
+        qwB = da_words[:, 2 * TC : 2 * TC + 2 * REST].rearrange("p (n h) -> p n h", h=2)
+
+        def make_da(h, g):
+            nc.gpsimd.tensor_tensor(
+                da[h][:, tokens(g), :].rearrange("p (b i) e -> p b e i", i=4),
+                m[h, g].rearrange("p e (b i) -> p b e i", i=4),
+                p_sb[h, g].rearrange("p e (b i) -> p b e i", i=4),
+                ALU.mult,
+            )
+
+        make_p(0, 0)
+        make_p(0, 1)
+        gather(qgB[:, 0, :], dc[0][:], idx2, HEAD, T)
+        make_p(0, 2)
+        make_p(1, 0)
+        make_da(0, 0)
+        make_da(0, 1)
+        w = tile([P, 2, T], F32, "w", tag="m1")[:]
+
+        def make_w(e, lo, hi):
+            nc.vector.scalar_tensor_tensor(w[:, e, lo:hi], z[e][:, lo:hi], 1.0, c_sb[1][:, e, lo:hi], ALU.subtract, ALU.mult)
+
+        make_w(1, 0, T)
+        weave_vector(qwB, qgB)
+        qcB, qsB = quantise(qwB, REST, "qB")
+        make_w(0, 0, T // 2)
+        make_w(0, T // 2, T)
+        for g in range(G):
+            m[1, g] = w[:, :, tokens(g)]
+        make_p(1, 1)
+        for piece in order[2:5]:
+            make_da(*piece)
 
         def q_matmul(dst, f, kb, codes, scales, lo):
             nc.tensor.matmul_mx(
@@ -187,53 +268,13 @@ def tile_moe_plb_silu_kernel(
             )
 
         q_win = [tile([P, T], F32, f"q_win{kb}") for kb in range(4)]
-        r_win = [tile([P, T], F32, f"r_win{kb}") for kb in range(4)]
+        r_win = [tile([P, WIDE if kb == 1 else T], F32, f"r_win{kb}") for kb in range(4)]
 
         def scatter_vector(win, idx, lo, hi, src):
             nc.vector.tensor_copy(win[:].indirect(offsets(idx, lo, hi)), src)
 
-        def scatter_scalar(win, idx, lo, hi, src):
-            nc.scalar.activation(win[:].indirect(offsets(idx, lo, hi)), src, ACT.Copy)
-
-        w_both = tile([P, 2, T, 2], F32, "w", tag="sg12")
-        w = [w_both[:, 1], w_both[:, 0]]
-        w_words = w_both[:].rearrange("p h t e -> p (h t e)").bitcast(U32)
-        qgA = w_words[:, 2 * T - HEAD : 2 * T + HEAD].rearrange("p (h n) -> p h n", h=2)
-        qgB = w_words[:, 2 * T : 2 * T + 2 * REST].rearrange("p (h n) -> p h n", h=2)
-        qwA = tile([P, HEAD, 2], U32, "qwA")[:]
-        qwB = tile([P, REST, 2], U32, "qwB")
-        gather(qgA[:, 0, :], dc[0], idx2, 0, HEAD)
-        gather(qgA[:, 1, :], dc[1], idx2, 0, HEAD)
-        nc.scalar.copy(qwA, qgA.rearrange("p h n -> p n h"))
-        gather(qgB[:, 1, :], dc[1], idx2, HEAD, T)
-        qcA, qsA = quantise(qwA, HEAD, "qA")
-        gather(qgB[:, 0, :], dc[0], idx2, HEAD, T)
-
-        def make_w(h, lo, hi):
-            nc.vector.scalar_tensor_tensor(
-                w[h][:, lo:hi],
-                z[:, 3 * h : 3 * h + 3].rearrange("p g t e -> p (g t) e")[:, lo:hi],
-                1.0,
-                c_sb[h][:, :, lo:hi].rearrange("p e t -> p t e"),
-                ALU.subtract,
-                ALU.mult,
-            )
-
-        da = [tile([P, T, 2], BF16, "da0")]
-
-        def make_da(engine, h, lo, hi):
-            p_pair = p_sb[:, 3 * h : 3 * h + 3].rearrange("p g t e -> p (g t) e")
-            engine.tensor_tensor(da[h][:, lo:hi], p_pair[:, lo:hi], w[h][:, lo:hi], ALU.mult)
-
-        make_w(0, LATE, T)
-        make_w(1, 0, T)
-        weave_vector(qwB[:], qgB)
-        qcB, qsB = quantise(qwB[:], REST, "qB")
-        make_da(nc.vector, 0, LATE, T)
-        make_w(0, 0, LATE)
-        da.append(tile([P, T, 2], BF16, "da1", tag="z"))
-        make_da(nc.gpsimd, 1, 0, T)
-        make_da(nc.gpsimd, 0, 0, LATE)
+        def scatter_scalar(win, idx, lo, hi, src, factor):
+            nc.scalar.activation(win[:].indirect(offsets(idx, lo, hi)), src, ACT.Copy, scale=factor)
 
         def q_products(dst, kb, lo, hi):
             for f in range(lo // C2, hi // C2):
@@ -249,49 +290,46 @@ def tile_moe_plb_silu_kernel(
 
         staged = []
 
-        def fill(products, name, number, runs):
-            bank = bank_tile([P, sum(hi - lo for kb, lo, hi in runs)], name, number)
-            at = 0
-            parts = []
-            for kb, lo, hi in runs:
-                parts.append(bank[:, at : at + hi - lo])
-                products(parts[-1], kb, lo, hi)
-                at += hi - lo
-            return parts
+        def scalar_unit(products, wins, idx, name, number, kb, lo, hi):
+            bank = bank_tile([P, hi - lo], name, number)
+            products(bank[:], kb, lo, hi)
+            step = 256 if hi - lo > 384 else hi - lo
+            for x in range(0, hi - lo, step):
+                stage = tile([P, step], F32, f"{name}_{x}", tag=f"stage{len(staged) % 3}")
+                staged.append(stage)
+                nc.scalar.copy(stage[:], bank[:, x : x + step])
+                scatter_scalar(wins[kb], idx, lo + x, lo + x + step, stage[:], 1.0 if wins is q_win else -0.5)
 
-        def scalar_unit(products, wins, idx, name, number, runs):
-            for part, (kb, lo, hi) in zip(fill(products, name, number, runs), runs):
-                step = 256 if hi - lo > 384 else hi - lo
-                for x in range(0, hi - lo, step):
-                    stage = tile([P, step], F32, f"{name}_{kb}_{x}", tag=f"stage{len(staged) % 3}")
-                    staged.append(stage)
-                    nc.scalar.copy(stage[:], part[:, x : x + step])
-                    scatter_scalar(wins[kb], idx, lo + x, lo + x + step, stage[:])
+        def vector_unit(products, wins, idx, name, number, kb, lo, hi):
+            bank = bank_tile([P, hi - lo], name, number)
+            products(bank[:], kb, lo, hi)
+            stage = tile([P, hi - lo], F32, f"{name}_stage")
+            if wins is q_win:
+                nc.vector.tensor_copy(stage[:], bank[:])
+            else:
+                nc.vector.tensor_scalar(stage[:], bank[:], -0.5, None, ALU.mult)
+            return lambda: scatter_vector(wins[kb], idx, lo, hi, stage[:])
 
-        def vector_unit(products, wins, idx, name, number, runs, tag=None):
-            for part, (kb, lo, hi) in zip(fill(products, name, number, runs), runs):
-                stage = tile([P, hi - lo], F32, f"{name}_{kb}", tag=tag)
-                nc.vector.tensor_copy(stage[:], part)
-                scatter_vector(wins[kb], idx, lo, hi, stage[:])
-
-        for kb, number in ((3, 6), (2, 7), (0, 4), (1, 5)):
-            scalar_unit(q_products, q_win, idx2, f"qa{kb}", number, [(kb, 0, 256)])
-        vector_unit(q_products, q_win, idx2, "qe", 1, [(3, 256, 768)])
-        vector_unit(q_products, q_win, idx2, "qh", 3, [(2, 640, 768)])
-        scalar_unit(q_products, q_win, idx2, "qc", 0, [(0, 256, 768)])
-        scalar_unit(q_products, q_win, idx2, "qf", 2, [(2, 256, 640)])
-        scalar_unit(q_products, q_win, idx2, "qi", 6, [(1, 256, 512)])
+        for kb, number in ((3, 6), (2, 7), (0, 6), (1, 7)):
+            scalar_unit(q_products, q_win, idx2, f"qa{kb}", number, kb, 0, HEAD)
+        scalar_unit(q_products, q_win, idx2, "qc", 1, 0, 256, 768)
+        scatter_qe = vector_unit(q_products, q_win, idx2, "qe", 0, 3, 256, 768)
+        make_p(1, 2)
+        make_da(1, 2)
+        scatter_qe()
+        scalar_unit(q_products, q_win, idx2, "qi", 2, 1, 256, 512)
+        scalar_unit(q_products, q_win, idx2, "qf", 6, 2, 256, 768)
 
         rgA = tile([P, 2, HEAD], U32, "rgA")
         rwA = tile([P, HEAD, 2], U32, "rwA")
         rgB = tile([P, 2, REST], U32, "rgB")
         rwB = tile([P, REST, 2], U32, "rwB")
-        for h in (1, 0):
-            gather(rgA[:, h, :], da[h][:], idx1, 0, HEAD)
+        for h in range(2):
+            gather(rgA[:, h, :], da[h], idx1, 0, HEAD)
         weave_vector(rwA[:], rgA[:])
         rcA, rsA = quantise(rwA[:], HEAD, "rA")
-        for h in (1, 0):
-            gather(rgB[:, h, :], da[h][:], idx1, HEAD, T)
+        for h in range(2):
+            gather(rgB[:, h, :], da[h], idx1, HEAD, T)
         weave_vector(rwB[:], rgB[:])
         rcB, rsB = quantise(rwB[:], REST, "rB")
 
@@ -299,23 +337,31 @@ def tile_moe_plb_silu_kernel(
             rows = slice(kb * P, (kb + 1) * P)
             for x in range(pieces):
                 cols = slice(x * T // pieces, (x + 1) * T // pieces)
-                nc.gpsimd.tensor_tensor(q_win[kb][:, cols], q_win[kb][:, cols], r_win[kb][:, cols], ALU.subtract)
+                nc.gpsimd.tensor_tensor(q_win[kb][:, cols], q_win[kb][:, cols], r_win[kb][:, cols], ALU.add)
                 nc.sync.dma_start(out[rows, cols], q_win[kb][:, cols])
 
-        vector_unit(r_products, r_win, idx1, "rb", 5, [(0, 0, 256)])
-        scalar_unit(r_products, r_win, idx1, "ra", 3, [(2, 0, 256)])
-        scalar_unit(r_products, r_win, idx1, "rj", 0, [(3, 0, 256)])
-        vector_unit(r_products, r_win, idx1, "ri", 5, [(2, 640, 768)])
-        vector_unit(r_products, r_win, idx1, "rd", 7, [(0, 256, 768)])
-        vector_unit(r_products, r_win, idx1, "rg", 4, [(1, 512, 768)])
-        vector_unit(r_products, r_win, idx1, "rf", 1, [(1, 0, 512)])
-        scalar_unit(r_products, r_win, idx1, "rc", 6, [(2, 256, 640)])
-        finish(0, 1)
+        vector_unit(r_products, r_win, idx1, "rb", 5, 0, 0, 256)()
+        scalar_unit(r_products, r_win, idx1, "ra", 4, 2, 0, 256)
+        scalar_unit(r_products, r_win, idx1, "rj", 7, 3, 0, 256)
+        scatters = [
+            vector_unit(r_products, r_win, idx1, "ri", 5, 2, 512, 768),
+            vector_unit(r_products, r_win, idx1, "rd", 0, 0, 256, 768),
+        ]
+        whole = tile([P, T], F32, "whole")
+        for name, number, lo, hi in (("rg", 2, 512, 768), ("rf", 3, 0, 512)):
+            bank = bank_tile([P, hi - lo], name, number)
+            r_products(bank[:], 1, lo, hi)
+            nc.vector.tensor_scalar(whole[:, lo:hi], bank[:], -0.5, None, ALU.mult)
+        for scatter in scatters:
+            scatter()
+        scatter_vector(r_win[1], idx1, 0, T, whole[:])
+        scalar_unit(r_products, r_win, idx1, "rc", 6, 2, 256, 512)
         finish(2, 1)
-        scalar_unit(r_products, r_win, idx1, "re", 3, [(3, 256, 768)])
+        finish(0, 1)
+        scalar_unit(r_products, r_win, idx1, "re", 1, 3, 256, 768)
         finish(3, 2)
-        scalar_unit(q_products, q_win, idx2, "qg", 2, [(1, 512, 768)])
+        scalar_unit(q_products, q_win, idx2, "qg", 4, 1, 512, 768)
         for half in range(2):
             cols = slice(half * T // 2, (half + 1) * T // 2)
-            nc.vector.tensor_tensor(q_win[1][:, cols], q_win[1][:, cols], r_win[1][:, cols], ALU.subtract)
+            nc.vector.tensor_tensor(q_win[1][:, cols], q_win[1][:, cols], r_win[1][:, cols], ALU.add)
             nc.scalar.dma_start(out[P : 2 * P, cols], q_win[1][:, cols])

@@ -21,6 +21,7 @@ G = T // TC
 HEAD = 256
 REST = T - HEAD
 WIDE = 1024
+STEP = 256
 FLOPS = 2 * N * H * T + 2 * 2 * H * K * T
 
 
@@ -200,11 +201,13 @@ def tile_moe_plb_silu_kernel(
         nc.scalar.copy(qwA[:], qgA.rearrange("p h n -> p n h"))
         for e in range(2):
             nc.scalar.activation(z[e], a_pair[:, e], ACT.Silu, scale=-1.0)
-        qcA, qsA = quantise(qwA[:], HEAD, "qA")
-        gather(qgB[:, 1, :], dc[1][:], idx2, HEAD, T)
 
         def make_p(h, g):
             nc.vector.scalar_tensor_tensor(p_sb[h, g], th[h][:, :, tokens(g)], 1.0, dh[h, g][:], ALU.add, ALU.mult)
+
+        make_p(0, 0)
+        qcA, qsA = quantise(qwA[:], HEAD, "qA")
+        gather(qgB[:, 1, :], dc[1][:], idx2, HEAD, T)
 
         m = {}
         for g in range(G):
@@ -222,7 +225,6 @@ def tile_moe_plb_silu_kernel(
                 ALU.mult,
             )
 
-        make_p(0, 0)
         make_p(0, 1)
         gather(qgB[:, 0, :], dc[0][:], idx2, HEAD, T)
         make_p(0, 2)
@@ -268,7 +270,7 @@ def tile_moe_plb_silu_kernel(
             )
 
         q_win = [tile([P, T], F32, f"q_win{kb}") for kb in range(4)]
-        r_win = [tile([P, WIDE if kb == 1 else T], F32, f"r_win{kb}") for kb in range(4)]
+        r_win = [tile([P, WIDE if kb < 2 else T], F32, f"r_win{kb}") for kb in range(4)]
 
         def scatter_vector(win, idx, lo, hi, src):
             nc.vector.tensor_copy(win[:].indirect(offsets(idx, lo, hi)), src)
@@ -290,15 +292,22 @@ def tile_moe_plb_silu_kernel(
 
         staged = []
 
-        def scalar_unit(products, wins, idx, name, number, kb, lo, hi):
+        def scalar_bank(products, wins, idx, name, number, kb, lo, hi):
             bank = bank_tile([P, hi - lo], name, number)
             products(bank[:], kb, lo, hi)
-            step = 256 if hi - lo > 384 else hi - lo
-            for x in range(0, hi - lo, step):
-                stage = tile([P, step], F32, f"{name}_{x}", tag=f"stage{len(staged) % 3}")
+
+            def piece(x):
+                stage = tile([P, STEP], F32, f"{name}_{x}", tag=f"stage{len(staged) % 3}")
                 staged.append(stage)
-                nc.scalar.copy(stage[:], bank[:, x : x + step])
-                scatter_scalar(wins[kb], idx, lo + x, lo + x + step, stage[:], 1.0 if wins is q_win else -0.5)
+                nc.scalar.copy(stage[:], bank[:, x - lo : x - lo + STEP])
+                scatter_scalar(wins[kb], idx, x, x + STEP, stage[:], 1.0 if wins is q_win else -0.5)
+
+            return piece
+
+        def scalar_unit(products, wins, idx, name, number, kb, lo, hi):
+            piece = scalar_bank(products, wins, idx, name, number, kb, lo, hi)
+            for x in range(lo, hi, STEP):
+                piece(x)
 
         def vector_unit(products, wins, idx, name, number, kb, lo, hi):
             bank = bank_tile([P, hi - lo], name, number)
@@ -312,13 +321,17 @@ def tile_moe_plb_silu_kernel(
 
         for kb, number in ((3, 6), (2, 7), (0, 6), (1, 7)):
             scalar_unit(q_products, q_win, idx2, f"qa{kb}", number, kb, 0, HEAD)
-        scalar_unit(q_products, q_win, idx2, "qc", 1, 0, 256, 768)
         scatter_qe = vector_unit(q_products, q_win, idx2, "qe", 0, 3, 256, 768)
         make_p(1, 2)
         make_da(1, 2)
         scatter_qe()
+        piece_q0 = scalar_bank(q_products, q_win, idx2, "qc", 1, 0, 256, 768)
+        piece_q2 = scalar_bank(q_products, q_win, idx2, "qf", 6, 2, 256, 768)
+        piece_q0(256)
+        piece_q2(256)
+        piece_q0(512)
         scalar_unit(q_products, q_win, idx2, "qi", 2, 1, 256, 512)
-        scalar_unit(q_products, q_win, idx2, "qf", 6, 2, 256, 768)
+        piece_q2(512)
 
         rgA = tile([P, 2, HEAD], U32, "rgA")
         rwA = tile([P, HEAD, 2], U32, "rwA")
@@ -340,27 +353,33 @@ def tile_moe_plb_silu_kernel(
                 nc.gpsimd.tensor_tensor(q_win[kb][:, cols], q_win[kb][:, cols], r_win[kb][:, cols], ALU.add)
                 nc.sync.dma_start(out[rows, cols], q_win[kb][:, cols])
 
-        vector_unit(r_products, r_win, idx1, "rb", 5, 0, 0, 256)()
-        scalar_unit(r_products, r_win, idx1, "ra", 4, 2, 0, 256)
-        scalar_unit(r_products, r_win, idx1, "rj", 7, 3, 0, 256)
-        scatters = [
-            vector_unit(r_products, r_win, idx1, "ri", 5, 2, 512, 768),
-            vector_unit(r_products, r_win, idx1, "rd", 0, 0, 256, 768),
-        ]
-        whole = tile([P, T], F32, "whole")
-        for name, number, lo, hi in (("rg", 2, 512, 768), ("rf", 3, 0, 512)):
+        scatter_ra = vector_unit(r_products, r_win, idx1, "ra", 5, 2, 0, HEAD)
+        whole = [tile([P, T], F32, f"whole{kb}") for kb in range(2)]
+
+        def empty(name, number, kb, lo, hi):
             bank = bank_tile([P, hi - lo], name, number)
-            r_products(bank[:], 1, lo, hi)
-            nc.vector.tensor_scalar(whole[:, lo:hi], bank[:], -0.5, None, ALU.mult)
-        for scatter in scatters:
-            scatter()
-        scatter_vector(r_win[1], idx1, 0, T, whole[:])
-        scalar_unit(r_products, r_win, idx1, "rc", 6, 2, 256, 512)
+            r_products(bank[:], kb, lo, hi)
+            nc.vector.tensor_scalar(whole[kb][:, lo:hi], bank[:], -0.5, None, ALU.mult)
+
+        empty("rb", 4, 0, 0, HEAD)
+        scatter_ra()
+        scalar_unit(r_products, r_win, idx1, "rj", 7, 3, 0, HEAD)
+        empty("rd", 0, 0, HEAD, T)
+        empty("rf", 4, 1, 0, HEAD)
+        empty("rg", 3, 1, HEAD, T)
+        for kb in range(2):
+            scatter_vector(r_win[kb], idx1, 0, T, whole[kb][:])
+        scalar_unit(r_products, r_win, idx1, "rc", 1, 2, HEAD, T)
         finish(2, 1)
         finish(0, 1)
-        scalar_unit(r_products, r_win, idx1, "re", 1, 3, 256, 768)
-        finish(3, 2)
-        scalar_unit(q_products, q_win, idx2, "qg", 4, 1, 512, 768)
+        scalar_unit(r_products, r_win, idx1, "re", 5, 3, HEAD, T)
+        rows = slice(3 * P, 4 * P)
+        left, right = slice(0, T // 2), slice(T // 2, T)
+        nc.gpsimd.tensor_tensor(q_win[3][:, left], q_win[3][:, left], r_win[3][:, left], ALU.add)
+        nc.sync.dma_start(out[rows, left], q_win[3][:, left])
+        nc.vector.tensor_tensor(whole[1][:, right], q_win[3][:, right], r_win[3][:, right], ALU.add)
+        nc.sync.dma_start(out[rows, right], whole[1][:, right])
+        scalar_unit(q_products, q_win, idx2, "qg", 2, 1, 512, 768)
         for half in range(2):
             cols = slice(half * T // 2, (half + 1) * T // 2)
             nc.vector.tensor_tensor(q_win[1][:, cols], q_win[1][:, cols], r_win[1][:, cols], ALU.add)

@@ -68,14 +68,14 @@ def tile_moe_plb_silu_kernel(
         idx1 = tile([P, T // 16], U16, "idx1")
         w2_raw = tile([P, 2, H], U32, "w2_raw")
         ac = tile([P, 8, T], F32, "ac")
-        a_plane = [ac[:, 0], ac[:, 1]]
-        a_pair = ac[:, 2:4]
+        a_all = ac[:, 0:4].rearrange("p j t -> p (j t)").rearrange("p (k e t) -> p k e t", k=2 * G, e=2)
+        a_first, a_pair = a_all[:, 0:G], a_all[:, G : 2 * G]
         c_sb = [ac[:, 4:6], ac[:, 6:8]]
         dy_all = tile([P, G, 2, TC], U32, "dy")
         dy = [dy_all[:, g] for g in range(G)]
 
-        def load_a(j):
-            nc.sync.dma_start(a_plane[j], a_v[:, j])
+        def load_a(g):
+            nc.sync.dma_start(a_first[:, g], a_v[:, 0:2, tokens(g)])
 
         def load_dy(g):
             nc.sync.dma_start(dy[g].bitcast(I32), dy_v[:, :, tokens(g)])
@@ -86,30 +86,19 @@ def tile_moe_plb_silu_kernel(
         for q in range(4):
             nc.sync.dma_start(w2_sc_raw[32 * q : 32 * q + 8, :].bitcast(I32), w2_sc_hbm[:, 4 * q : 4 * q + 4, :])
         load_a(0)
-        load_a(1)
         load_dy(0)
+        load_a(1)
         for q in range(4):
             nc.sync.dma_start(dy_sc[32 * q : 32 * q + 8, :].bitcast(I32), dy_sc_hbm[:, 4 * q : 4 * q + 4, :])
         load_dy(1)
+        load_a(2)
         load_dy(2)
         for g in range(G):
-            nc.sync.dma_start(a_pair[:, :, tokens(g)], a_v[:, 2:4, tokens(g)])
+            nc.sync.dma_start(a_pair[:, g], a_v[:, 2:4, tokens(g)])
         nc.sync.dma_start(c_sb[0][:, :, 0:TC], c_v[:, 0:2, 0:TC])
         nc.sync.dma_start(c_sb[0][:, :, TC:T], c_v[:, 0:2, TC:T])
         for r in range(4):
             nc.sync.dma_start(wb_sc[r:P:32, :, :].bitcast(I32), wb_sc_hbm[r])
-
-        for number in (6, 7):
-            warm = bank_tile([P, H], f"warm{number}", number)
-            nc.tensor.matmul_mx(
-                out=warm[:],
-                lhsT=w2_raw[:, 0, 0:P].bitcast(FP8X4),
-                lhsT_scale=w2_sc_raw[:, 0:P],
-                rhs=w2_raw[:, 0, :].bitcast(FP8X4),
-                rhs_scale=w2_sc_raw[:],
-                start=True,
-                stop=True,
-            )
 
         w2 = tile([P, 2, H], U32, "w2")
         w2_sc = tile([P, H], U8, "w2_sc")
@@ -132,20 +121,34 @@ def tile_moe_plb_silu_kernel(
             nc.sync.dma_start(wa_sc[r:P:32, :, :].bitcast(I32), wa_sc_hbm[r])
         nc.sync.dma_start(wa[:].bitcast(I32), wat_words.rearrange("e s p k d -> p (e s) (k d)").bitcast(I32))
 
-        s_first = tile([P, 2, T], F32, "s_first")
-        s_sb = {(0, g): s_first[:, :, tokens(g)] for g in range(G)}
-        e_sb = tile([P, 2, T], F32, "e")
-        th = [tile([P, 2, T], F32, f"th{h}") for h in range(2)]
+        for number in (6, 7):
+            warm = bank_tile([P, H], f"warm{number}", number)
+            nc.tensor.matmul_mx(
+                out=warm[:],
+                lhsT=w2[:, 0, 0:P].bitcast(FP8X4),
+                lhsT_scale=w2_sc[:, 0:P],
+                rhs=w2[:, 0, :].bitcast(FP8X4),
+                rhs_scale=w2_sc[:],
+                start=True,
+                stop=True,
+            )
+
+        s_sb = {}
+        e_sb = tile([P, G, 2, TC], F32, "e")
+        th_all = tile([P, 2 * G, 2, TC], F32, "th")
+        th = {(h, g): th_all[:, G * h + g] for h in range(2) for g in range(G)}
         da_words = tile([P, 2 * T], U32, "da")
-        z = [tile([P, T], F32, "z")[:], da_words[:, T : 2 * T].bitcast(F32)]
-        for e in range(2):
-            nc.scalar.activation(s_first[:, e], a_plane[e], ACT.Silu)
-            nc.vector.scalar_tensor_tensor(e_sb[:, e], s_first[:, e], 1.0, a_plane[e], ALU.subtract, ALU.subtract)
+        z_rest = tile([P, G - 1, 2, TC], F32, "z_rest")
+        z = [da_words[:, T : T + 2 * TC].bitcast(F32).rearrange("p (e t) -> p e t", e=2), z_rest[:, 0], z_rest[:, 1]]
+        for g in range(G):
+            s_sb[0, g] = tile([P, 2, TC], F32, f"s_first{g}")[:]
+            nc.scalar.activation(s_sb[0, g], a_first[:, g], ACT.Silu)
+            nc.vector.scalar_tensor_tensor(e_sb[:, g], s_sb[0, g], 1.0, a_first[:, g], ALU.subtract, ALU.subtract)
         for g in range(G):
             s_sb[1, g] = tile([P, 2, TC], F32, f"s{g}")[:]
-            nc.scalar.activation(s_sb[1, g], a_pair[:, :, tokens(g)], ACT.Silu)
-        nc.scalar.activation(th[0][:], ac[:, 0:2], ACT.Tanh, scale=0.5)
-        nc.scalar.activation(th[1][:], a_pair, ACT.Tanh, scale=0.5)
+            nc.scalar.activation(s_sb[1, g], a_pair[:, g], ACT.Silu)
+        for part in (slice(0, 1), slice(1, 2), slice(2, 2 * G)):
+            nc.scalar.activation(th_all[:, part], a_all[:, part], ACT.Tanh, scale=0.5)
 
         dc = [tile([P, T, 2], BF16, f"dc{h}") for h in range(2)]
         dh = {}
@@ -171,7 +174,6 @@ def tile_moe_plb_silu_kernel(
                     s_sb[h, g].rearrange("p e t -> p t e"),
                     ALU.mult,
                 )
-
         def offsets(idx, lo, hi):
             return idx[:, lo // 16 : hi // 16]
 
@@ -199,11 +201,11 @@ def tile_moe_plb_silu_kernel(
         gather(qgA[:, 0, :], dc[0][:], idx2, 0, HEAD)
         gather(qgA[:, 1, :], dc[1][:], idx2, 0, HEAD)
         nc.scalar.copy(qwA[:], qgA.rearrange("p h n -> p n h"))
-        for e in range(2):
-            nc.scalar.activation(z[e], a_pair[:, e], ACT.Silu, scale=-1.0)
+        nc.scalar.activation(z[0], a_pair[:, 0], ACT.Silu, scale=-1.0)
+        nc.scalar.activation(z_rest[:], a_pair[:, 1:G], ACT.Silu, scale=-1.0)
 
         def make_p(h, g):
-            nc.vector.scalar_tensor_tensor(p_sb[h, g], th[h][:, :, tokens(g)], 1.0, dh[h, g][:], ALU.add, ALU.mult)
+            nc.vector.scalar_tensor_tensor(p_sb[h, g], th[h, g], 1.0, dh[h, g][:], ALU.add, ALU.mult)
 
         make_p(0, 0)
         qcA, qsA = quantise(qwA[:], HEAD, "qA")
@@ -212,7 +214,7 @@ def tile_moe_plb_silu_kernel(
         m = {}
         for g in range(G):
             m[0, g] = tile([P, 2, TC], F32, f"m{g}")[:]
-            nc.gpsimd.tensor_tensor(m[0, g], e_sb[:, :, tokens(g)], c_sb[0][:, :, tokens(g)], ALU.mult)
+            nc.gpsimd.tensor_tensor(m[0, g], e_sb[:, g], c_sb[0][:, :, tokens(g)], ALU.mult)
 
         da = [da_words[:, h * T : (h + 1) * T].bitcast(BF16).rearrange("p (t e) -> p t e", e=2) for h in range(2)]
         qwB = da_words[:, 2 * TC : 2 * TC + 2 * REST].rearrange("p (n h) -> p n h", h=2)
@@ -231,18 +233,18 @@ def tile_moe_plb_silu_kernel(
         make_p(1, 0)
         make_da(0, 0)
         make_da(0, 1)
-        w = tile([P, 2, T], F32, "w", tag="m1")[:]
+        w = tile([P, G, 2, TC], F32, "w", tag="m1")
 
-        def make_w(e, lo, hi):
-            nc.vector.scalar_tensor_tensor(w[:, e, lo:hi], z[e][:, lo:hi], 1.0, c_sb[1][:, e, lo:hi], ALU.subtract, ALU.mult)
+        def make_w(g):
+            nc.vector.scalar_tensor_tensor(w[:, g], z[g], 1.0, c_sb[1][:, :, tokens(g)], ALU.subtract, ALU.mult)
 
-        make_w(1, 0, T)
+        make_w(0)
         weave_vector(qwB, qgB)
         qcB, qsB = quantise(qwB, REST, "qB")
-        make_w(0, 0, T // 2)
-        make_w(0, T // 2, T)
+        make_w(1)
+        make_w(2)
         for g in range(G):
-            m[1, g] = w[:, :, tokens(g)]
+            m[1, g] = w[:, g]
         make_p(1, 1)
         for piece in order[2:5]:
             make_da(*piece)

@@ -86,8 +86,8 @@ def tile_moe_plb_silu_kernel(
         for q in range(4):
             nc.sync.dma_start(w2_sc_raw[32 * q : 32 * q + 8, :].bitcast(I32), w2_sc_hbm[:, 4 * q : 4 * q + 4, :])
         load_a(0)
-        load_dy(0)
         load_a(1)
+        load_dy(0)
         for q in range(4):
             nc.sync.dma_start(dy_sc[32 * q : 32 * q + 8, :].bitcast(I32), dy_sc_hbm[:, 4 * q : 4 * q + 4, :])
         load_dy(1)
@@ -112,14 +112,13 @@ def tile_moe_plb_silu_kernel(
             in_=w2_sc_raw[:].rearrange("p (m j) -> p m j", j=4),
         )
 
-        wb = tile([P, E2, 2 * K], U8, "wb", tag="w2_raw")
-        wa = tile([P, E1, K], U32, "wa", tag="w2_sc_raw")
-        nc.sync.dma_start(wb[:, 0 : HEAD // C2].bitcast(I32), wb_v[:, 0 : HEAD // C2])
+        wb_head = tile([P, HEAD // C2, 2 * K], U8, "wb_head", tag="w2_raw")
+        wb_rest = tile([P, REST // C2, 2 * K], U8, "wb_rest", tag="w2_sc_raw")
+        nc.sync.dma_start(wb_head[:].bitcast(I32), wb_v[:, 0 : HEAD // C2])
         nc.sync.dma_start(c_sb[1], c_v[:, 2:4, :])
-        nc.sync.dma_start(wb[:, HEAD // C2 : E2].bitcast(I32), wb_v[:, HEAD // C2 : E2])
+        nc.sync.dma_start(wb_rest[:].bitcast(I32), wb_v[:, HEAD // C2 : E2])
         for r in range(4):
             nc.sync.dma_start(wa_sc[r:P:32, :, :].bitcast(I32), wa_sc_hbm[r])
-        nc.sync.dma_start(wa[:].bitcast(I32), wat_words.rearrange("e s p k d -> p (e s) (k d)").bitcast(I32))
 
         for number in (6, 7):
             warm = bank_tile([P, H], f"warm{number}", number)
@@ -147,7 +146,7 @@ def tile_moe_plb_silu_kernel(
         for g in range(G):
             s_sb[1, g] = tile([P, 2, TC], F32, f"s{g}")[:]
             nc.scalar.activation(s_sb[1, g], a_pair[:, g], ACT.Silu)
-        for part in (slice(0, 1), slice(1, 2), slice(2, 2 * G)):
+        for part in (slice(0, 1), slice(1, 2), slice(2, G), slice(G, 2 * G)):
             nc.scalar.activation(th_all[:, part], a_all[:, part], ACT.Tanh, scale=0.5)
 
         dc = [tile([P, T, 2], BF16, f"dc{h}") for h in range(2)]
@@ -174,6 +173,9 @@ def tile_moe_plb_silu_kernel(
                     s_sb[h, g].rearrange("p e t -> p t e"),
                     ALU.mult,
                 )
+        wa = tile([P, E1, K], U32, "wa", tag="w2")
+        nc.sync.dma_start(wa[:].bitcast(I32), wat_words.rearrange("e s p k d -> p (e s) (k d)").bitcast(I32))
+
         def offsets(idx, lo, hi):
             return idx[:, lo // 16 : hi // 16]
 
@@ -195,26 +197,27 @@ def tile_moe_plb_silu_kernel(
         p_words = tile([P, 2 * G * 2 * TC], U32, "p")
         p_all = p_words[:].bitcast(F32).rearrange("p (k e t) -> p k e t", e=2, t=TC)
         p_sb = {piece: p_all[:, k] for k, piece in enumerate(order)}
-        qgA = p_words[:, 0:3072].rearrange("p (h n) -> p h n", h=2)[:, :, 384 : 384 + HEAD]
+        qgA = p_words[:, 384 : 384 + 2048].rearrange("p (h n) -> p h n", h=2)[:, :, 0:HEAD]
         qgB = p_words[:, 2048:3072].rearrange("p (h n) -> p h n", h=2)
-        qwA = tile([P, HEAD, 2], U32, "qwA")
+        qwA = p_words[:, 2048 : 2048 + 2 * HEAD].rearrange("p (n h) -> p n h", h=2)
         gather(qgA[:, 0, :], dc[0][:], idx2, 0, HEAD)
         gather(qgA[:, 1, :], dc[1][:], idx2, 0, HEAD)
-        nc.scalar.copy(qwA[:], qgA.rearrange("p h n -> p n h"))
-        nc.scalar.activation(z[0], a_pair[:, 0], ACT.Silu, scale=-1.0)
-        nc.scalar.activation(z_rest[:], a_pair[:, 1:G], ACT.Silu, scale=-1.0)
+        nc.scalar.copy(qwA, qgA.rearrange("p h n -> p n h"))
+        for g in range(G):
+            nc.scalar.activation(z[g], a_pair[:, g], ACT.Silu, scale=-1.0)
 
         def make_p(h, g):
             nc.vector.scalar_tensor_tensor(p_sb[h, g], th[h, g], 1.0, dh[h, g][:], ALU.add, ALU.mult)
 
-        make_p(0, 0)
-        qcA, qsA = quantise(qwA[:], HEAD, "qA")
+        qcA, qsA = quantise(qwA, HEAD, "qA")
         gather(qgB[:, 1, :], dc[1][:], idx2, HEAD, T)
+        make_p(0, 1)
 
-        m = {}
-        for g in range(G):
-            m[0, g] = tile([P, 2, TC], F32, f"m{g}")[:]
-            nc.gpsimd.tensor_tensor(m[0, g], e_sb[:, g], c_sb[0][:, :, tokens(g)], ALU.mult)
+        m_head = tile([P, 2, TC], F32, "m_head")
+        m_rest = tile([P, G - 1, 2, TC], F32, "m_rest")
+        m = {(0, 0): m_head[:], (0, 1): m_rest[:, 0], (0, 2): m_rest[:, 1]}
+        nc.gpsimd.tensor_tensor(m_head[:], e_sb[:, 0], c_sb[0][:, :, 0:TC], ALU.mult)
+        nc.gpsimd.tensor_tensor(m_rest[:], e_sb[:, 1:G], c_sb[0][:, :, TC:T].rearrange("p e (g t) -> p g e t", t=TC), ALU.mult)
 
         da = [da_words[:, h * T : (h + 1) * T].bitcast(BF16).rearrange("p (t e) -> p t e", e=2) for h in range(2)]
         qwB = da_words[:, 2 * TC : 2 * TC + 2 * REST].rearrange("p (n h) -> p n h", h=2)
@@ -227,13 +230,13 @@ def tile_moe_plb_silu_kernel(
                 ALU.mult,
             )
 
-        make_p(0, 1)
+        make_p(0, 0)
         gather(qgB[:, 0, :], dc[0][:], idx2, HEAD, T)
         make_p(0, 2)
         make_p(1, 0)
-        make_da(0, 0)
         make_da(0, 1)
-        w = tile([P, G, 2, TC], F32, "w", tag="m1")
+        make_da(0, 0)
+        w = tile([P, G, 2, TC], F32, "w", tag="m_head")
 
         def make_w(g):
             nc.vector.scalar_tensor_tensor(w[:, g], z[g], 1.0, c_sb[1][:, :, tokens(g)], ALU.subtract, ALU.mult)
@@ -250,9 +253,10 @@ def tile_moe_plb_silu_kernel(
             make_da(*piece)
 
         def q_matmul(dst, f, kb, codes, scales, lo):
+            words = wb_head[:, f] if f * C2 < HEAD else wb_rest[:, f - HEAD // C2]
             nc.tensor.matmul_mx(
                 out=dst,
-                lhsT=wb[:, f, 2 * P * kb : 2 * P * (kb + 1)].bitcast(FP4X4),
+                lhsT=words[:, 2 * P * kb : 2 * P * (kb + 1)].bitcast(FP4X4),
                 lhsT_scale=wb_sc[:, f, P * kb : P * (kb + 1)],
                 rhs=codes[:, lo : lo + C2].bitcast(FP8X4),
                 rhs_scale=scales[:, lo : lo + C2],
@@ -376,7 +380,7 @@ def tile_moe_plb_silu_kernel(
         finish(0, 1)
         scalar_unit(r_products, r_win, idx1, "re", 5, 3, HEAD, T)
         rows = slice(3 * P, 4 * P)
-        left, right = slice(0, T // 2), slice(T // 2, T)
+        left, right = slice(0, 2 * T // 3), slice(2 * T // 3, T)
         nc.gpsimd.tensor_tensor(q_win[3][:, left], q_win[3][:, left], r_win[3][:, left], ALU.add)
         nc.sync.dma_start(out[rows, left], q_win[3][:, left])
         nc.vector.tensor_tensor(whole[1][:, right], q_win[3][:, right], r_win[3][:, right], ALU.add)

from contextlib import ExitStack

import concourse.mybir as mybir

F32 = mybir.dt.float32
BF16 = mybir.dt.bfloat16
I32 = mybir.dt.int32
U32 = mybir.dt.uint32
U16 = mybir.dt.uint16
U8 = mybir.dt.uint8
FP8X4 = mybir.dt.float8_e4m3fn_x4
FP4X4 = mybir.dt.float4_e2m1fn_x4
ACT = mybir.ActivationFunctionType
ALU = mybir.AluOpType

K, T, H, N = 512, 768, 512, 1024
E1, C1, E2, C2 = 3, 256, 6, 128
P = 128
TC = 256
G = T // TC
HEAD = 256
REST = T - HEAD
WIDE = 1024
STEP = 256
FLOPS = 2 * N * H * T + 2 * 2 * H * K * T


def tile_moe_plb_silu_kernel(
    tc, dy_words, dy_scales, w2t_words, w2t_scales, wat_words, wat_scales, wbt_words, wbt_scales, a, c, offs, offs2, out
):
    nc = tc.nc
    with ExitStack() as ctx:
        sb = ctx.enter_context(tc.tile_pool(name="sb", bufs=1))
        ps = ctx.enter_context(tc.psum_pool(name="ps", bufs=1))

        def tile(shape, dtype, name, tag=None):
            return sb.tile(shape, dtype, name=name, tag=tag or name, align_bytes=64)

        def bank_tile(shape, name, number):
            return ps.tile(shape, F32, name=name, tag=f"bank{number}")

        def tokens(g):
            return slice(g * TC, (g + 1) * TC)

        w2_sc_raw = tile([P, H], U8, "w2_sc_raw")
        dy_sc = tile([P, T], U8, "dy_sc")
        wb_sc = tile([P, E2, K], U8, "wb_sc")
        wa_sc = tile([P, E1, K], U8, "wa_sc")
        blank_w2 = tile([P, H // 4], I32, "blank_w2", tag="ac")
        blank_dy = tile([P, T // 4], I32, "blank_dy", tag="dy")
        nc.gpsimd.memset(blank_w2[:], 0)
        nc.gpsimd.tensor_copy(w2_sc_raw[:].bitcast(I32), blank_w2[:])
        nc.gpsimd.memset(blank_dy[:], 0)
        nc.gpsimd.tensor_copy(dy_sc[:].bitcast(I32), blank_dy[:])
        nc.gpsimd.memset(wb_sc[:].rearrange("p f k -> p (f k)").bitcast(I32), 0)
        nc.gpsimd.memset(wa_sc[:].rearrange("p f k -> p (f k)").bitcast(I32), 0)

        w2_sc_hbm = w2t_scales.bitcast(I32)
        dy_sc_hbm = dy_scales.bitcast(I32)
        a_v = a.rearrange("(p j) t -> p j t", j=4)
        c_v = c.rearrange("(p j) t -> p j t", j=4)
        dy_v = dy_words.rearrange("s p t d -> p s (t d)").bitcast(I32)
        wb_v = wbt_words.bitcast(I32).rearrange("f s p k -> p (f s) k")
        wb_sc_hbm = wbt_scales.bitcast(I32).rearrange("f s (q r) k -> r q (f s) k", r=4)
        wa_sc_hbm = wat_scales.bitcast(I32).rearrange("f s (q r) k -> r q (f s) k", r=4)

        idx2 = tile([P, T // 16], U16, "idx2")
        idx1 = tile([P, T // 16], U16, "idx1")
        w2_raw = tile([P, 2, H], U32, "w2_raw")
        ac = tile([P, 8, T], F32, "ac")
        a_all = ac[:, 0:4].rearrange("p j t -> p (j t)").rearrange("p (k e t) -> p k e t", k=2 * G, e=2)
        a_first, a_pair = a_all[:, 0:G], a_all[:, G : 2 * G]
        c_sb = [ac[:, 4:6], ac[:, 6:8]]
        dy_all = tile([P, G, 2, TC], U32, "dy")
        dy = [dy_all[:, g] for g in range(G)]

        def load_a(g):
            nc.sync.dma_start(a_first[:, g], a_v[:, 0:2, tokens(g)])

        def load_dy(g):
            nc.sync.dma_start(dy[g].bitcast(I32), dy_v[:, :, tokens(g)])

        nc.sync.dma_start(idx2[:], offs2)
        nc.sync.dma_start(idx1[:], offs)
        nc.sync.dma_start(w2_raw[:].bitcast(I32), w2t_words.rearrange("s p i d -> p s (i d)").bitcast(I32))
        for q in range(4):
            nc.sync.dma_start(w2_sc_raw[32 * q : 32 * q + 8, :].bitcast(I32), w2_sc_hbm[:, 4 * q : 4 * q + 4, :])
        load_a(0)
        load_a(1)
        load_dy(0)
        for q in range(4):
            nc.sync.dma_start(dy_sc[32 * q : 32 * q + 8, :].bitcast(I32), dy_sc_hbm[:, 4 * q : 4 * q + 4, :])
        load_dy(1)
        load_a(2)
        load_dy(2)
        for g in range(G):
            nc.sync.dma_start(a_pair[:, g], a_v[:, 2:4, tokens(g)])
        nc.sync.dma_start(c_sb[0][:, :, 0:TC], c_v[:, 0:2, 0:TC])
        nc.sync.dma_start(c_sb[0][:, :, TC:T], c_v[:, 0:2, TC:T])
        for r in range(4):
            nc.sync.dma_start(wb_sc[r:P:32, :, :].bitcast(I32), wb_sc_hbm[r])

        w2 = tile([P, 2, H], U32, "w2")
        w2_sc = tile([P, H], U8, "w2_sc")
        for s in range(2):
            nc.vector.tensor_copy(
                out=w2[:, s, :].bitcast(I32).rearrange("p (j b i) -> p b j i", j=4, i=4),
                in_=w2_raw[:, s, :].bitcast(I32).rearrange("p (b i j) -> p b j i", j=4, i=4),
            )
        nc.vector.tensor_copy(
            out=w2_sc[:].rearrange("p (j m) -> p m j", j=4),
            in_=w2_sc_raw[:].rearrange("p (m j) -> p m j", j=4),
        )

        wb_head = tile([P, HEAD // C2, 2 * K], U8, "wb_head", tag="w2_raw")
        wb_rest = tile([P, REST // C2, 2 * K], U8, "wb_rest", tag="w2_sc_raw")
        nc.sync.dma_start(wb_head[:].bitcast(I32), wb_v[:, 0 : HEAD // C2])
        nc.sync.dma_start(c_sb[1], c_v[:, 2:4, :])
        nc.sync.dma_start(wb_rest[:].bitcast(I32), wb_v[:, HEAD // C2 : E2])
        for r in range(4):
            nc.sync.dma_start(wa_sc[r:P:32, :, :].bitcast(I32), wa_sc_hbm[r])

        for number in (6, 7):
            warm = bank_tile([P, H], f"warm{number}", number)
            nc.tensor.matmul_mx(
                out=warm[:],
                lhsT=w2[:, 0, 0:P].bitcast(FP8X4),
                lhsT_scale=w2_sc[:, 0:P],
                rhs=w2[:, 0, :].bitcast(FP8X4),
                rhs_scale=w2_sc[:],
                start=True,
                stop=True,
            )

        s_sb = {}
        e_sb = tile([P, G, 2, TC], F32, "e")
        th_all = tile([P, 2 * G, 2, TC], F32, "th")
        th = {(h, g): th_all[:, G * h + g] for h in range(2) for g in range(G)}
        da_words = tile([P, 2 * T], U32, "da")
        z_rest = tile([P, G - 1, 2, TC], F32, "z_rest")
        z = [da_words[:, T : T + 2 * TC].bitcast(F32).rearrange("p (e t) -> p e t", e=2), z_rest[:, 0], z_rest[:, 1]]
        for g in range(G):
            s_sb[0, g] = tile([P, 2, TC], F32, f"s_first{g}")[:]
            nc.scalar.activation(s_sb[0, g], a_first[:, g], ACT.Silu)
            nc.vector.scalar_tensor_tensor(e_sb[:, g], s_sb[0, g], 1.0, a_first[:, g], ALU.subtract, ALU.subtract)
        for g in range(G):
            s_sb[1, g] = tile([P, 2, TC], F32, f"s{g}")[:]
            nc.scalar.activation(s_sb[1, g], a_pair[:, g], ACT.Silu)
        for part in (slice(0, 1), slice(1, 2), slice(2, G), slice(G, 2 * G)):
            nc.scalar.activation(th_all[:, part], a_all[:, part], ACT.Tanh, scale=0.5)

        dc = [tile([P, T, 2], BF16, f"dc{h}") for h in range(2)]
        dh = {}
        for h in range(2):
            for g in range(G):
                bank = bank_tile([P, 2, TC], f"dh{h}{g}", G * h + g)
                dh[h, g] = bank
                for e in range(2):
                    j = 2 * h + e
                    for s in range(2):
                        nc.tensor.matmul_mx(
                            out=bank[:, e, :],
                            lhsT=w2[:, s, j * P : (j + 1) * P].bitcast(FP8X4),
                            lhsT_scale=w2_sc[4 * s : P, j * P : (j + 1) * P],
                            rhs=dy[g][:, s, :].bitcast(FP8X4),
                            rhs_scale=dy_sc[4 * s : P, tokens(g)],
                            start=(s == 0),
                            stop=(s == 1),
                        )
                nc.vector.tensor_tensor(
                    dc[h][:, tokens(g), :],
                    bank[:].rearrange("p e t -> p t e"),
                    s_sb[h, g].rearrange("p e t -> p t e"),
                    ALU.mult,
                )
        wa = tile([P, E1, K], U32, "wa", tag="w2")
        nc.sync.dma_start(wa[:].bitcast(I32), wat_words.rearrange("e s p k d -> p (e s) (k d)").bitcast(I32))

        def offsets(idx, lo, hi):
            return idx[:, lo // 16 : hi // 16]

        def gather(dst, src, idx, lo, hi):
            nc.vector.tensor_copy(dst, src.rearrange("p t e -> p (t e)").bitcast(U32).indirect(offsets(idx, lo, hi)))

        def weave_vector(dst, src):
            nc.vector.tensor_copy(
                dst.bitcast(I32).rearrange("p (b i) h -> p b h i", i=4), src.bitcast(I32).rearrange("p h (b i) -> p b h i", i=4)
            )

        def quantise(src, n, name):
            codes = tile([P, n], U32, name + "_codes")
            scales = tile([P, n], U8, name + "_scales")
            nc.vector.quantize_mx(out=codes[:].bitcast(FP8X4), scales=scales[:], in_=src.rearrange("p n h -> p (n h)").bitcast(BF16))
            return codes, scales

        order = [(h, g) for h in range(2) for g in range(G)]
        p_words = tile([P, 2 * G * 2 * TC], U32, "p")
        p_all = p_words[:].bitcast(F32).rearrange("p (k e t) -> p k e t", e=2, t=TC)
        p_sb = {piece: p_all[:, k] for k, piece in enumerate(order)}
        qgA = p_words[:, 384 : 384 + 2048].rearrange("p (h n) -> p h n", h=2)[:, :, 0:HEAD]
        qgB = p_words[:, 2048:3072].rearrange("p (h n) -> p h n", h=2)
        qwA = p_words[:, 2048 : 2048 + 2 * HEAD].rearrange("p (n h) -> p n h", h=2)
        gather(qgA[:, 0, :], dc[0][:], idx2, 0, HEAD)
        gather(qgA[:, 1, :], dc[1][:], idx2, 0, HEAD)
        nc.scalar.copy(qwA, qgA.rearrange("p h n -> p n h"))
        for g in range(G):
            nc.scalar.activation(z[g], a_pair[:, g], ACT.Silu, scale=-1.0)

        def make_p(h, g):
            nc.vector.scalar_tensor_tensor(p_sb[h, g], th[h, g], 1.0, dh[h, g][:], ALU.add, ALU.mult)

        qcA, qsA = quantise(qwA, HEAD, "qA")
        gather(qgB[:, 1, :], dc[1][:], idx2, HEAD, T)
        make_p(0, 1)

        m_head = tile([P, 2, TC], F32, "m_head")
        m_rest = tile([P, G - 1, 2, TC], F32, "m_rest")
        m = {(0, 0): m_head[:], (0, 1): m_rest[:, 0], (0, 2): m_rest[:, 1]}
        nc.gpsimd.tensor_tensor(m_head[:], e_sb[:, 0], c_sb[0][:, :, 0:TC], ALU.mult)
        nc.gpsimd.tensor_tensor(m_rest[:], e_sb[:, 1:G], c_sb[0][:, :, TC:T].rearrange("p e (g t) -> p g e t", t=TC), ALU.mult)

        da = [da_words[:, h * T : (h + 1) * T].bitcast(BF16).rearrange("p (t e) -> p t e", e=2) for h in range(2)]
        qwB = da_words[:, 2 * TC : 2 * TC + 2 * REST].rearrange("p (n h) -> p n h", h=2)

        def make_da(h, g):
            nc.gpsimd.tensor_tensor(
                da[h][:, tokens(g), :].rearrange("p (b i) e -> p b e i", i=4),
                m[h, g].rearrange("p e (b i) -> p b e i", i=4),
                p_sb[h, g].rearrange("p e (b i) -> p b e i", i=4),
                ALU.mult,
            )

        make_p(0, 0)
        gather(qgB[:, 0, :], dc[0][:], idx2, HEAD, T)
        make_p(0, 2)
        make_p(1, 0)
        make_da(0, 1)
        make_da(0, 0)
        w = tile([P, G, 2, TC], F32, "w", tag="m_head")

        def make_w(g):
            nc.vector.scalar_tensor_tensor(w[:, g], z[g], 1.0, c_sb[1][:, :, tokens(g)], ALU.subtract, ALU.mult)

        make_w(0)
        weave_vector(qwB, qgB)
        qcB, qsB = quantise(qwB, REST, "qB")
        make_w(1)
        make_w(2)
        for g in range(G):
            m[1, g] = w[:, g]
        make_p(1, 1)
        for piece in order[2:5]:
            make_da(*piece)

        def q_matmul(dst, f, kb, codes, scales, lo):
            words = wb_head[:, f] if f * C2 < HEAD else wb_rest[:, f - HEAD // C2]
            nc.tensor.matmul_mx(
                out=dst,
                lhsT=words[:, 2 * P * kb : 2 * P * (kb + 1)].bitcast(FP4X4),
                lhsT_scale=wb_sc[:, f, P * kb : P * (kb + 1)],
                rhs=codes[:, lo : lo + C2].bitcast(FP8X4),
                rhs_scale=scales[:, lo : lo + C2],
                start=True,
                stop=True,
            )

        def r_matmul(dst, e, kb, codes, scales, lo, hi):
            nc.tensor.matmul_mx(
                out=dst,
                lhsT=wa[:, e, P * kb : P * (kb + 1)].bitcast(FP8X4),
                lhsT_scale=wa_sc[:, e, P * kb : P * (kb + 1)],
                rhs=codes[:, lo:hi].bitcast(FP8X4),
                rhs_scale=scales[:, lo:hi],
                start=True,
                stop=True,
            )

        q_win = [tile([P, T], F32, f"q_win{kb}") for kb in range(4)]
        r_win = [tile([P, WIDE if kb < 2 else T], F32, f"r_win{kb}") for kb in range(4)]

        def scatter_vector(win, idx, lo, hi, src):
            nc.vector.tensor_copy(win[:].indirect(offsets(idx, lo, hi)), src)

        def scatter_scalar(win, idx, lo, hi, src, factor):
            nc.scalar.activation(win[:].indirect(offsets(idx, lo, hi)), src, ACT.Copy, scale=factor)

        def q_products(dst, kb, lo, hi):
            for f in range(lo // C2, hi // C2):
                codes, scales, first = (qcA, qsA, 0) if f * C2 < HEAD else (qcB, qsB, HEAD)
                q_matmul(dst[:, f * C2 - lo : (f + 1) * C2 - lo], f, kb, codes, scales, f * C2 - first)

        def r_products(dst, kb, lo, hi):
            for e in range(E1):
                x, y = max(lo, e * C1), min(hi, (e + 1) * C1)
                if x < y:
                    codes, scales, first = (rcA, rsA, 0) if x < HEAD else (rcB, rsB, HEAD)
                    r_matmul(dst[:, x - lo : y - lo], e, kb, codes, scales, x - first, y - first)

        staged = []

        def scalar_bank(products, wins, idx, name, number, kb, lo, hi):
            bank = bank_tile([P, hi - lo], name, number)
            products(bank[:], kb, lo, hi)

            def piece(x):
                stage = tile([P, STEP], F32, f"{name}_{x}", tag=f"stage{len(staged) % 3}")
                staged.append(stage)
                nc.scalar.copy(stage[:], bank[:, x - lo : x - lo + STEP])
                scatter_scalar(wins[kb], idx, x, x + STEP, stage[:], 1.0 if wins is q_win else -0.5)

            return piece

        def scalar_unit(products, wins, idx, name, number, kb, lo, hi):
            piece = scalar_bank(products, wins, idx, name, number, kb, lo, hi)
            for x in range(lo, hi, STEP):
                piece(x)

        def vector_unit(products, wins, idx, name, number, kb, lo, hi):
            bank = bank_tile([P, hi - lo], name, number)
            products(bank[:], kb, lo, hi)
            stage = tile([P, hi - lo], F32, f"{name}_stage")
            if wins is q_win:
                nc.vector.tensor_copy(stage[:], bank[:])
            else:
                nc.vector.tensor_scalar(stage[:], bank[:], -0.5, None, ALU.mult)
            return lambda: scatter_vector(wins[kb], idx, lo, hi, stage[:])

        for kb, number in ((3, 6), (2, 7), (0, 6), (1, 7)):
            scalar_unit(q_products, q_win, idx2, f"qa{kb}", number, kb, 0, HEAD)
        scatter_qe = vector_unit(q_products, q_win, idx2, "qe", 0, 3, 256, 768)
        make_p(1, 2)
        make_da(1, 2)
        scatter_qe()
        piece_q0 = scalar_bank(q_products, q_win, idx2, "qc", 1, 0, 256, 768)
        piece_q2 = scalar_bank(q_products, q_win, idx2, "qf", 6, 2, 256, 768)
        piece_q0(256)
        piece_q2(256)
        piece_q0(512)
        scalar_unit(q_products, q_win, idx2, "qi", 2, 1, 256, 512)
        piece_q2(512)

        rgA = tile([P, 2, HEAD], U32, "rgA")
        rwA = tile([P, HEAD, 2], U32, "rwA")
        rgB = tile([P, 2, REST], U32, "rgB")
        rwB = tile([P, REST, 2], U32, "rwB")
        for h in range(2):
            gather(rgA[:, h, :], da[h], idx1, 0, HEAD)
        weave_vector(rwA[:], rgA[:])
        rcA, rsA = quantise(rwA[:], HEAD, "rA")
        for h in range(2):
            gather(rgB[:, h, :], da[h], idx1, HEAD, T)
        weave_vector(rwB[:], rgB[:])
        rcB, rsB = quantise(rwB[:], REST, "rB")

        def finish(kb, pieces):
            rows = slice(kb * P, (kb + 1) * P)
            for x in range(pieces):
                cols = slice(x * T // pieces, (x + 1) * T // pieces)
                nc.gpsimd.tensor_tensor(q_win[kb][:, cols], q_win[kb][:, cols], r_win[kb][:, cols], ALU.add)
                nc.sync.dma_start(out[rows, cols], q_win[kb][:, cols])

        scatter_ra = vector_unit(r_products, r_win, idx1, "ra", 5, 2, 0, HEAD)
        whole = [tile([P, T], F32, f"whole{kb}") for kb in range(2)]

        def empty(name, number, kb, lo, hi):
            bank = bank_tile([P, hi - lo], name, number)
            r_products(bank[:], kb, lo, hi)
            nc.vector.tensor_scalar(whole[kb][:, lo:hi], bank[:], -0.5, None, ALU.mult)

        empty("rb", 4, 0, 0, HEAD)
        scatter_ra()
        scalar_unit(r_products, r_win, idx1, "rj", 7, 3, 0, HEAD)
        empty("rd", 0, 0, HEAD, T)
        empty("rf", 4, 1, 0, HEAD)
        empty("rg", 3, 1, HEAD, T)
        for kb in range(2):
            scatter_vector(r_win[kb], idx1, 0, T, whole[kb][:])
        scalar_unit(r_products, r_win, idx1, "rc", 1, 2, HEAD, T)
        finish(2, 1)
        finish(0, 1)
        scalar_unit(r_products, r_win, idx1, "re", 5, 3, HEAD, T)
        rows = slice(3 * P, 4 * P)
        left, right = slice(0, 2 * T // 3), slice(2 * T // 3, T)
        nc.gpsimd.tensor_tensor(q_win[3][:, left], q_win[3][:, left], r_win[3][:, left], ALU.add)
        nc.sync.dma_start(out[rows, left], q_win[3][:, left])
        nc.vector.tensor_tensor(whole[1][:, right], q_win[3][:, right], r_win[3][:, right], ALU.add)
        nc.sync.dma_start(out[rows, right], whole[1][:, right])
        scalar_unit(q_products, q_win, idx2, "qg", 2, 1, 512, 768)
        for half in range(2):
            cols = slice(half * T // 2, (half + 1) * T // 2)
            nc.vector.tensor_tensor(q_win[1][:, cols], q_win[1][:, cols], r_win[1][:, cols], ALU.add)
            nc.scalar.dma_start(out[P : 2 * P, cols], q_win[1][:, cols])
